import numpy as np
import ml_dtypes


def mxq(x, axis, fmt="e4m3"):
    dtype, down = {"e4m3": (ml_dtypes.float8_e4m3fn, 7), "e5m2": (ml_dtypes.float8_e5m2, 14)}[fmt]
    v = np.moveaxis(np.asarray(x, np.float32).astype(ml_dtypes.bfloat16).astype(np.float64), axis, -1)
    blocks = v.reshape(v.shape[:-1] + (-1, 32))
    amax = np.abs(blocks).max(-1, keepdims=True)
    byte = np.maximum(np.where(amax > 0, np.frexp(amax)[1] - 1 + 127, 0) - down, 1)
    scale = np.exp2(byte - 127.0)
    codes = (blocks / scale).astype(np.float32).astype(dtype).astype(np.float64)
    return np.moveaxis((codes * scale).reshape(v.shape), -1, axis)


WIDE = False


def mx_kscale(k):
    if not WIDE:
        return np.ones(k)
    levels = np.array([24, -24, 12, -12, 0])
    if k % 512:
        return np.exp2(np.random.permutation(np.resize(levels, k // 32))).repeat(32)
    a = np.empty((k // 512, 16))
    for p in range(k // 512):
        a[p, :8] = np.random.permutation(np.resize(levels, 8))
        for g in range(8):
            far = levels[np.abs(levels - a[p, g]) >= 10]
            a[p, g + 8] = far[np.random.randint(len(far))]
    return np.exp2(a.ravel()).repeat(32)


def f64(x):
    return np.asarray(x).astype(np.float64)


def striped(idx):
    return np.tile(idx.reshape(-1, 16).T, (8, 1)).astype(np.uint16)


def unstriped(offs):
    return offs[:16].T.reshape(-1).astype(np.int64)


E2M1 = np.array([0.0, 0.5, 1.0, 1.5, 2.0, 3.0, 4.0, 6.0, -0.0, -0.5, -1.0, -1.5, -2.0, -3.0, -4.0, -6.0])


def pack_weight(w, fmt):
    k, n = w.shape
    w = f64(np.asarray(w, np.float32).astype(ml_dtypes.bfloat16)).reshape(k // 32, 32, n)
    amax = np.abs(w).max(1)
    if fmt == "e4m3":
        byte = np.frexp(amax)[1] - 1 + 127 - 7
    else:
        mant, ex = np.frexp(amax / 6.0)
        byte = np.where(mant > 0.5, ex, ex - 1) + 127
    byte = np.clip(np.where(amax > 0, byte, 1), 1, 254)
    scaled = (w * np.exp2(127.0 - byte)[:, None, :]).reshape(k, n).astype(np.float32)
    by_word = np.ascontiguousarray(scaled.reshape(k // 512, 128, 4, n).transpose(0, 1, 3, 2))
    if fmt == "e4m3":
        words = by_word.astype(ml_dtypes.float8_e4m3fn).view(np.uint8)
    else:
        c = by_word.astype(ml_dtypes.float4_e2m1fn).view(np.uint8) & 0xF
        words = (c[..., 0::2] | (c[..., 1::2] << 4)).reshape(k // 512, 128, 2 * n)
    return np.ascontiguousarray(words), np.ascontiguousarray(byte.astype(np.uint8).reshape(k // 512, 16, n))


def unpack_weight(words, scales, fmt):
    g, _, n = scales.shape
    words = np.ascontiguousarray(words).reshape(g, 128, n, -1)
    if fmt == "e4m3":
        vals = words.view(ml_dtypes.float8_e4m3fn).astype(np.float64)
    else:
        nib = np.empty((g, 128, n, 4), np.uint8)
        nib[..., 0::2] = words & 0xF
        nib[..., 1::2] = words >> 4
        vals = E2M1[nib]
    vals = vals * np.repeat(np.exp2(scales.astype(np.float64) - 127.0), 8, axis=1)[..., None]
    return vals.transpose(0, 1, 3, 2).reshape(g * 512, n)


def planes(y):
    n, m = y.shape
    v = y.astype(np.float32).astype(ml_dtypes.bfloat16).astype(np.float64).reshape(n // 32, 32, m)
    top = np.abs(v).max(1)
    byte = np.clip(np.where(top > 0, np.frexp(top)[1] - 1 + 127 - 7, 1), 1, 254)
    codes = (v * np.exp2(127.0 - byte)[:, None, :]).reshape(n, m).astype(np.float32).astype(ml_dtypes.float8_e4m3fn).view(np.uint8)
    words = codes.reshape(n // 512, 128, 4, m).transpose(0, 1, 3, 2)
    return np.ascontiguousarray(words), np.ascontiguousarray(byte.astype(np.uint8).reshape(n // 512, 16, m))


K, M, N, T, J = 1024, 512, 512, 2048, 1024


def setup_inputs():
    n = np.random.standard_normal
    s = mx_kscale(K)[:, None]
    s2 = mx_kscale(M)[:, None]
    h = np.tanh(n((N, T)))
    p_tab = pack_weight(h * s2, "e4m3")
    p_wn = pack_weight(n((K, N)) / np.sqrt(K) / s, "e2m1")
    return {
        "x": (n((K, J)) * s).astype(np.float32),
        "tab_words": p_tab[0],
        "tab_scales": p_tab[1],
        "wn_words": p_wn[0],
        "wn_scales": p_wn[1],
        "un": (n((M, N)) / np.sqrt(M) / s2).astype(np.float32),
        "bn": (0.3 * n(N)).astype(np.float32),
        "hT": (h).astype(np.float32),
        "wgo": np.tile(np.random.uniform(0.5, 2.0, J), (128, 1)).astype(np.float32),
        "offs": striped(np.random.permutation(T)[:J]),
    }


def reference(x, tab_words, tab_scales, wn_words, wn_scales, un, bn, hT, wgo, offs):
    idx = unstriped(offs)
    x_ = mxq(f64(x), 0, "e4m3")
    tab_ = unpack_weight(tab_words, tab_scales, "e4m3")[:, idx]
    wn_ = unpack_weight(wn_words, wn_scales, "e2m1")
    un_ = mxq(f64(un), 0, "e4m3")
    sn = wn_.T @ x_ + un_.T @ tab_
    out = np.zeros((N, T))
    out[:, idx] = f64(wgo)[0] * (np.tanh(sn + f64(bn)[:, None]) + f64(hT)[:, idx])
    return (out,) + planes(out)

@@ -1,0 +1,240 @@
+from contextlib import ExitStack
+
+import concourse.mybir as mybir
+
+K, M, N, T, J = 1024, 512, 512, 2048, 1024
+FLOPS = 2 * (K + M) * N * J
+
+F32 = mybir.dt.float32
+BF16 = mybir.dt.bfloat16
+I32 = mybir.dt.int32
+U32 = mybir.dt.uint32
+U16 = mybir.dt.uint16
+U8 = mybir.dt.uint8
+FP8X4 = mybir.dt.float8_e4m3fn_x4
+FP4X4 = mybir.dt.float4_e2m1fn_x4
+ADD = mybir.AluOpType.add
+MULT = mybir.AluOpType.mult
+TANH = mybir.ActivationFunctionType.Tanh
+
+P = 128
+PACK = 4
+PASSES = K // (P * PACK)
+HALF = J // 2
+PIECE = 512
+PIECES = T // PIECE
+
+
+def tile_list_tgn_rnnP_kernel(
+    tc, x, tab_words, tab_scales, wn_words, wn_scales, un, bn, hT, wgo, offs, out_0, out_1, out_2
+):
+    nc = tc.nc
+    with ExitStack() as ctx:
+        sb = ctx.enter_context(tc.tile_pool(name="sb", bufs=1))
+        ps = ctx.enter_context(tc.psum_pool(name="ps", bufs=1))
+
+        def tile(name, shape, dtype):
+            return sb.tile(shape, dtype, name=name, align_bytes=64)
+
+        offsets = tile("offsets", [P, J // 16], U16)
+        wn_raw = tile("wn_raw", [P, PASSES * N // 2], I32)
+        wn_dealt = tile("wn_dealt", [P, PASSES * N // 2], I32)
+        wn_scale_raw = tile("wn_scale_raw", [P, PASSES * N], U8)
+        wn_scale = tile("wn_scale", [P, PASSES * N], U8)
+        table = tile("table", [P, T], I32)
+        table_scale = tile("table_scale", [P, T], U8)
+        picked = [tile("picked%d" % c, [P, HALF], I32) for c in range(2)]
+        picked_scale = [tile("picked_scale%d" % c, [P, HALF], U8) for c in range(2)]
+        un_raw = tile("un_raw", [P, PACK, N], F32)
+        un_bf = [tile("un_bf0", [P, P * PACK], BF16), tile("un_bf1", [P, P * PACK], BF16), tile("un_bf23", [P, 2 * P * PACK], BF16)]
+        un_codes = tile("un_codes", [P, N], U32)
+        un_scale = tile("un_scale", [P, N], U8)
+        bias = tile("bias", [P, PACK], F32)
+        weight = tile("weight", [P, J], F32)
+        x_raw = {(c, a): tile("x_raw%d%d" % (c, a), [P, PACK, HALF], F32) for c in range(2) for a in range(PASSES)}
+        x_bf = {(c, a): tile("x_bf%d%d" % (c, a), [P, HALF * PACK], BF16) for c in range(2) for a in range(PASSES)}
+        x_codes = {(c, a): tile("x_codes%d%d" % (c, a), [P, HALF], U32) for c in range(2) for a in range(PASSES)}
+        x_scale = {(c, a): tile("x_scale%d%d" % (c, a), [P, HALF], U8) for c in range(2) for a in range(PASSES)}
+        state = [tile("state%d" % t, [P, T], F32) for t in range(PACK)]
+        act = [tile("act%d" % t, [P, J], F32) for t in range(PACK)]
+        updated = [tile("updated%d" % t, [P, J], F32) for t in range(PACK)]
+        pages = [tile("page%d" % t, [P, T], F32) for t in range(PACK - 1)]
+        page = [pages[t % (PACK - 1)] for t in range(PACK)]
+        y_bf = [tile("y_bf%d" % q, [P, PIECE, PACK], BF16) for q in range(PIECES)]
+        y_codes = [tile("y_codes%d" % q, [P, PIECE], I32) for q in range(PIECES)]
+        y_scale = tile("y_scale", [P, T], U8)
+        acc = {(t, c): ps.tile([P, HALF], F32, name="acc%d%d" % (t, c)) for t in range(PACK) for c in range(2)}
+
+        x_rows = x.rearrange("(a p i) j -> a p i j", a=PASSES, i=PACK)
+        h_rows = hT.rearrange("(p t) c -> t p c", t=PACK)
+        y_rows = out_0.rearrange("(p t) c -> t p c", t=PACK)
+        y_words = out_1[0].rearrange("p t i -> p (t i)").bitcast(I32)
+
+        def cols(c):
+            return slice(c * HALF, (c + 1) * HALF)
+
+        def entries(c):
+            return offsets[:, c * HALF // 16 : (c + 1) * HALF // 16]
+
+        def load_x(c, a):
+            nc.sync.dma_start(out=x_raw[c, a][:], in_=x_rows[a][:, :, cols(c)])
+
+        nc.vector.memset(wn_scale_raw[:].bitcast(I32), 0)
+        nc.vector.memset(table_scale[:].bitcast(I32), 0)
+        for t in range(PACK - 1):
+            nc.vector.memset(pages[t][:], 0.0)
+
+        nc.sync.dma_start(offsets[:], offs)
+        nc.sync.dma_start(
+            out=wn_raw[:].rearrange("p (a w) -> p a w", a=PASSES),
+            in_=wn_words.bitcast(I32).rearrange("a p w -> p a w"),
+        )
+        nc.sync.dma_start(out=table[:], in_=tab_words[0].rearrange("p t i -> p (t i)").bitcast(I32))
+        for q in range(4):
+            nc.sync.dma_start(
+                out=wn_scale_raw[32 * q : 32 * q + 4, :].bitcast(I32).rearrange("r (a w) -> r a w", a=PASSES),
+                in_=wn_scales.bitcast(I32)[:, 4 * q : 4 * q + 4, :].rearrange("a r w -> r a w"),
+            )
+        load_x(0, 0)
+        for q in range(4):
+            nc.sync.dma_start(
+                out=table_scale[32 * q : 32 * q + 4, :].bitcast(I32),
+                in_=tab_scales.bitcast(I32)[0, 4 * q : 4 * q + 4, :],
+            )
+        load_x(0, 1)
+        nc.sync.dma_start(out=bias[:], in_=bn.rearrange("(p t) -> p t", t=PACK))
+        nc.sync.dma_start(out=un_raw[:], in_=un.rearrange("(p i) n -> p i n", i=PACK))
+        nc.sync.dma_start(out=state[0][:], in_=h_rows[0])
+        nc.sync.dma_start(out=weight[:, cols(0)], in_=wgo[:, cols(0)])
+        load_x(1, 0)
+        nc.sync.dma_start(out=state[1][:], in_=h_rows[1])
+        load_x(1, 1)
+        nc.sync.dma_start(out=state[2][:], in_=h_rows[2])
+        nc.sync.dma_start(out=weight[:, cols(1)], in_=wgo[:, cols(1)])
+        nc.sync.dma_start(out=state[3][:], in_=h_rows[3])
+
+        nc.vector.tensor_copy(
+            out=wn_dealt[:].bitcast(U16).rearrange("p (a t m) -> p a m t", a=PASSES, t=PACK),
+            in_=wn_raw[:].bitcast(U16).rearrange("p (a m t) -> p a m t", a=PASSES, t=PACK),
+        )
+        nc.vector.tensor_copy(
+            out=wn_scale[:].rearrange("p (a t m) -> p a m t", a=PASSES, t=PACK),
+            in_=wn_scale_raw[:].rearrange("p (a m t) -> p a m t", a=PASSES, t=PACK),
+        )
+        for c in range(2):
+            nc.vector.tensor_copy(picked[c][:].bitcast(U32), table[:].bitcast(U32).indirect(entries(c)))
+        for c in range(2):
+            nc.vector.tensor_copy(picked_scale[c][:], table_scale[:].indirect(entries(c)))
+
+        def round_x(c, a):
+            nc.scalar.copy(
+                out=x_bf[c, a][:].rearrange("p (g e i) -> p g i e", e=4, i=PACK),
+                in_=x_raw[c, a][:].rearrange("p i (g e) -> p g i e", e=4),
+            )
+
+        def quantize_x(c, a):
+            nc.vector.quantize_mx(out=x_codes[c, a][:].bitcast(FP8X4), scales=x_scale[c, a][:], in_=x_bf[c, a][:])
+
+        def message_pass(t, c, a):
+            first = (a * PACK + t) * P
+            nc.tensor.matmul_mx(
+                out=acc[t, c][:],
+                lhsT=wn_dealt[:].bitcast(U8)[:, 2 * first : 2 * (first + P)].bitcast(FP4X4),
+                lhsT_scale=wn_scale[:, first : first + P],
+                rhs=x_codes[c, a][:].bitcast(FP8X4),
+                rhs_scale=x_scale[c, a][:],
+                start=(a == 0),
+                stop=False,
+            )
+
+        def state_pass(t, c):
+            nc.tensor.matmul_mx(
+                out=acc[t, c][:],
+                lhsT=un_codes[:, t * P : (t + 1) * P].bitcast(FP8X4),
+                lhsT_scale=un_scale[:, t * P : (t + 1) * P],
+                rhs=picked[c][:].bitcast(FP8X4),
+                rhs_scale=picked_scale[c][:],
+                start=False,
+                stop=True,
+            )
+
+        def activate(t, c):
+            nc.scalar.activation(out=act[t][:, cols(c)], in_=acc[t, c][:], func=TANH, bias=bias[:, t : t + 1])
+
+        def gather_add(t, c):
+            nc.vector.tensor_tensor(updated[t][:, cols(c)], state[t][:].indirect(entries(c)), act[t][:, cols(c)], ADD)
+
+        def scatter(t, c):
+            nc.vector.tensor_tensor(page[t][:].indirect(entries(c)), updated[t][:, cols(c)], weight[:, cols(c)], MULT)
+
+        def weave(engine_copy, t, q):
+            engine_copy(out=y_bf[q][:, :, t], in_=page[t][:, q * PIECE : (q + 1) * PIECE])
+
+        def finish_plane(t):
+            nc.sync.dma_start(out=y_rows[t], in_=page[t][:])
+            for q in range(PIECES):
+                if t == 2 and q >= 2:
+                    piece = page[t][:, q * PIECE : (q + 1) * PIECE]
+                    nc.scalar.copy(out=y_bf[q][:, :, 2:4], in_=piece.unsqueeze(2).to_broadcast([P, PIECE, 2]))
+                else:
+                    weave(nc.scalar.copy, t, q)
+
+        un_view = un_raw[:].rearrange("p i (m t) -> p m i t", t=PACK)
+        for a in range(PASSES):
+            round_x(0, a)
+            quantize_x(0, a)
+            for t in range(PACK):
+                message_pass(t, 0, a)
+        for t in range(2):
+            nc.vector.tensor_copy(out=un_bf[t][:].rearrange("p (m i) -> p m i", i=PACK), in_=un_view[:, :, :, t])
+            nc.vector.quantize_mx(
+                out=un_codes[:, t * P : (t + 1) * P].bitcast(FP8X4), scales=un_scale[:, t * P : (t + 1) * P], in_=un_bf[t][:]
+            )
+        nc.scalar.copy(out=un_bf[2][:].rearrange("p (t m i) -> p m i t", t=2, i=PACK), in_=un_view[:, :, :, 2:4])
+        nc.vector.quantize_mx(out=un_codes[:, 2 * P :].bitcast(FP8X4), scales=un_scale[:, 2 * P :], in_=un_bf[2][:])
+        for t in range(PACK):
+            state_pass(t, 0)
+            activate(t, 0)
+
+        gather_add(0, 0)
+        scatter(0, 0)
+        round_x(1, 0)
+        gather_add(1, 0)
+        quantize_x(1, 0)
+        for t in range(PACK):
+            message_pass(t, 1, 0)
+        scatter(1, 0)
+        round_x(1, 1)
+        quantize_x(1, 1)
+        for t in range(PACK):
+            message_pass(t, 1, 1)
+            state_pass(t, 1)
+            activate(t, 1)
+        gather_add(2, 0)
+        gather_add(0, 1)
+        gather_add(1, 1)
+        scatter(0, 1)
+        finish_plane(0)
+        gather_add(2, 1)
+        scatter(1, 1)
+        finish_plane(1)
+        nc.vector.tensor_tensor(updated[3][:], state[3][:].indirect(offsets[:]), act[3][:], ADD)
+        nc.vector.tensor_tensor(page[2][:].indirect(offsets[:]), updated[2][:], weight[:], MULT)
+        finish_plane(2)
+        nc.vector.tensor_tensor(page[3][:].indirect(offsets[:]), updated[3][:], weight[:], MULT)
+        nc.sync.dma_start(out=y_rows[3], in_=page[3][:])
+        for q in (0, 1):
+            weave(nc.scalar.copy, 3, q)
+        for q in (2, 3):
+            weave(nc.vector.tensor_copy, 3, q)
+        for q in (2, 3, 0, 1):
+            nc.vector.quantize_mx(
+                out=y_codes[q][:].bitcast(FP8X4),
+                scales=y_scale[:, q * PIECE : (q + 1) * PIECE],
+                in_=y_bf[q][:].rearrange("p c i -> p (c i)"),
+            )
+            nc.sync.dma_start(out=y_words[:, q * PIECE : (q + 1) * PIECE], in_=y_codes[q][:])
+        for q in range(4):
+            nc.scalar.dma_start(
+                out=out_2.bitcast(I32)[0, 4 * q : 4 * q + 4, :], in_=y_scale[32 * q : 32 * q + 4, :].bitcast(I32)
+            )

@@ -33,33 +33,33 @@ def tile_list_tgn_rnnP_kernel(
         sb = ctx.enter_context(tc.tile_pool(name="sb", bufs=1))
         ps = ctx.enter_context(tc.psum_pool(name="ps", bufs=1))
 
-        def tile(name, shape, dtype):
-            return sb.tile(shape, dtype, name=name, align_bytes=64)
+        def tile(name, shape, dtype, tag=None):
+            return sb.tile(shape, dtype, name=name, tag=tag or name, align_bytes=64)
 
         offsets = tile("offsets", [P, J // 16], U16)
         wn_raw = tile("wn_raw", [P, PASSES * N // 2], I32)
         wn_dealt = tile("wn_dealt", [P, PASSES * N // 2], I32)
         wn_scale_raw = tile("wn_scale_raw", [P, PASSES * N], U8)
-        wn_scale = tile("wn_scale", [P, PASSES * N], U8)
         table = tile("table", [P, T], I32)
         table_scale = tile("table_scale", [P, T], U8)
         picked = [tile("picked%d" % c, [P, HALF], I32) for c in range(2)]
         picked_scale = [tile("picked_scale%d" % c, [P, HALF], U8) for c in range(2)]
-        un_raw = tile("un_raw", [P, PACK, N], F32)
-        un_bf = [tile("un_bf0", [P, P * PACK], BF16), tile("un_bf1", [P, P * PACK], BF16), tile("un_bf23", [P, 2 * P * PACK], BF16)]
+        un_raw = tile("un_raw", [P, PACK, N], F32, "slot_c")
         un_codes = tile("un_codes", [P, N], U32)
         un_scale = tile("un_scale", [P, N], U8)
         bias = tile("bias", [P, PACK], F32)
         weight = tile("weight", [P, J], F32)
-        x_raw = {(c, a): tile("x_raw%d%d" % (c, a), [P, PACK, HALF], F32) for c in range(2) for a in range(PASSES)}
-        x_bf = {(c, a): tile("x_bf%d%d" % (c, a), [P, HALF * PACK], BF16) for c in range(2) for a in range(PASSES)}
+        x_slot = {(0, 0): "slot_a", (0, 1): "slot_b", (1, 0): "slot_b", (1, 1): "slot_c"}
+        x_raw = {}
+        x_bf = {ca: tile("x_bf%d%d" % ca, [P, HALF * PACK], BF16) for ca in ((0, 0), (1, 0), (1, 1))}
         x_codes = {(c, a): tile("x_codes%d%d" % (c, a), [P, HALF], U32) for c in range(2) for a in range(PASSES)}
         x_scale = {(c, a): tile("x_scale%d%d" % (c, a), [P, HALF], U8) for c in range(2) for a in range(PASSES)}
-        state = [tile("state%d" % t, [P, T], F32) for t in range(PACK)]
+        state_slot = {0: "state0", 1: "slot_a", 2: "picked1", 3: "slot_b"}
+        state = {}
         act = [tile("act%d" % t, [P, J], F32) for t in range(PACK)]
-        updated = [tile("updated%d" % t, [P, J], F32) for t in range(PACK)]
-        pages = [tile("page%d" % t, [P, T], F32) for t in range(PACK - 1)]
-        page = [pages[t % (PACK - 1)] for t in range(PACK)]
+        updated = {t: tile("updated%d" % t, [P, J], F32) for t in (0, 1, 3)}
+        page = {0: tile("page0", [P, T], F32)}
+        page[3] = page[0]
         y_bf = [tile("y_bf%d" % q, [P, PIECE, PACK], BF16) for q in range(PIECES)]
         y_codes = [tile("y_codes%d" % q, [P, PIECE], I32) for q in range(PIECES)]
         y_scale = tile("y_scale", [P, T], U8)
@@ -76,13 +76,17 @@ def tile_list_tgn_rnnP_kernel(
         def entries(c):
             return offsets[:, c * HALF // 16 : (c + 1) * HALF // 16]
 
+        def load_state(t):
+            state[t] = tile("state%d" % t, [P, T], F32, state_slot[t])
+            nc.sync.dma_start(out=state[t][:], in_=h_rows[t])
+
         def load_x(c, a):
+            x_raw[c, a] = tile("x_raw%d%d" % (c, a), [P, PACK, HALF], F32, x_slot[c, a])
             nc.sync.dma_start(out=x_raw[c, a][:], in_=x_rows[a][:, :, cols(c)])
 
         nc.vector.memset(wn_scale_raw[:].bitcast(I32), 0)
         nc.vector.memset(table_scale[:].bitcast(I32), 0)
-        for t in range(PACK - 1):
-            nc.vector.memset(pages[t][:], 0.0)
+        nc.vector.memset(page[0][:], 0.0)
 
         nc.sync.dma_start(offsets[:], offs)
         nc.sync.dma_start(
@@ -92,50 +96,45 @@ def tile_list_tgn_rnnP_kernel(
         nc.sync.dma_start(out=table[:], in_=tab_words[0].rearrange("p t i -> p (t i)").bitcast(I32))
         for q in range(4):
             nc.sync.dma_start(
-                out=wn_scale_raw[32 * q : 32 * q + 4, :].bitcast(I32).rearrange("r (a w) -> r a w", a=PASSES),
-                in_=wn_scales.bitcast(I32)[:, 4 * q : 4 * q + 4, :].rearrange("a r w -> r a w"),
+                out=table_scale[32 * q : 32 * q + 4, :].bitcast(I32),
+                in_=tab_scales.bitcast(I32)[0, 4 * q : 4 * q + 4, :],
             )
         load_x(0, 0)
         for q in range(4):
             nc.sync.dma_start(
-                out=table_scale[32 * q : 32 * q + 4, :].bitcast(I32),
-                in_=tab_scales.bitcast(I32)[0, 4 * q : 4 * q + 4, :],
+                out=wn_scale_raw[32 * q : 32 * q + 4, :].bitcast(I32).rearrange("r (a w) -> r a w", a=PASSES),
+                in_=wn_scales.bitcast(I32)[:, 4 * q : 4 * q + 4, :].rearrange("a r w -> r a w"),
             )
         load_x(0, 1)
         nc.sync.dma_start(out=bias[:], in_=bn.rearrange("(p t) -> p t", t=PACK))
         nc.sync.dma_start(out=un_raw[:], in_=un.rearrange("(p i) n -> p i n", i=PACK))
-        nc.sync.dma_start(out=state[0][:], in_=h_rows[0])
-        nc.sync.dma_start(out=weight[:, cols(0)], in_=wgo[:, cols(0)])
-        load_x(1, 0)
-        nc.sync.dma_start(out=state[1][:], in_=h_rows[1])
-        load_x(1, 1)
-        nc.sync.dma_start(out=state[2][:], in_=h_rows[2])
-        nc.sync.dma_start(out=weight[:, cols(1)], in_=wgo[:, cols(1)])
-        nc.sync.dma_start(out=state[3][:], in_=h_rows[3])
+        load_state(0)
+        nc.sync.dma_start(out=weight[:], in_=wgo)
 
         nc.vector.tensor_copy(
-            out=wn_dealt[:].bitcast(U16).rearrange("p (a t m) -> p a m t", a=PASSES, t=PACK),
-            in_=wn_raw[:].bitcast(U16).rearrange("p (a m t) -> p a m t", a=PASSES, t=PACK),
-        )
-        nc.vector.tensor_copy(
-            out=wn_scale[:].rearrange("p (a t m) -> p a m t", a=PASSES, t=PACK),
-            in_=wn_scale_raw[:].rearrange("p (a m t) -> p a m t", a=PASSES, t=PACK),
+            out=wn_dealt[:].bitcast(U16).rearrange("p (a t m) -> p a t m", a=PASSES, t=PACK),
+            in_=wn_raw[:].bitcast(U16).rearrange("p (a m t) -> p a t m", a=PASSES, t=PACK),
         )
         for c in range(2):
             nc.vector.tensor_copy(picked[c][:].bitcast(U32), table[:].bitcast(U32).indirect(entries(c)))
         for c in range(2):
             nc.vector.tensor_copy(picked_scale[c][:], table_scale[:].indirect(entries(c)))
+        wn_scale = tile("wn_scale", [P, PASSES * N], U8, "table")
+        nc.vector.tensor_copy(
+            out=wn_scale[:].rearrange("p (a t m) -> p a t m", a=PASSES, t=PACK),
+            in_=wn_scale_raw[:].rearrange("p (a m t) -> p a t m", a=PASSES, t=PACK),
+        )
 
-        def round_x(c, a):
-            nc.scalar.copy(
-                out=x_bf[c, a][:].rearrange("p (g e i) -> p g i e", e=4, i=PACK),
-                in_=x_raw[c, a][:].rearrange("p i (g e) -> p g i e", e=4),
+        def round_x(c, a, engine_copy=nc.scalar.copy, first=0, last=HALF):
+            engine_copy(
+                out=x_bf[c, a][:, first * PACK : last * PACK].rearrange("p (g e i) -> p g i e", e=4, i=PACK),
+                in_=x_raw[c, a][:, :, first:last].rearrange("p i (g e) -> p g i e", e=4),
             )
 
         def quantize_x(c, a):
             nc.vector.quantize_mx(out=x_codes[c, a][:].bitcast(FP8X4), scales=x_scale[c, a][:], in_=x_bf[c, a][:])
 
-        def message_pass(t, c, a):
+        def message_pass(t, c, a, start=False, stop=False):
             first = (a * PACK + t) * P
             nc.tensor.matmul_mx(
                 out=acc[t, c][:],
@@ -143,19 +142,19 @@ def tile_list_tgn_rnnP_kernel(
                 lhsT_scale=wn_scale[:, first : first + P],
                 rhs=x_codes[c, a][:].bitcast(FP8X4),
                 rhs_scale=x_scale[c, a][:],
-                start=(a == 0),
-                stop=False,
+                start=start,
+                stop=stop,
             )
 
-        def state_pass(t, c):
+        def state_pass(t, c, start=False, stop=False):
             nc.tensor.matmul_mx(
                 out=acc[t, c][:],
                 lhsT=un_codes[:, t * P : (t + 1) * P].bitcast(FP8X4),
                 lhsT_scale=un_scale[:, t * P : (t + 1) * P],
                 rhs=picked[c][:].bitcast(FP8X4),
                 rhs_scale=picked_scale[c][:],
-                start=False,
-                stop=True,
+                start=start,
+                stop=stop,
             )
 
         def activate(t, c):
@@ -172,7 +171,7 @@ def tile_list_tgn_rnnP_kernel(
 
         def finish_plane(t):
             nc.sync.dma_start(out=y_rows[t], in_=page[t][:])
-            for q in range(PIECES):
+            for q in (2, 3, 0, 1):
                 if t == 2 and q >= 2:
                     piece = page[t][:, q * PIECE : (q + 1) * PIECE]
                     nc.scalar.copy(out=y_bf[q][:, :, 2:4], in_=piece.unsqueeze(2).to_broadcast([P, PIECE, 2]))
@@ -180,36 +179,62 @@ def tile_list_tgn_rnnP_kernel(
                     weave(nc.scalar.copy, t, q)
 
         un_view = un_raw[:].rearrange("p i (m t) -> p m i t", t=PACK)
-        for a in range(PASSES):
-            round_x(0, a)
-            quantize_x(0, a)
-            for t in range(PACK):
-                message_pass(t, 0, a)
-        for t in range(2):
-            nc.vector.tensor_copy(out=un_bf[t][:].rearrange("p (m i) -> p m i", i=PACK), in_=un_view[:, :, :, t])
+        round_x(0, 0)
+        load_state(1)
+        quantize_x(0, 0)
+        message_pass(0, 0, 0, start=True)
+        x_bf[0, 1] = tile("x_bf01", [P, HALF * PACK], BF16, "table_scale")
+        round_x(0, 1, nc.scalar.copy, 0, HALF // 2)
+        round_x(0, 1, nc.vector.tensor_copy, HALF // 2, HALF)
+        load_x(1, 0)
+        quantize_x(0, 1)
+        message_pass(0, 0, 1)
+
+        def quantize_un(first, last, source):
             nc.vector.quantize_mx(
-                out=un_codes[:, t * P : (t + 1) * P].bitcast(FP8X4), scales=un_scale[:, t * P : (t + 1) * P], in_=un_bf[t][:]
+                out=un_codes[:, first * P : last * P].bitcast(FP8X4), scales=un_scale[:, first * P : last * P], in_=source
             )
-        nc.scalar.copy(out=un_bf[2][:].rearrange("p (t m i) -> p m i t", t=2, i=PACK), in_=un_view[:, :, :, 2:4])
-        nc.vector.quantize_mx(out=un_codes[:, 2 * P :].bitcast(FP8X4), scales=un_scale[:, 2 * P :], in_=un_bf[2][:])
-        for t in range(PACK):
-            state_pass(t, 0)
+
+        un_first = tile("un_first", [P, P * PACK], BF16, "table_scale")
+        nc.vector.tensor_copy(out=un_first[:].rearrange("p (m i) -> p m i", i=PACK), in_=un_view[:, :, :, 0])
+        quantize_un(0, 1, un_first[:])
+        un_rest = tile("un_rest", [P, 3 * P * PACK], BF16, "slot_d")
+        nc.scalar.copy(out=un_rest[:].rearrange("p (t m i) -> p m i t", t=3, i=PACK), in_=un_view[:, :, :, 1:4])
+        load_x(1, 1)
+        state_pass(0, 0, stop=True)
+        activate(0, 0)
+        quantize_un(1, 2, un_rest[:, : P * PACK])
+        quantize_un(2, 4, un_rest[:, P * PACK :])
+        page[1] = tile("page1", [P, T], F32, "slot_d")
+        nc.gpsimd.memset(page[1][:], 0.0)
+        for t in range(1, PACK):
+            state_pass(t, 0, start=True)
+            message_pass(t, 0, 0)
+            message_pass(t, 0, 1, stop=True)
             activate(t, 0)
+        for t in range(PACK):
+            state_pass(t, 1, start=True)
+        load_state(2)
 
         gather_add(0, 0)
         scatter(0, 0)
         round_x(1, 0)
+        load_state(3)
         gather_add(1, 0)
         quantize_x(1, 0)
-        for t in range(PACK):
-            message_pass(t, 1, 0)
+        message_pass(0, 1, 0)
         scatter(1, 0)
         round_x(1, 1)
         quantize_x(1, 1)
-        for t in range(PACK):
+        message_pass(0, 1, 1, stop=True)
+        activate(0, 1)
+        for t in range(1, PACK):
             message_pass(t, 1, 1)
-            state_pass(t, 1)
+            message_pass(t, 1, 0, stop=True)
             activate(t, 1)
+        page[2] = tile("page2", [P, T], F32, "x_codes11")
+        nc.gpsimd.memset(page[2][:], 0.0)
+        updated[2] = tile("updated2", [P, J], F32, "x_bf11")
         gather_add(2, 0)
         gather_add(0, 1)
         gather_add(1, 1)

@@ -36,28 +36,32 @@ def tile_list_tgn_rnnP_kernel(
         def tile(name, shape, dtype, tag=None):
             return sb.tile(shape, dtype, name=name, tag=tag or name, align_bytes=64)
 
+        halves = [(c, a) for c in range(2) for a in range(PASSES)]
         offsets = tile("offsets", [P, J // 16], U16)
         wn_raw = tile("wn_raw", [P, PASSES * N // 2], I32)
         wn_dealt = tile("wn_dealt", [P, PASSES * N // 2], I32)
         wn_scale_raw = tile("wn_scale_raw", [P, PASSES * N], U8)
+        wn_scale = tile("wn_scale", [P, PASSES * N], U8)
         table = tile("table", [P, T], I32)
         table_scale = tile("table_scale", [P, T], U8)
-        picked = [tile("picked%d" % c, [P, HALF], I32) for c in range(2)]
-        picked_scale = [tile("picked_scale%d" % c, [P, HALF], U8) for c in range(2)]
-        un_raw = tile("un_raw", [P, PACK, N], F32, "slot_c")
+        picked = tile("picked", [P, J], I32)
+        picked_scale = {0: tile("picked_scale0", [P, HALF], U8)}
+        un_raw = tile("un_raw", [P, PACK, N], F32)
         un_codes = tile("un_codes", [P, N], U32)
         un_scale = tile("un_scale", [P, N], U8)
         bias = tile("bias", [P, PACK], F32)
         weight = tile("weight", [P, J], F32)
-        x_slot = {(0, 0): "slot_a", (0, 1): "slot_b", (1, 0): "slot_b", (1, 1): "slot_c"}
-        x_raw = {}
-        x_bf = {ca: tile("x_bf%d%d" % ca, [P, HALF * PACK], BF16) for ca in ((0, 0), (1, 0), (1, 1))}
-        x_codes = {(c, a): tile("x_codes%d%d" % (c, a), [P, HALF], U32) for c in range(2) for a in range(PASSES)}
-        x_scale = {(c, a): tile("x_scale%d%d" % (c, a), [P, HALF], U8) for c in range(2) for a in range(PASSES)}
-        state_slot = {0: "state0", 1: "slot_a", 2: "picked1", 3: "slot_b"}
-        state = {}
-        act = [tile("act%d" % t, [P, J], F32) for t in range(PACK)]
-        updated = {t: tile("updated%d" % t, [P, J], F32) for t in (0, 1, 3)}
+        x_raw = {ca: tile("x_raw%d%d" % ca, [P, PACK, HALF], F32) for ca in halves}
+        x_bf = {(0, a): tile("x_bf0%d" % a, [P, HALF * PACK], BF16) for a in range(PASSES)}
+        x_codes = {ca: tile("x_codes%d%d" % ca, [P, HALF], U32) for ca in halves}
+        x_scale = {ca: tile("x_scale%d%d" % ca, [P, HALF], U8) for ca in halves}
+        state = [tile("state%d" % t, [P, T], F32) for t in range(PACK)]
+        act = {(t, c): tile("act%d%d" % (t, c), [P, HALF], F32) for t in range(PACK) for c in range(2)}
+        updated = {(t, c): tile("updated%d%d" % (t, c), [P, HALF], F32)[:] for t in (0, 1) for c in range(2)}
+        updated_whole = {t: tile("updated%d" % t, [P, J], F32) for t in (2, 3)}
+        for t in (2, 3):
+            for c in range(2):
+                updated[t, c] = updated_whole[t][:, c * HALF : (c + 1) * HALF]
         page = {0: tile("page0", [P, T], F32)}
         page[3] = page[0]
         y_bf = [tile("y_bf%d" % q, [P, PIECE, PACK], BF16) for q in range(PIECES)]
@@ -77,15 +81,16 @@ def tile_list_tgn_rnnP_kernel(
             return offsets[:, c * HALF // 16 : (c + 1) * HALF // 16]
 
         def load_state(t):
-            state[t] = tile("state%d" % t, [P, T], F32, state_slot[t])
             nc.sync.dma_start(out=state[t][:], in_=h_rows[t])
 
         def load_x(c, a):
-            x_raw[c, a] = tile("x_raw%d%d" % (c, a), [P, PACK, HALF], F32, x_slot[c, a])
             nc.sync.dma_start(out=x_raw[c, a][:], in_=x_rows[a][:, :, cols(c)])
 
-        nc.vector.memset(wn_scale_raw[:].bitcast(I32), 0)
-        nc.vector.memset(table_scale[:].bitcast(I32), 0)
+        def load_weight(c):
+            nc.sync.dma_start(out=weight[:, cols(c)], in_=wgo[:, cols(c)])
+
+        nc.gpsimd.memset(wn_scale_raw[:].bitcast(I32), 0)
+        nc.gpsimd.memset(table_scale[:].bitcast(I32), 0)
         nc.vector.memset(page[0][:], 0.0)
 
         nc.sync.dma_start(offsets[:], offs)
@@ -93,37 +98,40 @@ def tile_list_tgn_rnnP_kernel(
             out=wn_raw[:].rearrange("p (a w) -> p a w", a=PASSES),
             in_=wn_words.bitcast(I32).rearrange("a p w -> p a w"),
         )
-        nc.sync.dma_start(out=table[:], in_=tab_words[0].rearrange("p t i -> p (t i)").bitcast(I32))
-        for q in range(4):
-            nc.sync.dma_start(
-                out=table_scale[32 * q : 32 * q + 4, :].bitcast(I32),
-                in_=tab_scales.bitcast(I32)[0, 4 * q : 4 * q + 4, :],
-            )
-        load_x(0, 0)
         for q in range(4):
             nc.sync.dma_start(
                 out=wn_scale_raw[32 * q : 32 * q + 4, :].bitcast(I32).rearrange("r (a w) -> r a w", a=PASSES),
                 in_=wn_scales.bitcast(I32)[:, 4 * q : 4 * q + 4, :].rearrange("a r w -> r a w"),
             )
-        load_x(0, 1)
+        nc.sync.dma_start(out=table[:], in_=tab_words[0].rearrange("p t i -> p (t i)").bitcast(I32))
+        for q in range(4):
+            nc.sync.dma_start(
+                out=table_scale[32 * q + 4 : 32 * q + 8, :].bitcast(I32),
+                in_=tab_scales.bitcast(I32)[0, 4 * q : 4 * q + 4, :],
+            )
+        load_x(0, 0)
         nc.sync.dma_start(out=bias[:], in_=bn.rearrange("(p t) -> p t", t=PACK))
+        load_x(0, 1)
         nc.sync.dma_start(out=un_raw[:], in_=un.rearrange("(p i) n -> p i n", i=PACK))
         load_state(0)
-        nc.sync.dma_start(out=weight[:], in_=wgo)
+        load_weight(0)
+        load_state(1)
+        load_x(1, 0)
+        load_x(1, 1)
+        load_state(2)
+        load_weight(1)
+        load_state(3)
 
         nc.vector.tensor_copy(
             out=wn_dealt[:].bitcast(U16).rearrange("p (a t m) -> p a t m", a=PASSES, t=PACK),
             in_=wn_raw[:].bitcast(U16).rearrange("p (a m t) -> p a t m", a=PASSES, t=PACK),
         )
-        for c in range(2):
-            nc.vector.tensor_copy(picked[c][:].bitcast(U32), table[:].bitcast(U32).indirect(entries(c)))
-        for c in range(2):
-            nc.vector.tensor_copy(picked_scale[c][:], table_scale[:].indirect(entries(c)))
-        wn_scale = tile("wn_scale", [P, PASSES * N], U8, "table")
         nc.vector.tensor_copy(
             out=wn_scale[:].rearrange("p (a t m) -> p a t m", a=PASSES, t=PACK),
             in_=wn_scale_raw[:].rearrange("p (a m t) -> p a t m", a=PASSES, t=PACK),
         )
+        nc.vector.tensor_copy(picked[:].bitcast(U32), table[:].bitcast(U32).indirect(offsets[:]))
+        nc.vector.tensor_copy(picked_scale[0][:], table_scale[:].indirect(entries(0)))
 
         def round_x(c, a, engine_copy=nc.scalar.copy, first=0, last=HALF):
             engine_copy(
@@ -151,20 +159,23 @@ def tile_list_tgn_rnnP_kernel(
                 out=acc[t, c][:],
                 lhsT=un_codes[:, t * P : (t + 1) * P].bitcast(FP8X4),
                 lhsT_scale=un_scale[:, t * P : (t + 1) * P],
-                rhs=picked[c][:].bitcast(FP8X4),
-                rhs_scale=picked_scale[c][:],
+                rhs=picked[:, cols(c)].bitcast(FP8X4),
+                rhs_scale=picked_scale[c][4:P, :],
                 start=start,
                 stop=stop,
             )
 
         def activate(t, c):
-            nc.scalar.activation(out=act[t][:, cols(c)], in_=acc[t, c][:], func=TANH, bias=bias[:, t : t + 1])
+            nc.scalar.activation(out=act[t, c][:], in_=acc[t, c][:], func=TANH, bias=bias[:, t : t + 1])
 
         def gather_add(t, c):
-            nc.vector.tensor_tensor(updated[t][:, cols(c)], state[t][:].indirect(entries(c)), act[t][:, cols(c)], ADD)
+            nc.vector.tensor_tensor(updated[t, c], state[t][:].indirect(entries(c)), act[t, c][:], ADD)
 
         def scatter(t, c):
-            nc.vector.tensor_tensor(page[t][:].indirect(entries(c)), updated[t][:, cols(c)], weight[:, cols(c)], MULT)
+            nc.vector.tensor_tensor(page[t][:].indirect(entries(c)), updated[t, c], weight[:, cols(c)], MULT)
+
+        def scatter_whole(t):
+            nc.vector.tensor_tensor(page[t][:].indirect(offsets[:]), updated_whole[t][:], weight[:], MULT)
 
         def weave(engine_copy, t, q):
             engine_copy(out=y_bf[q][:, :, t], in_=page[t][:, q * PIECE : (q + 1) * PIECE])
@@ -178,54 +189,52 @@ def tile_list_tgn_rnnP_kernel(
                 else:
                     weave(nc.scalar.copy, t, q)
 
-        un_view = un_raw[:].rearrange("p i (m t) -> p m i t", t=PACK)
-        round_x(0, 0)
-        load_state(1)
-        quantize_x(0, 0)
-        message_pass(0, 0, 0, start=True)
-        x_bf[0, 1] = tile("x_bf01", [P, HALF * PACK], BF16, "table_scale")
-        round_x(0, 1, nc.scalar.copy, 0, HALF // 2)
-        round_x(0, 1, nc.vector.tensor_copy, HALF // 2, HALF)
-        load_x(1, 0)
-        quantize_x(0, 1)
-        message_pass(0, 0, 1)
-
         def quantize_un(first, last, source):
             nc.vector.quantize_mx(
                 out=un_codes[:, first * P : last * P].bitcast(FP8X4), scales=un_scale[:, first * P : last * P], in_=source
             )
 
-        un_first = tile("un_first", [P, P * PACK], BF16, "table_scale")
-        nc.vector.tensor_copy(out=un_first[:].rearrange("p (m i) -> p m i", i=PACK), in_=un_view[:, :, :, 0])
-        quantize_un(0, 1, un_first[:])
-        un_rest = tile("un_rest", [P, 3 * P * PACK], BF16, "slot_d")
+        un_view = un_raw[:].rearrange("p i (m t) -> p m i t", t=PACK)
+        for a in range(PASSES):
+            round_x(0, a, nc.scalar.copy, 0, HALF // 2)
+            round_x(0, a, nc.vector.tensor_copy, HALF // 2, HALF)
+            quantize_x(0, a)
+            message_pass(0, 0, a, start=a == 0)
+
+        un_bf0 = tile("un_bf0", [P, P * PACK], BF16)
+        nc.vector.tensor_copy(out=un_bf0[:].rearrange("p (m i) -> p m i", i=PACK), in_=un_view[:, :, :, 0])
+        quantize_un(0, 1, un_bf0[:])
+        un_rest = tile("un_rest", [P, 3 * P * PACK], BF16, "page1")
         nc.scalar.copy(out=un_rest[:].rearrange("p (t m i) -> p m i t", t=3, i=PACK), in_=un_view[:, :, :, 1:4])
-        load_x(1, 1)
         state_pass(0, 0, stop=True)
         activate(0, 0)
+        picked_scale[1] = tile("picked_scale1", [P, HALF], U8, "un_bf0")
+        nc.vector.tensor_copy(picked_scale[1][:], table_scale[:].indirect(entries(1)))
         quantize_un(1, 2, un_rest[:, : P * PACK])
         quantize_un(2, 4, un_rest[:, P * PACK :])
-        page[1] = tile("page1", [P, T], F32, "slot_d")
+        page[1] = tile("page1", [P, T], F32)
         nc.gpsimd.memset(page[1][:], 0.0)
+        gather_add(0, 0)
+        scatter(0, 0)
         for t in range(1, PACK):
             state_pass(t, 0, start=True)
             message_pass(t, 0, 0)
             message_pass(t, 0, 1, stop=True)
-            activate(t, 0)
         for t in range(PACK):
             state_pass(t, 1, start=True)
-        load_state(2)
-
-        gather_add(0, 0)
-        scatter(0, 0)
-        round_x(1, 0)
-        load_state(3)
+        activate(1, 0)
         gather_add(1, 0)
+        scatter(1, 0)
+        x_bf[1, 0] = tile("x_bf10", [P, HALF * PACK], BF16, "updated00")
+        round_x(1, 0)
+        x_bf[1, 1] = tile("x_bf11", [P, HALF * PACK], BF16, "x_raw10")
+        round_x(1, 1)
         quantize_x(1, 0)
         message_pass(0, 1, 0)
-        scatter(1, 0)
-        round_x(1, 1)
         quantize_x(1, 1)
+        activate(2, 0)
+        activate(3, 0)
+        gather_add(2, 0)
         message_pass(0, 1, 1, stop=True)
         activate(0, 1)
         for t in range(1, PACK):
@@ -234,8 +243,7 @@ def tile_list_tgn_rnnP_kernel(
             activate(t, 1)
         page[2] = tile("page2", [P, T], F32, "x_codes11")
         nc.gpsimd.memset(page[2][:], 0.0)
-        updated[2] = tile("updated2", [P, J], F32, "x_bf11")
-        gather_add(2, 0)
+        gather_add(3, 0)
         gather_add(0, 1)
         gather_add(1, 1)
         scatter(0, 1)
@@ -243,10 +251,10 @@ def tile_list_tgn_rnnP_kernel(
         gather_add(2, 1)
         scatter(1, 1)
         finish_plane(1)
-        nc.vector.tensor_tensor(updated[3][:], state[3][:].indirect(offsets[:]), act[3][:], ADD)
-        nc.vector.tensor_tensor(page[2][:].indirect(offsets[:]), updated[2][:], weight[:], MULT)
+        gather_add(3, 1)
+        scatter_whole(2)
         finish_plane(2)
-        nc.vector.tensor_tensor(page[3][:].indirect(offsets[:]), updated[3][:], weight[:], MULT)
+        scatter_whole(3)
         nc.sync.dma_start(out=y_rows[3], in_=page[3][:])
         for q in (0, 1):
             weave(nc.scalar.copy, 3, q)

@@ -89,8 +89,8 @@ def tile_list_tgn_rnnP_kernel(
         def load_weight(c):
             nc.sync.dma_start(out=weight[:, cols(c)], in_=wgo[:, cols(c)])
 
-        nc.gpsimd.memset(wn_scale_raw[:].bitcast(I32), 0)
         nc.gpsimd.memset(table_scale[:].bitcast(I32), 0)
+        nc.gpsimd.memset(wn_scale_raw[:].bitcast(I32), 0)
         nc.vector.memset(page[0][:], 0.0)
 
         nc.sync.dma_start(offsets[:], offs)
@@ -98,20 +98,20 @@ def tile_list_tgn_rnnP_kernel(
             out=wn_raw[:].rearrange("p (a w) -> p a w", a=PASSES),
             in_=wn_words.bitcast(I32).rearrange("a p w -> p a w"),
         )
-        for q in range(4):
-            nc.sync.dma_start(
-                out=wn_scale_raw[32 * q : 32 * q + 4, :].bitcast(I32).rearrange("r (a w) -> r a w", a=PASSES),
-                in_=wn_scales.bitcast(I32)[:, 4 * q : 4 * q + 4, :].rearrange("a r w -> r a w"),
-            )
         nc.sync.dma_start(out=table[:], in_=tab_words[0].rearrange("p t i -> p (t i)").bitcast(I32))
         for q in range(4):
             nc.sync.dma_start(
-                out=table_scale[32 * q + 4 : 32 * q + 8, :].bitcast(I32),
-                in_=tab_scales.bitcast(I32)[0, 4 * q : 4 * q + 4, :],
+                out=table_scale[4 + q : P : 32, :].bitcast(I32),
+                in_=tab_scales.bitcast(I32)[0, q:16:4, :],
             )
         load_x(0, 0)
-        nc.sync.dma_start(out=bias[:], in_=bn.rearrange("(p t) -> p t", t=PACK))
+        for q in range(4):
+            nc.sync.dma_start(
+                out=wn_scale_raw[q:P:32, :].bitcast(I32).rearrange("r (a w) -> r a w", a=PASSES),
+                in_=wn_scales.bitcast(I32)[:, q:16:4, :].rearrange("a r w -> r a w"),
+            )
         load_x(0, 1)
+        nc.sync.dma_start(out=bias[:], in_=bn.rearrange("(p t) -> p t", t=PACK))
         nc.sync.dma_start(out=un_raw[:], in_=un.rearrange("(p i) n -> p i n", i=PACK))
         load_state(0)
         load_weight(0)
@@ -195,11 +195,13 @@ def tile_list_tgn_rnnP_kernel(
             )
 
         un_view = un_raw[:].rearrange("p i (m t) -> p m i t", t=PACK)
-        for a in range(PASSES):
-            round_x(0, a, nc.scalar.copy, 0, HALF // 2)
-            round_x(0, a, nc.vector.tensor_copy, HALF // 2, HALF)
-            quantize_x(0, a)
-            message_pass(0, 0, a, start=a == 0)
+        round_x(0, 0)
+        quantize_x(0, 0)
+        message_pass(0, 0, 0, start=True)
+        round_x(0, 1, nc.scalar.copy, 0, HALF // 2)
+        round_x(0, 1, nc.vector.tensor_copy, HALF // 2, HALF)
+        quantize_x(0, 1)
+        message_pass(0, 0, 1)
 
         un_bf0 = tile("un_bf0", [P, P * PACK], BF16)
         nc.vector.tensor_copy(out=un_bf0[:].rearrange("p (m i) -> p m i", i=PACK), in_=un_view[:, :, :, 0])
@@ -269,5 +271,5 @@ def tile_list_tgn_rnnP_kernel(
             nc.sync.dma_start(out=y_words[:, q * PIECE : (q + 1) * PIECE], in_=y_codes[q][:])
         for q in range(4):
             nc.scalar.dma_start(
-                out=out_2.bitcast(I32)[0, 4 * q : 4 * q + 4, :], in_=y_scale[32 * q : 32 * q + 4, :].bitcast(I32)
+                out=out_2.bitcast(I32)[0, q:16:4, :], in_=y_scale[q:P:32, :].bitcast(I32)
             )

@@ -1,6 +1,7 @@
 from contextlib import ExitStack
 
 import concourse.mybir as mybir
+from concourse.masks import make_identity
 
 K, M, N, T, J = 1024, 512, 512, 2048, 1024
 FLOPS = 2 * (K + M) * N * J
@@ -51,6 +52,8 @@ def tile_list_tgn_rnnP_kernel(
         un_scale = tile("un_scale", [P, N], U8)
         bias = tile("bias", [P, PACK], F32)
         weight = tile("weight", [P, J], F32)
+        weight_row = tile("weight_row", [P, J // P], F32)
+        identity = tile("identity", [P, P], F32)
         x_raw = {ca: tile("x_raw%d%d" % ca, [P, PACK, HALF], F32) for ca in halves}
         x_bf = {(0, a): tile("x_bf0%d" % a, [P, HALF * PACK], BF16) for a in range(PASSES)}
         x_codes = {ca: tile("x_codes%d%d" % ca, [P, HALF], U32) for ca in halves}
@@ -67,7 +70,8 @@ def tile_list_tgn_rnnP_kernel(
         y_bf = [tile("y_bf%d" % q, [P, PIECE, PACK], BF16) for q in range(PIECES)]
         y_codes = [tile("y_codes%d" % q, [P, PIECE], I32) for q in range(PIECES)]
         y_scale = tile("y_scale", [P, T], U8)
-        acc = {(t, c): ps.tile([P, HALF], F32, name="acc%d%d" % (t, c)) for t in range(PACK) for c in range(2)}
+        spread = [ps.tile([P, 4, P], F32, name="spread%d" % h, tag="acc%d1" % (2 + h)) for h in range(2)]
+        acc = {}
 
         x_rows = x.rearrange("(a p i) j -> a p i j", a=PASSES, i=PACK)
         h_rows = hT.rearrange("(p t) c -> t p c", t=PACK)
@@ -86,14 +90,13 @@ def tile_list_tgn_rnnP_kernel(
         def load_x(c, a):
             nc.sync.dma_start(out=x_raw[c, a][:], in_=x_rows[a][:, :, cols(c)])
 
-        def load_weight(c):
-            nc.sync.dma_start(out=weight[:, cols(c)], in_=wgo[:, cols(c)])
-
         nc.gpsimd.memset(table_scale[:].bitcast(I32), 0)
         nc.gpsimd.memset(wn_scale_raw[:].bitcast(I32), 0)
+        make_identity(nc, identity[:])
         nc.vector.memset(page[0][:], 0.0)
 
         nc.sync.dma_start(offsets[:], offs)
+        nc.sync.dma_start(out=weight_row[:], in_=wgo[0].rearrange("(r m) -> r m", m=J // P))
         nc.sync.dma_start(
             out=wn_raw[:].rearrange("p (a w) -> p a w", a=PASSES),
             in_=wn_words.bitcast(I32).rearrange("a p w -> p a w"),
@@ -114,13 +117,23 @@ def tile_list_tgn_rnnP_kernel(
         nc.sync.dma_start(out=bias[:], in_=bn.rearrange("(p t) -> p t", t=PACK))
         nc.sync.dma_start(out=un_raw[:], in_=un.rearrange("(p i) n -> p i n", i=PACK))
         load_state(0)
-        load_weight(0)
-        load_state(1)
         load_x(1, 0)
+        load_state(1)
         load_x(1, 1)
         load_state(2)
-        load_weight(1)
         load_state(3)
+
+        for h in range(2):
+            for m in range(4):
+                column = weight_row[:, 4 * h + m : 4 * h + m + 1]
+                nc.tensor.transpose(spread[h][:, m, :], column.to_broadcast([P, P]), identity[:])
+            nc.scalar.copy(
+                out=weight[:].rearrange("p (r m) -> p r m", m=J // P)[:, :, 4 * h : 4 * h + 4],
+                in_=spread[h][:].rearrange("p m r -> p r m"),
+            )
+        for t in range(PACK):
+            for c in range(2):
+                acc[t, c] = ps.tile([P, HALF], F32, name="acc%d%d" % (t, c))
 
         nc.vector.tensor_copy(
             out=wn_dealt[:].bitcast(U16).rearrange("p (a t m) -> p a t m", a=PASSES, t=PACK),
@@ -222,12 +235,11 @@ def tile_list_tgn_rnnP_kernel(
             state_pass(t, 0, start=True)
             message_pass(t, 0, 0)
             message_pass(t, 0, 1, stop=True)
-        for t in range(PACK):
-            state_pass(t, 1, start=True)
+        state_pass(0, 1, start=True)
         activate(1, 0)
         gather_add(1, 0)
         scatter(1, 0)
-        x_bf[1, 0] = tile("x_bf10", [P, HALF * PACK], BF16, "updated00")
+        x_bf[1, 0] = tile("x_bf10", [P, HALF * PACK], BF16, "act00")
         round_x(1, 0)
         x_bf[1, 1] = tile("x_bf11", [P, HALF * PACK], BF16, "x_raw10")
         round_x(1, 1)
@@ -240,16 +252,17 @@ def tile_list_tgn_rnnP_kernel(
         message_pass(0, 1, 1, stop=True)
         activate(0, 1)
         for t in range(1, PACK):
-            message_pass(t, 1, 1)
-            message_pass(t, 1, 0, stop=True)
+            message_pass(t, 1, 1, start=True)
+            message_pass(t, 1, 0)
+            state_pass(t, 1, stop=True)
             activate(t, 1)
         page[2] = tile("page2", [P, T], F32, "x_codes11")
         nc.gpsimd.memset(page[2][:], 0.0)
         gather_add(3, 0)
         gather_add(0, 1)
-        gather_add(1, 1)
         scatter(0, 1)
         finish_plane(0)
+        gather_add(1, 1)
         gather_add(2, 1)
         scatter(1, 1)
         finish_plane(1)

@@ -65,7 +65,7 @@ def tile_list_tgn_rnnP_kernel(
         for t in (2, 3):
             for c in range(2):
                 updated[t, c] = updated_whole[t][:, c * HALF : (c + 1) * HALF]
-        page = {0: tile("page0", [P, T], F32)}
+        page = {t: tile("page%d" % t, [P, T], F32) for t in range(3)}
         page[3] = page[0]
         y_bf = [tile("y_bf%d" % q, [P, PIECE, PACK], BF16) for q in range(PIECES)]
         y_codes = [tile("y_codes%d" % q, [P, PIECE], I32) for q in range(PIECES)]
@@ -93,7 +93,8 @@ def tile_list_tgn_rnnP_kernel(
         nc.gpsimd.memset(table_scale[:].bitcast(I32), 0)
         nc.gpsimd.memset(wn_scale_raw[:].bitcast(I32), 0)
         make_identity(nc, identity[:])
-        nc.vector.memset(page[0][:], 0.0)
+        for t in range(3):
+            nc.vector.memset(page[t][:].bitcast(I32), 0)
 
         nc.sync.dma_start(offsets[:], offs)
         nc.sync.dma_start(out=weight_row[:], in_=wgo[0].rearrange("(r m) -> r m", m=J // P))
@@ -219,7 +220,7 @@ def tile_list_tgn_rnnP_kernel(
         un_bf0 = tile("un_bf0", [P, P * PACK], BF16)
         nc.vector.tensor_copy(out=un_bf0[:].rearrange("p (m i) -> p m i", i=PACK), in_=un_view[:, :, :, 0])
         quantize_un(0, 1, un_bf0[:])
-        un_rest = tile("un_rest", [P, 3 * P * PACK], BF16, "page1")
+        un_rest = tile("un_rest", [P, 3 * P * PACK], BF16)
         nc.scalar.copy(out=un_rest[:].rearrange("p (t m i) -> p m i t", t=3, i=PACK), in_=un_view[:, :, :, 1:4])
         state_pass(0, 0, stop=True)
         activate(0, 0)
@@ -227,8 +228,6 @@ def tile_list_tgn_rnnP_kernel(
         nc.vector.tensor_copy(picked_scale[1][:], table_scale[:].indirect(entries(1)))
         quantize_un(1, 2, un_rest[:, : P * PACK])
         quantize_un(2, 4, un_rest[:, P * PACK :])
-        page[1] = tile("page1", [P, T], F32)
-        nc.gpsimd.memset(page[1][:], 0.0)
         gather_add(0, 0)
         scatter(0, 0)
         for t in range(1, PACK):
@@ -256,8 +255,6 @@ def tile_list_tgn_rnnP_kernel(
             message_pass(t, 1, 0)
             state_pass(t, 1, stop=True)
             activate(t, 1)
-        page[2] = tile("page2", [P, T], F32, "x_codes11")
-        nc.gpsimd.memset(page[2][:], 0.0)
         gather_add(3, 0)
         gather_add(0, 1)
         scatter(0, 1)

@@ -22,6 +22,7 @@ P = 128
 PACK = 4
 PASSES = K // (P * PACK)
 HALF = J // 2
+LEAD = HALF // 2
 PIECE = 512
 PIECES = T // PIECE
 
@@ -46,7 +47,7 @@ def tile_list_tgn_rnnP_kernel(
         table = tile("table", [P, T], I32)
         table_scale = tile("table_scale", [P, T], U8)
         picked = tile("picked", [P, J], I32)
-        picked_scale = {0: tile("picked_scale0", [P, HALF], U8)}
+        picked_scale = tile("picked_scale", [P, J], U8)
         un_raw = tile("un_raw", [P, PACK, N], F32)
         un_codes = tile("un_codes", [P, N], U32)
         un_scale = tile("un_scale", [P, N], U8)
@@ -59,7 +60,7 @@ def tile_list_tgn_rnnP_kernel(
         x_codes = {ca: tile("x_codes%d%d" % ca, [P, HALF], U32) for ca in halves}
         x_scale = {ca: tile("x_scale%d%d" % ca, [P, HALF], U8) for ca in halves}
         state = [tile("state%d" % t, [P, T], F32) for t in range(PACK)]
-        act = {(t, c): tile("act%d%d" % (t, c), [P, HALF], F32) for t in range(PACK) for c in range(2)}
+        act = {(t, c): tile("act%d%d" % (t, c), [P, HALF], F32) for t in range(PACK) for c in range(2) if c == 1 or t == 1}
         updated = {(t, c): tile("updated%d%d" % (t, c), [P, HALF], F32)[:] for t in (0, 1) for c in range(2)}
         updated_whole = {t: tile("updated%d" % t, [P, J], F32) for t in (2, 3)}
         for t in (2, 3):
@@ -93,8 +94,9 @@ def tile_list_tgn_rnnP_kernel(
         nc.gpsimd.memset(table_scale[:].bitcast(I32), 0)
         nc.gpsimd.memset(wn_scale_raw[:].bitcast(I32), 0)
         make_identity(nc, identity[:])
-        for t in range(3):
-            nc.vector.memset(page[t][:].bitcast(I32), 0)
+        nc.vector.memset(page[0][:].bitcast(I32), 0)
+        for t in (1, 2):
+            nc.gpsimd.memset(page[t][:].bitcast(I32), 0)
 
         nc.sync.dma_start(offsets[:], offs)
         nc.sync.dma_start(out=weight_row[:], in_=wgo[0].rearrange("(r m) -> r m", m=J // P))
@@ -132,9 +134,11 @@ def tile_list_tgn_rnnP_kernel(
                 out=weight[:].rearrange("p (r m) -> p r m", m=J // P)[:, :, 4 * h : 4 * h + 4],
                 in_=spread[h][:].rearrange("p m r -> p r m"),
             )
+        lead = [ps.tile([P, LEAD], F32, name="lead%d" % g, tag=("acc00", "acc31")[g]) for g in range(2)]
         for t in range(PACK):
             for c in range(2):
-                acc[t, c] = ps.tile([P, HALF], F32, name="acc%d%d" % (t, c))
+                if (t, c) != (0, 0):
+                    acc[t, c] = ps.tile([P, HALF], F32, name="acc%d%d" % (t, c))
 
         nc.vector.tensor_copy(
             out=wn_dealt[:].bitcast(U16).rearrange("p (a t m) -> p a t m", a=PASSES, t=PACK),
@@ -145,7 +149,7 @@ def tile_list_tgn_rnnP_kernel(
             in_=wn_scale_raw[:].rearrange("p (a m t) -> p a t m", a=PASSES, t=PACK),
         )
         nc.vector.tensor_copy(picked[:].bitcast(U32), table[:].bitcast(U32).indirect(offsets[:]))
-        nc.vector.tensor_copy(picked_scale[0][:], table_scale[:].indirect(entries(0)))
+        nc.vector.tensor_copy(picked_scale[:], table_scale[:].indirect(offsets[:]))
 
         def round_x(c, a, engine_copy=nc.scalar.copy, first=0, last=HALF):
             engine_copy(
@@ -174,7 +178,7 @@ def tile_list_tgn_rnnP_kernel(
                 lhsT=un_codes[:, t * P : (t + 1) * P].bitcast(FP8X4),
                 lhsT_scale=un_scale[:, t * P : (t + 1) * P],
                 rhs=picked[:, cols(c)].bitcast(FP8X4),
-                rhs_scale=picked_scale[c][4:P, :],
+                rhs_scale=picked_scale[4:P, cols(c)],
                 start=start,
                 stop=stop,
             )
@@ -209,26 +213,58 @@ def tile_list_tgn_rnnP_kernel(
             )
 
         un_view = un_raw[:].rearrange("p i (m t) -> p m i t", t=PACK)
+
+        def lead_message_passes(a):
+            for g in range(2):
+                for n in range(LEAD // P):
+                    j0 = g * LEAD + n * P
+                    nc.tensor.matmul_mx(
+                        out=lead[g][:, n * P : (n + 1) * P],
+                        lhsT=wn_dealt[:].bitcast(U8)[:, 2 * a * N : 2 * (a * N + P)].bitcast(FP4X4),
+                        lhsT_scale=wn_scale[:, a * N : a * N + P],
+                        rhs=x_codes[0, a][:, j0 : j0 + P].bitcast(FP8X4),
+                        rhs_scale=x_scale[0, a][:, j0 : j0 + P],
+                        start=a == 0 and n == 0,
+                        stop=False,
+                    )
+
         round_x(0, 0)
         quantize_x(0, 0)
-        message_pass(0, 0, 0, start=True)
+        lead_message_passes(0)
         round_x(0, 1, nc.scalar.copy, 0, HALF // 2)
         round_x(0, 1, nc.vector.tensor_copy, HALF // 2, HALF)
         quantize_x(0, 1)
-        message_pass(0, 0, 1)
+        lead_message_passes(1)
 
-        un_bf0 = tile("un_bf0", [P, P * PACK], BF16)
-        nc.vector.tensor_copy(out=un_bf0[:].rearrange("p (m i) -> p m i", i=PACK), in_=un_view[:, :, :, 0])
-        quantize_un(0, 1, un_bf0[:])
-        un_rest = tile("un_rest", [P, 3 * P * PACK], BF16)
-        nc.scalar.copy(out=un_rest[:].rearrange("p (t m i) -> p m i t", t=3, i=PACK), in_=un_view[:, :, :, 1:4])
-        state_pass(0, 0, stop=True)
-        activate(0, 0)
-        picked_scale[1] = tile("picked_scale1", [P, HALF], U8, "un_bf0")
-        nc.vector.tensor_copy(picked_scale[1][:], table_scale[:].indirect(entries(1)))
-        quantize_un(1, 2, un_rest[:, : P * PACK])
-        quantize_un(2, 4, un_rest[:, P * PACK :])
-        gather_add(0, 0)
+        un_bf0 = tile("un_bf0", [P, P, PACK], BF16)
+        nc.vector.tensor_copy(out=un_bf0[:, : P // 2, :], in_=un_view[:, : P // 2, :, 0])
+        nc.scalar.copy(out=un_bf0[:, P // 2 :, :], in_=un_view[:, P // 2 :, :, 0])
+        quantize_un(0, 1, un_bf0[:].rearrange("p m i -> p (m i)"))
+        un_bf3 = tile("un_bf3", [P, P * PACK], BF16)
+        nc.scalar.copy(out=un_bf3[:].rearrange("p (m i) -> p m i", i=PACK), in_=un_view[:, :, :, 3])
+        lead_act = [tile("lead_act%d" % g, [P, LEAD], F32) for g in range(2)]
+        for g in range(2):
+            nc.tensor.matmul_mx(
+                out=lead[g][:],
+                lhsT=un_codes[:, :P].bitcast(FP8X4),
+                lhsT_scale=un_scale[:, :P],
+                rhs=picked[:, g * LEAD : (g + 1) * LEAD].bitcast(FP8X4),
+                rhs_scale=picked_scale[4:P, g * LEAD : (g + 1) * LEAD],
+                start=False,
+                stop=True,
+            )
+            nc.scalar.activation(out=lead_act[g][:], in_=lead[g][:], func=TANH, bias=bias[:, 0:1])
+        quantize_un(3, 4, un_bf3[:])
+        un_bf12 = tile("un_bf12", [P, 2 * P * PACK], BF16, "un_bf0")
+        nc.vector.tensor_copy(out=un_bf12[:].rearrange("p (t m i) -> p m i t", t=2, i=PACK), in_=un_view[:, :, :, 1:3])
+        quantize_un(1, 3, un_bf12[:])
+        for g in range(2):
+            nc.vector.tensor_tensor(
+                updated[0, 0][:, g * LEAD : (g + 1) * LEAD],
+                state[0][:].indirect(offsets[:, g * LEAD // 16 : (g + 1) * LEAD // 16]),
+                lead_act[g][:],
+                ADD,
+            )
         scatter(0, 0)
         for t in range(1, PACK):
             state_pass(t, 0, start=True)
@@ -238,14 +274,16 @@ def tile_list_tgn_rnnP_kernel(
         activate(1, 0)
         gather_add(1, 0)
         scatter(1, 0)
-        x_bf[1, 0] = tile("x_bf10", [P, HALF * PACK], BF16, "act00")
+        x_bf[1, 0] = tile("x_bf10", [P, HALF * PACK], BF16, "lead_act1")
         round_x(1, 0)
-        x_bf[1, 1] = tile("x_bf11", [P, HALF * PACK], BF16, "x_raw10")
+        x_bf[1, 1] = tile("x_bf11", [P, HALF * PACK], BF16, "act10")
         round_x(1, 1)
         quantize_x(1, 0)
         message_pass(0, 1, 0)
         quantize_x(1, 1)
+        act[2, 0] = tile("act20", [P, HALF], F32, "x_raw11")
         activate(2, 0)
+        act[3, 0] = tile("act30", [P, HALF], F32, "act10")
         activate(3, 0)
         gather_add(2, 0)
         message_pass(0, 1, 1, stop=True)

@@ -21,10 +21,19 @@ TANH = mybir.ActivationFunctionType.Tanh
 P = 128
 PACK = 4
 PASSES = K // (P * PACK)
+GROUP = 16
+QUADRANT = 32
+RUN = 4
+SCALE_ROWS = 16
+SCALE_ROW0 = 4
 HALF = J // 2
 LEAD = HALF // 2
+SPREAD = J // P
+BANK_BLOCKS = 4
 PIECE = 512
 PIECES = T // PIECE
+VECTOR_PIECES = (2, 3)
+SCALAR_PIECES = (0, 1)
 
 
 def tile_list_tgn_rnnP_kernel(
@@ -35,11 +44,11 @@ def tile_list_tgn_rnnP_kernel(
         sb = ctx.enter_context(tc.tile_pool(name="sb", bufs=1))
         ps = ctx.enter_context(tc.psum_pool(name="ps", bufs=1))
 
-        def tile(name, shape, dtype, tag=None):
-            return sb.tile(shape, dtype, name=name, tag=tag or name, align_bytes=64)
+        def tile(name, shape, dtype, after=None):
+            return sb.tile(shape, dtype, name=name, tag=after or name, align_bytes=64)
 
-        halves = [(c, a) for c in range(2) for a in range(PASSES)]
-        offsets = tile("offsets", [P, J // 16], U16)
+        x_parts = [(c, a) for c in range(2) for a in range(PASSES)]
+        offsets = tile("offsets", [P, J // GROUP], U16)
         wn_raw = tile("wn_raw", [P, PASSES * N // 2], I32)
         wn_dealt = tile("wn_dealt", [P, PASSES * N // 2], I32)
         wn_scale_raw = tile("wn_scale_raw", [P, PASSES * N], U8)
@@ -49,29 +58,29 @@ def tile_list_tgn_rnnP_kernel(
         picked = tile("picked", [P, J], I32)
         picked_scale = tile("picked_scale", [P, J], U8)
         un_raw = tile("un_raw", [P, PACK, N], F32)
-        un_codes = tile("un_codes", [P, N], U32)
+        un_codes = {0: tile("un_codes0", [P, P], U32)[:]}
         un_scale = tile("un_scale", [P, N], U8)
         bias = tile("bias", [P, PACK], F32)
         weight = tile("weight", [P, J], F32)
-        weight_row = tile("weight_row", [P, J // P], F32)
+        weight_row = tile("weight_row", [P, SPREAD], F32)
         identity = tile("identity", [P, P], F32)
-        x_raw = {ca: tile("x_raw%d%d" % ca, [P, PACK, HALF], F32) for ca in halves}
+        x_raw = {ca: tile("x_raw%d%d" % ca, [P, PACK, HALF], F32) for ca in x_parts}
         x_bf = {(0, a): tile("x_bf0%d" % a, [P, HALF * PACK], BF16) for a in range(PASSES)}
-        x_codes = {ca: tile("x_codes%d%d" % ca, [P, HALF], U32) for ca in halves}
-        x_scale = {ca: tile("x_scale%d%d" % ca, [P, HALF], U8) for ca in halves}
+        x_codes = {ca: tile("x_codes%d%d" % ca, [P, HALF], U32) for ca in x_parts}
+        x_scale = {ca: tile("x_scale%d%d" % ca, [P, HALF], U8) for ca in x_parts}
         state = [tile("state%d" % t, [P, T], F32) for t in range(PACK)]
-        act = {(t, c): tile("act%d%d" % (t, c), [P, HALF], F32) for t in range(PACK) for c in range(2) if c == 1 or t == 1}
-        updated = {(t, c): tile("updated%d%d" % (t, c), [P, HALF], F32)[:] for t in (0, 1) for c in range(2)}
+        act = {(t, c): tile("act%d%d" % (t, c), [P, HALF], F32) for t, c in ((0, 1), (1, 0), (1, 1), (2, 1), (3, 1))}
+        updated = {(t, c): tile("updated%d%d" % (t, c), [P, HALF], F32)[:] for t, c in ((0, 0), (0, 1), (1, 1))}
         updated_whole = {t: tile("updated%d" % t, [P, J], F32) for t in (2, 3)}
         for t in (2, 3):
             for c in range(2):
                 updated[t, c] = updated_whole[t][:, c * HALF : (c + 1) * HALF]
-        page = {t: tile("page%d" % t, [P, T], F32) for t in range(3)}
+        page = {0: tile("page0", [P, T], F32)}
         page[3] = page[0]
         y_bf = [tile("y_bf%d" % q, [P, PIECE, PACK], BF16) for q in range(PIECES)]
         y_codes = [tile("y_codes%d" % q, [P, PIECE], I32) for q in range(PIECES)]
         y_scale = tile("y_scale", [P, T], U8)
-        spread = [ps.tile([P, 4, P], F32, name="spread%d" % h, tag="acc%d1" % (2 + h)) for h in range(2)]
+        spread = [ps.tile([P, BANK_BLOCKS, P], F32, name="spread%d" % h, tag="acc%d1" % (2 + h)) for h in range(2)]
         acc = {}
 
         x_rows = x.rearrange("(a p i) j -> a p i j", a=PASSES, i=PACK)
@@ -83,7 +92,7 @@ def tile_list_tgn_rnnP_kernel(
             return slice(c * HALF, (c + 1) * HALF)
 
         def entries(c):
-            return offsets[:, c * HALF // 16 : (c + 1) * HALF // 16]
+            return offsets[:, c * HALF // GROUP : (c + 1) * HALF // GROUP]
 
         def load_state(t):
             nc.sync.dma_start(out=state[t][:], in_=h_rows[t])
@@ -91,31 +100,29 @@ def tile_list_tgn_rnnP_kernel(
         def load_x(c, a):
             nc.sync.dma_start(out=x_raw[c, a][:], in_=x_rows[a][:, :, cols(c)])
 
-        nc.gpsimd.memset(table_scale[:].bitcast(I32), 0)
         nc.gpsimd.memset(wn_scale_raw[:].bitcast(I32), 0)
+        nc.gpsimd.memset(table_scale[:].bitcast(I32), 0)
         make_identity(nc, identity[:])
         nc.vector.memset(page[0][:].bitcast(I32), 0)
-        for t in (1, 2):
-            nc.gpsimd.memset(page[t][:].bitcast(I32), 0)
 
         nc.sync.dma_start(offsets[:], offs)
-        nc.sync.dma_start(out=weight_row[:], in_=wgo[0].rearrange("(r m) -> r m", m=J // P))
+        nc.sync.dma_start(out=weight_row[:], in_=wgo[0].rearrange("(r m) -> r m", m=SPREAD))
         nc.sync.dma_start(
             out=wn_raw[:].rearrange("p (a w) -> p a w", a=PASSES),
             in_=wn_words.bitcast(I32).rearrange("a p w -> p a w"),
         )
-        nc.sync.dma_start(out=table[:], in_=tab_words[0].rearrange("p t i -> p (t i)").bitcast(I32))
-        for q in range(4):
+        for r in range(RUN):
             nc.sync.dma_start(
-                out=table_scale[4 + q : P : 32, :].bitcast(I32),
-                in_=tab_scales.bitcast(I32)[0, q:16:4, :],
+                out=wn_scale_raw[r:P:QUADRANT, :].bitcast(I32).rearrange("r (a w) -> r a w", a=PASSES),
+                in_=wn_scales.bitcast(I32)[:, r:SCALE_ROWS:RUN, :].rearrange("a r w -> r a w"),
+            )
+        nc.sync.dma_start(out=table[:], in_=tab_words[0].rearrange("p t i -> p (t i)").bitcast(I32))
+        for r in range(RUN):
+            nc.sync.dma_start(
+                out=table_scale[SCALE_ROW0 + r : P : QUADRANT, :].bitcast(I32),
+                in_=tab_scales.bitcast(I32)[0, r:SCALE_ROWS:RUN, :],
             )
         load_x(0, 0)
-        for q in range(4):
-            nc.sync.dma_start(
-                out=wn_scale_raw[q:P:32, :].bitcast(I32).rearrange("r (a w) -> r a w", a=PASSES),
-                in_=wn_scales.bitcast(I32)[:, q:16:4, :].rearrange("a r w -> r a w"),
-            )
         load_x(0, 1)
         nc.sync.dma_start(out=bias[:], in_=bn.rearrange("(p t) -> p t", t=PACK))
         nc.sync.dma_start(out=un_raw[:], in_=un.rearrange("(p i) n -> p i n", i=PACK))
@@ -126,12 +133,12 @@ def tile_list_tgn_rnnP_kernel(
         load_state(2)
         load_state(3)
 
-        for h in range(2):
-            for m in range(4):
-                column = weight_row[:, 4 * h + m : 4 * h + m + 1]
+        for h in range(SPREAD // BANK_BLOCKS):
+            for m in range(BANK_BLOCKS):
+                column = weight_row[:, BANK_BLOCKS * h + m : BANK_BLOCKS * h + m + 1]
                 nc.tensor.transpose(spread[h][:, m, :], column.to_broadcast([P, P]), identity[:])
             nc.scalar.copy(
-                out=weight[:].rearrange("p (r m) -> p r m", m=J // P)[:, :, 4 * h : 4 * h + 4],
+                out=weight[:].rearrange("p (r m) -> p r m", m=SPREAD)[:, :, BANK_BLOCKS * h : BANK_BLOCKS * (h + 1)],
                 in_=spread[h][:].rearrange("p m r -> p r m"),
             )
         lead = [ps.tile([P, LEAD], F32, name="lead%d" % g, tag=("acc00", "acc31")[g]) for g in range(2)]
@@ -150,6 +157,9 @@ def tile_list_tgn_rnnP_kernel(
         )
         nc.vector.tensor_copy(picked[:].bitcast(U32), table[:].bitcast(U32).indirect(offsets[:]))
         nc.vector.tensor_copy(picked_scale[:], table_scale[:].indirect(offsets[:]))
+        for t, freed in ((1, "wn_scale_raw"), (2, "table")):
+            page[t] = tile("page%d" % t, [P, T], F32, freed)
+            nc.gpsimd.memset(page[t][:].bitcast(I32), 0)
 
         def round_x(c, a, engine_copy=nc.scalar.copy, first=0, last=HALF):
             engine_copy(
@@ -175,10 +185,10 @@ def tile_list_tgn_rnnP_kernel(
         def state_pass(t, c, start=False, stop=False):
             nc.tensor.matmul_mx(
                 out=acc[t, c][:],
-                lhsT=un_codes[:, t * P : (t + 1) * P].bitcast(FP8X4),
+                lhsT=un_codes[t].bitcast(FP8X4),
                 lhsT_scale=un_scale[:, t * P : (t + 1) * P],
                 rhs=picked[:, cols(c)].bitcast(FP8X4),
-                rhs_scale=picked_scale[4:P, cols(c)],
+                rhs_scale=picked_scale[SCALE_ROW0:P, cols(c)],
                 start=start,
                 stop=stop,
             )
@@ -195,92 +205,99 @@ def tile_list_tgn_rnnP_kernel(
         def scatter_whole(t):
             nc.vector.tensor_tensor(page[t][:].indirect(offsets[:]), updated_whole[t][:], weight[:], MULT)
 
-        def weave(engine_copy, t, q):
+        def interleave(engine_copy, t, q):
             engine_copy(out=y_bf[q][:, :, t], in_=page[t][:, q * PIECE : (q + 1) * PIECE])
 
-        def finish_plane(t):
+        def finish_row_set(t):
             nc.sync.dma_start(out=y_rows[t], in_=page[t][:])
-            for q in (2, 3, 0, 1):
-                if t == 2 and q >= 2:
+            for q in VECTOR_PIECES + SCALAR_PIECES:
+                if t == 2 and q in VECTOR_PIECES:
                     piece = page[t][:, q * PIECE : (q + 1) * PIECE]
                     nc.scalar.copy(out=y_bf[q][:, :, 2:4], in_=piece.unsqueeze(2).to_broadcast([P, PIECE, 2]))
                 else:
-                    weave(nc.scalar.copy, t, q)
+                    interleave(nc.scalar.copy, t, q)
 
-        def quantize_un(first, last, source):
-            nc.vector.quantize_mx(
-                out=un_codes[:, first * P : last * P].bitcast(FP8X4), scales=un_scale[:, first * P : last * P], in_=source
-            )
+        def quantize_un(first, last, codes, source):
+            nc.vector.quantize_mx(out=codes.bitcast(FP8X4), scales=un_scale[:, first * P : last * P], in_=source)
 
         un_view = un_raw[:].rearrange("p i (m t) -> p m i t", t=PACK)
 
         def lead_message_passes(a):
             for g in range(2):
-                for n in range(LEAD // P):
-                    j0 = g * LEAD + n * P
+                for block in range(LEAD // P):
+                    j0 = g * LEAD + block * P
                     nc.tensor.matmul_mx(
-                        out=lead[g][:, n * P : (n + 1) * P],
+                        out=lead[g][:, block * P : (block + 1) * P],
                         lhsT=wn_dealt[:].bitcast(U8)[:, 2 * a * N : 2 * (a * N + P)].bitcast(FP4X4),
                         lhsT_scale=wn_scale[:, a * N : a * N + P],
                         rhs=x_codes[0, a][:, j0 : j0 + P].bitcast(FP8X4),
                         rhs_scale=x_scale[0, a][:, j0 : j0 + P],
-                        start=a == 0 and n == 0,
+                        start=a == 0 and block == 0,
                         stop=False,
                     )
 
         round_x(0, 0)
         quantize_x(0, 0)
         lead_message_passes(0)
+        message_pass(1, 0, 0, start=True)
         round_x(0, 1, nc.scalar.copy, 0, HALF // 2)
         round_x(0, 1, nc.vector.tensor_copy, HALF // 2, HALF)
         quantize_x(0, 1)
         lead_message_passes(1)
+        message_pass(1, 0, 1)
 
         un_bf0 = tile("un_bf0", [P, P, PACK], BF16)
         nc.vector.tensor_copy(out=un_bf0[:, : P // 2, :], in_=un_view[:, : P // 2, :, 0])
         nc.scalar.copy(out=un_bf0[:, P // 2 :, :], in_=un_view[:, P // 2 :, :, 0])
-        quantize_un(0, 1, un_bf0[:].rearrange("p m i -> p (m i)"))
+        quantize_un(0, 1, un_codes[0], un_bf0[:].rearrange("p m i -> p (m i)"))
         un_bf3 = tile("un_bf3", [P, P * PACK], BF16)
         nc.scalar.copy(out=un_bf3[:].rearrange("p (m i) -> p m i", i=PACK), in_=un_view[:, :, :, 3])
         lead_act = [tile("lead_act%d" % g, [P, LEAD], F32) for g in range(2)]
         for g in range(2):
             nc.tensor.matmul_mx(
                 out=lead[g][:],
-                lhsT=un_codes[:, :P].bitcast(FP8X4),
+                lhsT=un_codes[0].bitcast(FP8X4),
                 lhsT_scale=un_scale[:, :P],
                 rhs=picked[:, g * LEAD : (g + 1) * LEAD].bitcast(FP8X4),
-                rhs_scale=picked_scale[4:P, g * LEAD : (g + 1) * LEAD],
+                rhs_scale=picked_scale[SCALE_ROW0:P, g * LEAD : (g + 1) * LEAD],
                 start=False,
                 stop=True,
             )
             nc.scalar.activation(out=lead_act[g][:], in_=lead[g][:], func=TANH, bias=bias[:, 0:1])
-        quantize_un(3, 4, un_bf3[:])
         un_bf12 = tile("un_bf12", [P, 2 * P * PACK], BF16, "un_bf0")
         nc.vector.tensor_copy(out=un_bf12[:].rearrange("p (t m i) -> p m i t", t=2, i=PACK), in_=un_view[:, :, :, 1:3])
-        quantize_un(1, 3, un_bf12[:])
+        un_codes12 = tile("un_codes12", [P, 2 * P], U32)
+        un_codes[1], un_codes[2] = un_codes12[:, :P], un_codes12[:, P:]
+        quantize_un(1, 3, un_codes12[:], un_bf12[:])
         for g in range(2):
             nc.vector.tensor_tensor(
                 updated[0, 0][:, g * LEAD : (g + 1) * LEAD],
-                state[0][:].indirect(offsets[:, g * LEAD // 16 : (g + 1) * LEAD // 16]),
+                state[0][:].indirect(offsets[:, g * LEAD // GROUP : (g + 1) * LEAD // GROUP]),
                 lead_act[g][:],
                 ADD,
             )
+        un_codes[3] = tile("un_codes3", [P, P], U32, "lead_act0")[:]
+        quantize_un(3, 4, un_codes[3], un_bf3[:])
         scatter(0, 0)
-        for t in range(1, PACK):
+        state_pass(1, 0, stop=True)
+        for t in range(2, PACK):
             state_pass(t, 0, start=True)
             message_pass(t, 0, 0)
             message_pass(t, 0, 1, stop=True)
         state_pass(0, 1, start=True)
         activate(1, 0)
-        gather_add(1, 0)
-        scatter(1, 0)
+
         x_bf[1, 0] = tile("x_bf10", [P, HALF * PACK], BF16, "lead_act1")
         round_x(1, 0)
+        updated[1, 0] = tile("updated10", [P, HALF], F32, "x_raw10")[:]
+        gather_add(1, 0)
+        quantize_x(1, 0)
+        scatter(1, 0)
         x_bf[1, 1] = tile("x_bf11", [P, HALF * PACK], BF16, "act10")
         round_x(1, 1)
-        quantize_x(1, 0)
         message_pass(0, 1, 0)
         quantize_x(1, 1)
+
         act[2, 0] = tile("act20", [P, HALF], F32, "x_raw11")
         activate(2, 0)
         act[3, 0] = tile("act30", [P, HALF], F32, "act10")
@@ -296,28 +313,29 @@ def tile_list_tgn_rnnP_kernel(
         gather_add(3, 0)
         gather_add(0, 1)
         scatter(0, 1)
-        finish_plane(0)
+        finish_row_set(0)
         gather_add(1, 1)
         gather_add(2, 1)
         scatter(1, 1)
-        finish_plane(1)
+        finish_row_set(1)
         gather_add(3, 1)
         scatter_whole(2)
-        finish_plane(2)
+        finish_row_set(2)
         scatter_whole(3)
+
         nc.sync.dma_start(out=y_rows[3], in_=page[3][:])
-        for q in (0, 1):
-            weave(nc.scalar.copy, 3, q)
-        for q in (2, 3):
-            weave(nc.vector.tensor_copy, 3, q)
-        for q in (2, 3, 0, 1):
+        for q in SCALAR_PIECES:
+            interleave(nc.scalar.copy, 3, q)
+        for q in VECTOR_PIECES:
+            interleave(nc.vector.tensor_copy, 3, q)
+        for q in VECTOR_PIECES + SCALAR_PIECES:
             nc.vector.quantize_mx(
                 out=y_codes[q][:].bitcast(FP8X4),
                 scales=y_scale[:, q * PIECE : (q + 1) * PIECE],
                 in_=y_bf[q][:].rearrange("p c i -> p (c i)"),
             )
             nc.sync.dma_start(out=y_words[:, q * PIECE : (q + 1) * PIECE], in_=y_codes[q][:])
-        for q in range(4):
+        for r in range(RUN):
             nc.scalar.dma_start(
-                out=out_2.bitcast(I32)[0, q:16:4, :], in_=y_scale[q:P:32, :].bitcast(I32)
+                out=out_2.bitcast(I32)[0, r:SCALE_ROWS:RUN, :], in_=y_scale[r:P:QUADRANT, :].bitcast(I32)
             )

@@ -27,13 +27,26 @@ RUN = 4
 SCALE_ROWS = 16
 SCALE_ROW0 = 4
 HALF = J // 2
-LEAD = HALF // 2
+FIRST = 384
+REST = J - FIRST
+SECOND = 768
+CHUNKS = {"a": (0, FIRST), "b": (FIRST, SECOND), "c": (SECOND, J)}
+UN_SCALAR = 80
 SPREAD = J // P
 BANK_BLOCKS = 4
 PIECE = 512
 PIECES = T // PIECE
 VECTOR_PIECES = (2, 3)
 SCALAR_PIECES = (0, 1)
+
+
+def runs(first, last, widths):
+    out = []
+    for width in widths:
+        while last - first >= width:
+            out.append((first, first + width))
+            first = first + width
+    return out
 
 
 def tile_list_tgn_rnnP_kernel(
@@ -47,7 +60,13 @@ def tile_list_tgn_rnnP_kernel(
         def tile(name, shape, dtype, after=None):
             return sb.tile(shape, dtype, name=name, tag=after or name, align_bytes=64)
 
-        x_parts = [(c, a) for c in range(2) for a in range(PASSES)]
+        def bank(name, number, width):
+            return ps.tile([P, width], F32, name=name, tag="bank%d" % number)
+
+        def width(c):
+            return CHUNKS[c][1] - CHUNKS[c][0]
+
+        x_parts = [(c, a) for c in CHUNKS for a in range(PASSES)]
         offsets = tile("offsets", [P, J // GROUP], U16)
         wn_raw = tile("wn_raw", [P, PASSES * N // 2], I32)
         wn_dealt = tile("wn_dealt", [P, PASSES * N // 2], I32)
@@ -58,79 +77,70 @@ def tile_list_tgn_rnnP_kernel(
         picked = tile("picked", [P, J], I32)
         picked_scale = tile("picked_scale", [P, J], U8)
         un_raw = tile("un_raw", [P, PACK, N], F32)
-        un_codes = {0: tile("un_codes0", [P, P], U32)[:]}
+        un_codes = tile("un_codes", [P, N], U32)
         un_scale = tile("un_scale", [P, N], U8)
         bias = tile("bias", [P, PACK], F32)
         weight = tile("weight", [P, J], F32)
         weight_row = tile("weight_row", [P, SPREAD], F32)
         identity = tile("identity", [P, P], F32)
-        x_raw = {ca: tile("x_raw%d%d" % ca, [P, PACK, HALF], F32) for ca in x_parts}
-        x_bf = {(0, a): tile("x_bf0%d" % a, [P, HALF * PACK], BF16) for a in range(PASSES)}
-        x_codes = {ca: tile("x_codes%d%d" % ca, [P, HALF], U32) for ca in x_parts}
-        x_scale = {ca: tile("x_scale%d%d" % ca, [P, HALF], U8) for ca in x_parts}
+        x_raw = {(c, a): tile("x_raw_%s%d" % (c, a), [P, PACK, width(c)], F32) for c, a in x_parts}
+        x_bf = {}
+        x_codes = [tile("x_codes%d" % a, [P, J], U32) for a in range(PASSES)]
+        x_scale = [tile("x_scale%d" % a, [P, J], U8) for a in range(PASSES)]
         state = [tile("state%d" % t, [P, T], F32) for t in range(PACK)]
-        act = {(t, c): tile("act%d%d" % (t, c), [P, HALF], F32) for t, c in ((0, 1), (1, 0), (1, 1), (2, 1), (3, 1))}
-        updated = {(t, c): tile("updated%d%d" % (t, c), [P, HALF], F32)[:] for t, c in ((0, 0), (0, 1), (1, 1))}
-        updated_whole = {t: tile("updated%d" % t, [P, J], F32) for t in (2, 3)}
-        for t in (2, 3):
-            for c in range(2):
-                updated[t, c] = updated_whole[t][:, c * HALF : (c + 1) * HALF]
         page = {0: tile("page0", [P, T], F32)}
         page[3] = page[0]
         y_bf = [tile("y_bf%d" % q, [P, PIECE, PACK], BF16) for q in range(PIECES)]
         y_codes = [tile("y_codes%d" % q, [P, PIECE], I32) for q in range(PIECES)]
+        pair01 = tile("pair01", [P, T], U32)
         y_scale = tile("y_scale", [P, T], U8)
-        spread = [ps.tile([P, BANK_BLOCKS, P], F32, name="spread%d" % h, tag="acc%d1" % (2 + h)) for h in range(2)]
-        acc = {}
+        spread = [ps.tile([P, BANK_BLOCKS, P], F32, name="spread%d" % h, tag="bank%d" % (6 + h)) for h in range(2)]
 
         x_rows = x.rearrange("(a p i) j -> a p i j", a=PASSES, i=PACK)
         h_rows = hT.rearrange("(p t) c -> t p c", t=PACK)
         y_rows = out_0.rearrange("(p t) c -> t p c", t=PACK)
         y_words = out_1[0].rearrange("p t i -> p (t i)").bitcast(I32)
 
-        def cols(c):
-            return slice(c * HALF, (c + 1) * HALF)
-
-        def entries(c):
-            return offsets[:, c * HALF // GROUP : (c + 1) * HALF // GROUP]
+        def entries(first, last):
+            return offsets[:, first // GROUP : last // GROUP]
 
         def load_state(t):
             nc.sync.dma_start(out=state[t][:], in_=h_rows[t])
 
-        def load_x(c, a):
-            nc.sync.dma_start(out=x_raw[c, a][:], in_=x_rows[a][:, :, cols(c)])
+        def load_x(c):
+            for a in range(PASSES):
+                nc.sync.dma_start(out=x_raw[c, a][:], in_=x_rows[a][:, :, CHUNKS[c][0] : CHUNKS[c][1]])
 
-        nc.gpsimd.memset(wn_scale_raw[:].bitcast(I32), 0)
         nc.gpsimd.memset(table_scale[:].bitcast(I32), 0)
+        nc.gpsimd.memset(wn_scale_raw[:].bitcast(I32), 0)
         make_identity(nc, identity[:])
         nc.vector.memset(page[0][:].bitcast(I32), 0)
 
         nc.sync.dma_start(offsets[:], offs)
-        nc.sync.dma_start(out=weight_row[:], in_=wgo[0].rearrange("(r m) -> r m", m=SPREAD))
         nc.sync.dma_start(
             out=wn_raw[:].rearrange("p (a w) -> p a w", a=PASSES),
             in_=wn_words.bitcast(I32).rearrange("a p w -> p a w"),
         )
         for r in range(RUN):
             nc.sync.dma_start(
-                out=wn_scale_raw[r:P:QUADRANT, :].bitcast(I32).rearrange("r (a w) -> r a w", a=PASSES),
-                in_=wn_scales.bitcast(I32)[:, r:SCALE_ROWS:RUN, :].rearrange("a r w -> r a w"),
-            )
-        nc.sync.dma_start(out=table[:], in_=tab_words[0].rearrange("p t i -> p (t i)").bitcast(I32))
-        for r in range(RUN):
-            nc.sync.dma_start(
                 out=table_scale[SCALE_ROW0 + r : P : QUADRANT, :].bitcast(I32),
                 in_=tab_scales.bitcast(I32)[0, r:SCALE_ROWS:RUN, :],
             )
-        load_x(0, 0)
-        load_x(0, 1)
-        nc.sync.dma_start(out=bias[:], in_=bn.rearrange("(p t) -> p t", t=PACK))
+        nc.sync.dma_start(out=table[:], in_=tab_words[0].rearrange("p t i -> p (t i)").bitcast(I32))
+        nc.sync.dma_start(out=weight_row[:], in_=wgo[0].rearrange("(r m) -> r m", m=SPREAD))
+        for r in range(RUN):
+            nc.sync.dma_start(
+                out=wn_scale_raw[r:P:QUADRANT, :].bitcast(I32).rearrange("r (a w) -> r a w", a=PASSES),
+                in_=wn_scales.bitcast(I32)[:, r:SCALE_ROWS:RUN, :].rearrange("a r w -> r a w"),
+            )
         nc.sync.dma_start(out=un_raw[:], in_=un.rearrange("(p i) n -> p i n", i=PACK))
+        load_x("a")
+        nc.sync.dma_start(out=bias[:], in_=bn.rearrange("(p t) -> p t", t=PACK))
         load_state(0)
-        load_x(1, 0)
         load_state(1)
-        load_x(1, 1)
+        load_x("b")
         load_state(2)
+        load_x("c")
         load_state(3)
 
         for h in range(SPREAD // BANK_BLOCKS):
@@ -141,187 +151,198 @@ def tile_list_tgn_rnnP_kernel(
                 out=weight[:].rearrange("p (r m) -> p r m", m=SPREAD)[:, :, BANK_BLOCKS * h : BANK_BLOCKS * (h + 1)],
                 in_=spread[h][:].rearrange("p m r -> p r m"),
             )
-        lead = [ps.tile([P, LEAD], F32, name="lead%d" % g, tag=("acc00", "acc31")[g]) for g in range(2)]
-        for t in range(PACK):
-            for c in range(2):
-                if (t, c) != (0, 0):
-                    acc[t, c] = ps.tile([P, HALF], F32, name="acc%d%d" % (t, c))
+
+        def clear_page(t, after):
+            page[t] = tile("page%d" % t, [P, T], F32, after)
+            nc.gpsimd.memset(page[t][:].bitcast(I32), 0)
 
         nc.vector.tensor_copy(
             out=wn_dealt[:].bitcast(U16).rearrange("p (a t m) -> p a t m", a=PASSES, t=PACK),
             in_=wn_raw[:].bitcast(U16).rearrange("p (a m t) -> p a t m", a=PASSES, t=PACK),
         )
+        clear_page(1, "wn_raw")
+        nc.vector.tensor_copy(picked_scale[:], table_scale[:].indirect(offsets[:]))
+        clear_page(2, "table_scale")
+        nc.vector.tensor_copy(picked[:].bitcast(U32), table[:].bitcast(U32).indirect(offsets[:]))
         nc.vector.tensor_copy(
             out=wn_scale[:].rearrange("p (a t m) -> p a t m", a=PASSES, t=PACK),
             in_=wn_scale_raw[:].rearrange("p (a m t) -> p a t m", a=PASSES, t=PACK),
         )
-        nc.vector.tensor_copy(picked[:].bitcast(U32), table[:].bitcast(U32).indirect(offsets[:]))
-        nc.vector.tensor_copy(picked_scale[:], table_scale[:].indirect(offsets[:]))
-        for t, freed in ((1, "wn_scale_raw"), (2, "table")):
-            page[t] = tile("page%d" % t, [P, T], F32, freed)
-            nc.gpsimd.memset(page[t][:].bitcast(I32), 0)
 
-        def round_x(c, a, engine_copy=nc.scalar.copy, first=0, last=HALF):
+        def make_x_bf(c, after):
+            both = tile("x_bf_" + c, [P, PASSES * width(c) * PACK], BF16, after)
+            for a in range(PASSES):
+                x_bf[c, a] = both[:, a * width(c) * PACK : (a + 1) * width(c) * PACK]
+
+        def round_x(c, a, engine_copy=nc.scalar.copy, first=0, last=None):
+            last = last or width(c)
             engine_copy(
-                out=x_bf[c, a][:, first * PACK : last * PACK].rearrange("p (g e i) -> p g i e", e=4, i=PACK),
-                in_=x_raw[c, a][:, :, first:last].rearrange("p i (g e) -> p g i e", e=4),
+                out=x_bf[c, a][:, first * PACK : last * PACK].rearrange("p (g e i) -> p g i e", e=2, i=PACK),
+                in_=x_raw[c, a][:, :, first:last].rearrange("p i (g e) -> p g i e", e=2),
             )
 
-        def quantize_x(c, a):
-            nc.vector.quantize_mx(out=x_codes[c, a][:].bitcast(FP8X4), scales=x_scale[c, a][:], in_=x_bf[c, a][:])
+        def quantize_x(c, a, widths=(256, 128)):
+            base = CHUNKS[c][0]
+            for first, last in runs(0, width(c), widths):
+                nc.vector.quantize_mx(
+                    out=x_codes[a][:, base + first : base + last].bitcast(FP8X4),
+                    scales=x_scale[a][:, base + first : base + last],
+                    in_=x_bf[c, a][:, first * PACK : last * PACK],
+                )
 
-        def message_pass(t, c, a, start=False, stop=False):
-            first = (a * PACK + t) * P
-            nc.tensor.matmul_mx(
-                out=acc[t, c][:],
-                lhsT=wn_dealt[:].bitcast(U8)[:, 2 * first : 2 * (first + P)].bitcast(FP4X4),
-                lhsT_scale=wn_scale[:, first : first + P],
-                rhs=x_codes[c, a][:].bitcast(FP8X4),
-                rhs_scale=x_scale[c, a][:],
-                start=start,
-                stop=stop,
-            )
+        def message_pass(acc, t, first, last, a, start=False, stop=False, backwards=False):
+            column = (a * PACK + t) * P
+            parts = runs(first, last, (512, 128))
+            if backwards:
+                parts = parts[::-1]
+            for j0, j1 in parts:
+                nc.tensor.matmul_mx(
+                    out=acc[:, j0 - first : j1 - first],
+                    lhsT=wn_dealt[:].bitcast(U8)[:, 2 * column : 2 * (column + P)].bitcast(FP4X4),
+                    lhsT_scale=wn_scale[:, column : column + P],
+                    rhs=x_codes[a][:, j0:j1].bitcast(FP8X4),
+                    rhs_scale=x_scale[a][:, j0:j1],
+                    start=start and (j0, j1) == parts[0],
+                    stop=stop and (j0, j1) == parts[-1],
+                )
 
-        def state_pass(t, c, start=False, stop=False):
-            nc.tensor.matmul_mx(
-                out=acc[t, c][:],
-                lhsT=un_codes[t].bitcast(FP8X4),
-                lhsT_scale=un_scale[:, t * P : (t + 1) * P],
-                rhs=picked[:, cols(c)].bitcast(FP8X4),
-                rhs_scale=picked_scale[SCALE_ROW0:P, cols(c)],
-                start=start,
-                stop=stop,
-            )
+        def state_pass(acc, t, first, last, start=False, stop=False):
+            for j0, j1 in runs(first, last, (512, 256, 128)):
+                nc.tensor.matmul_mx(
+                    out=acc[:, j0 - first : j1 - first],
+                    lhsT=un_codes[:, t * P : (t + 1) * P].bitcast(FP8X4),
+                    lhsT_scale=un_scale[:, t * P : (t + 1) * P],
+                    rhs=picked[:, j0:j1].bitcast(FP8X4),
+                    rhs_scale=picked_scale[SCALE_ROW0:P, j0:j1],
+                    start=start and j0 == first,
+                    stop=stop and j1 == last,
+                )
 
-        def activate(t, c):
-            nc.scalar.activation(out=act[t, c][:], in_=acc[t, c][:], func=TANH, bias=bias[:, t : t + 1])
+        def activate(out, acc, t):
+            nc.scalar.activation(out=out, in_=acc[:], func=TANH, bias=bias[:, t : t + 1])
 
-        def gather_add(t, c):
-            nc.vector.tensor_tensor(updated[t, c], state[t][:].indirect(entries(c)), act[t, c][:], ADD)
+        def gather_add(out, t, first, last, act):
+            nc.vector.tensor_tensor(out, state[t][:].indirect(entries(first, last)), act, ADD)
 
-        def scatter(t, c):
-            nc.vector.tensor_tensor(page[t][:].indirect(entries(c)), updated[t, c], weight[:, cols(c)], MULT)
-
-        def scatter_whole(t):
-            nc.vector.tensor_tensor(page[t][:].indirect(offsets[:]), updated_whole[t][:], weight[:], MULT)
+        def scatter(t, first, last, values):
+            nc.vector.tensor_tensor(page[t][:].indirect(entries(first, last)), values, weight[:, first:last], MULT)
 
         def interleave(engine_copy, t, q):
             engine_copy(out=y_bf[q][:, :, t], in_=page[t][:, q * PIECE : (q + 1) * PIECE])
 
         def finish_row_set(t):
             nc.sync.dma_start(out=y_rows[t], in_=page[t][:])
+            if t < 2:
+                pairs = pair01[:].bitcast(BF16).rearrange("p (c u) -> p c u", u=2)
+                nc.scalar.copy(out=pairs[:, :, t], in_=page[t][:])
             for q in VECTOR_PIECES + SCALAR_PIECES:
-                if t == 2 and q in VECTOR_PIECES:
-                    piece = page[t][:, q * PIECE : (q + 1) * PIECE]
+                columns = slice(q * PIECE, (q + 1) * PIECE)
+                if t == 1:
+                    words = y_bf[q][:].rearrange("p c i -> p (c i)").bitcast(U32).rearrange("p (c u) -> p c u", u=2)
+                    nc.scalar.copy(out=words, in_=pair01[:, columns].unsqueeze(2).to_broadcast([P, PIECE, 2]))
+                elif t == 2 and q in VECTOR_PIECES:
+                    piece = page[t][:, columns]
                     nc.scalar.copy(out=y_bf[q][:, :, 2:4], in_=piece.unsqueeze(2).to_broadcast([P, PIECE, 2]))
-                else:
+                elif t == 2:
                     interleave(nc.scalar.copy, t, q)
-
-        def quantize_un(first, last, codes, source):
-            nc.vector.quantize_mx(out=codes.bitcast(FP8X4), scales=un_scale[:, first * P : last * P], in_=source)
 
         un_view = un_raw[:].rearrange("p i (m t) -> p m i t", t=PACK)
 
-        def lead_message_passes(a):
-            for g in range(2):
-                for block in range(LEAD // P):
-                    j0 = g * LEAD + block * P
-                    nc.tensor.matmul_mx(
-                        out=lead[g][:, block * P : (block + 1) * P],
-                        lhsT=wn_dealt[:].bitcast(U8)[:, 2 * a * N : 2 * (a * N + P)].bitcast(FP4X4),
-                        lhsT_scale=wn_scale[:, a * N : a * N + P],
-                        rhs=x_codes[0, a][:, j0 : j0 + P].bitcast(FP8X4),
-                        rhs_scale=x_scale[0, a][:, j0 : j0 + P],
-                        start=a == 0 and block == 0,
-                        stop=False,
-                    )
+        un_bf = tile("un_bf", [P, PACK * N], BF16)
+        un_dealt = un_bf[:].rearrange("p (t m i) -> p m i t", t=PACK, i=PACK)
+        nc.scalar.copy(out=un_dealt[:, :UN_SCALAR], in_=un_view[:, :UN_SCALAR])
+        nc.vector.tensor_copy(out=un_dealt[:, UN_SCALAR:], in_=un_view[:, UN_SCALAR:])
+        nc.vector.quantize_mx(out=un_codes[:].bitcast(FP8X4), scales=un_scale[:], in_=un_bf[:])
 
-        round_x(0, 0)
-        quantize_x(0, 0)
-        lead_message_passes(0)
-        message_pass(1, 0, 0, start=True)
-        round_x(0, 1, nc.scalar.copy, 0, HALF // 2)
-        round_x(0, 1, nc.vector.tensor_copy, HALF // 2, HALF)
-        quantize_x(0, 1)
-        lead_message_passes(1)
-        message_pass(1, 0, 1)
+        blocks = runs(0, FIRST, (P,))
+        first_banks = [bank("first%d" % b, (0, 5, 6)[b], P) for b in range(len(blocks))]
+        lead = {t: bank("lead%d" % t, t, FIRST) for t in (1, 2)}
+        rest = {(0, c): bank("rest0" + c, number, width(c)) for c, number in (("b", 3), ("c", 4))}
+        for acc, block in zip(first_banks, blocks):
+            state_pass(acc, 0, *block, start=True)
+        for c in ("b", "c"):
+            state_pass(rest[0, c], 0, *CHUNKS[c], start=True)
+        x_bf["a", 0] = tile("x_bf_a0", [P, FIRST * PACK], BF16)[:]
+        round_x("a", 0, nc.scalar.copy, 0, 2 * P)
+        round_x("a", 0, nc.vector.tensor_copy, 2 * P, FIRST)
+        quantize_x("a", 0)
+        for acc, block in zip(first_banks, blocks):
+            message_pass(acc, 0, *block, 0)
+        x_bf["a", 1] = tile("x_bf_a1", [P, FIRST * PACK], BF16, "x_bf_a0")[:]
+        round_x("a", 1, nc.vector.tensor_copy, 0, P)
+        round_x("a", 1, nc.scalar.copy, P, 2 * P)
+        round_x("a", 1, nc.vector.tensor_copy, 2 * P, FIRST)
+        quantize_x("a", 1, (P,))
+        lead_updated = {t: tile("lead_updated%d" % t, [P, FIRST], F32) for t in range(2)}
+        first_act = tile("first_act", [P, FIRST], F32)
+        for acc, (first, last) in zip(first_banks, blocks):
+            message_pass(acc, 0, first, last, 1, stop=True)
+            activate(first_act[:, first:last], acc, 0)
+        gather_add(lead_updated[0][:], 0, 0, FIRST, first_act[:])
+        scatter(0, 0, FIRST, lead_updated[0][:])
+        for t in (1, 2):
+            message_pass(lead[t], t, 0, FIRST, 1, start=True, backwards=True)
+            message_pass(lead[t], t, 0, FIRST, 0)
+            state_pass(lead[t], t, 0, FIRST, stop=True)
+        lead_act = tile("lead_act1", [P, FIRST], F32, "first_act")
+        activate(lead_act[:], lead[1], 1)
+        gather_add(lead_updated[1][:], 1, 0, FIRST, lead_act[:])
+        scatter(1, 0, FIRST, lead_updated[1][:])
+        lead_act = tile("lead_act2", [P, FIRST], F32)
+        activate(lead_act[:], lead[2], 2)
+        make_x_bf("b", "lead_updated0")
+        round_x("b", 0)
+        round_x("b", 1)
+        quantize_x("b", 0)
+        message_pass(rest[0, "b"], 0, *CHUNKS["b"], 0)
+        lead_updated[2] = tile("lead_updated2", [P, FIRST], F32, "x_raw_b1")
+        gather_add(lead_updated[2][:], 2, 0, FIRST, lead_act[:])
+        quantize_x("b", 1)
+        message_pass(rest[0, "b"], 0, *CHUNKS["b"], 1, stop=True)
+        scatter(2, 0, FIRST, lead_updated[2][:])
+        rest[1, "b"] = bank("rest1b", 5, width("b"))
+        message_pass(rest[1, "b"], 1, *CHUNKS["b"], 1, start=True, backwards=True)
+        message_pass(rest[1, "b"], 1, *CHUNKS["b"], 0)
+        state_pass(rest[1, "b"], 1, *CHUNKS["b"], stop=True)
+        rest[1, "c"] = bank("rest1c", 6, width("c"))
+        state_pass(rest[1, "c"], 1, *CHUNKS["c"], start=True)
+        make_x_bf("c", "lead_updated0")
+        for a in range(PASSES):
+            round_x("c", a)
+            quantize_x("c", a)
+            for t in range(2):
+                message_pass(rest[t, "c"], t, *CHUNKS["c"], a, stop=a == 1)
 
-        un_bf0 = tile("un_bf0", [P, P, PACK], BF16)
-        nc.vector.tensor_copy(out=un_bf0[:, : P // 2, :], in_=un_view[:, : P // 2, :, 0])
-        nc.scalar.copy(out=un_bf0[:, P // 2 :, :], in_=un_view[:, P // 2 :, :, 0])
-        quantize_un(0, 1, un_codes[0], un_bf0[:].rearrange("p m i -> p (m i)"))
-        un_bf3 = tile("un_bf3", [P, P * PACK], BF16)
-        nc.scalar.copy(out=un_bf3[:].rearrange("p (m i) -> p m i", i=PACK), in_=un_view[:, :, :, 3])
-        lead_act = [tile("lead_act%d" % g, [P, LEAD], F32) for g in range(2)]
-        for g in range(2):
-            nc.tensor.matmul_mx(
-                out=lead[g][:],
-                lhsT=un_codes[0].bitcast(FP8X4),
-                lhsT_scale=un_scale[:, :P],
-                rhs=picked[:, g * LEAD : (g + 1) * LEAD].bitcast(FP8X4),
-                rhs_scale=picked_scale[SCALE_ROW0:P, g * LEAD : (g + 1) * LEAD],
-                start=False,
-                stop=True,
-            )
-            nc.scalar.activation(out=lead_act[g][:], in_=lead[g][:], func=TANH, bias=bias[:, 0:1])
-        un_bf12 = tile("un_bf12", [P, 2 * P * PACK], BF16, "un_bf0")
-        nc.vector.tensor_copy(out=un_bf12[:].rearrange("p (t m i) -> p m i t", t=2, i=PACK), in_=un_view[:, :, :, 1:3])
-        un_codes12 = tile("un_codes12", [P, 2 * P], U32)
-        un_codes[1], un_codes[2] = un_codes12[:, :P], un_codes12[:, P:]
-        quantize_un(1, 3, un_codes12[:], un_bf12[:])
-        for g in range(2):
-            nc.vector.tensor_tensor(
-                updated[0, 0][:, g * LEAD : (g + 1) * LEAD],
-                state[0][:].indirect(offsets[:, g * LEAD // GROUP : (g + 1) * LEAD // GROUP]),
-                lead_act[g][:],
-                ADD,
-            )
-        un_codes[3] = tile("un_codes3", [P, P], U32, "lead_act0")[:]
-        quantize_un(3, 4, un_codes[3], un_bf3[:])
-        scatter(0, 0)
-        state_pass(1, 0, stop=True)
-        for t in range(2, PACK):
-            state_pass(t, 0, start=True)
-            message_pass(t, 0, 0)
-            message_pass(t, 0, 1, stop=True)
-        state_pass(0, 1, start=True)
-        activate(1, 0)
-
-        x_bf[1, 0] = tile("x_bf10", [P, HALF * PACK], BF16, "lead_act1")
-        round_x(1, 0)
-        updated[1, 0] = tile("updated10", [P, HALF], F32, "x_raw10")[:]
-        gather_add(1, 0)
-        quantize_x(1, 0)
-        scatter(1, 0)
-        x_bf[1, 1] = tile("x_bf11", [P, HALF * PACK], BF16, "act10")
-        round_x(1, 1)
-        message_pass(0, 1, 0)
-        quantize_x(1, 1)
-
-        act[2, 0] = tile("act20", [P, HALF], F32, "x_raw11")
-        activate(2, 0)
-        act[3, 0] = tile("act30", [P, HALF], F32, "act10")
-        activate(3, 0)
-        gather_add(2, 0)
-        message_pass(0, 1, 1, stop=True)
-        activate(0, 1)
-        for t in range(1, PACK):
-            message_pass(t, 1, 1, start=True)
-            message_pass(t, 1, 0)
-            state_pass(t, 1, stop=True)
-            activate(t, 1)
-        gather_add(3, 0)
-        gather_add(0, 1)
-        scatter(0, 1)
+        act01 = tile("act01", [P, 2 * REST], F32, "x_raw_c1")
+        act = {t: act01[:, t * REST : (t + 1) * REST] for t in range(2)}
+        act[2] = tile("act2", [P, REST], F32)[:]
+        act[3] = tile("act3", [P, J], F32)[:]
+        updated = {t: tile("updated%d" % t, [P, REST], F32) for t in range(3)}
+        for c in ("b", "c"):
+            first, last = CHUNKS[c]
+            part = slice(first - FIRST, last - FIRST)
+            for t in range(2):
+                activate(act[t][:, part], rest[t, c], t)
+                gather_add(updated[t][:, part], t, first, last, act[t][:, part])
+        late = [(2, FIRST, FIRST + HALF, 7), (2, FIRST + HALF, J, 0), (3, 0, HALF, 4), (3, HALF, J, 3)]
+        for t, first, last, number in late:
+            acc = bank("late%d_%d" % (t, first), number, last - first)
+            message_pass(acc, t, first, last, 1, start=True)
+            message_pass(acc, t, first, last, 0)
+            state_pass(acc, t, first, last, stop=True)
+            base = 0 if t == 3 else FIRST
+            activate(act[t][:, first - base : last - base], acc, t)
+        scatter(0, FIRST, J, updated[0][:])
         finish_row_set(0)
-        gather_add(1, 1)
-        gather_add(2, 1)
-        scatter(1, 1)
+        scatter(1, FIRST, J, updated[1][:])
         finish_row_set(1)
-        gather_add(3, 1)
-        scatter_whole(2)
+        updated[3] = tile("updated3", [P, J], F32, "updated0")
+        gather_add(updated[2][:], 2, FIRST, J, act[2])
+        gather_add(updated[3][:, :HALF], 3, 0, HALF, act[3][:, :HALF])
+        scatter(2, FIRST, J, updated[2][:])
         finish_row_set(2)
-        scatter_whole(3)
+        gather_add(updated[3][:, HALF:], 3, HALF, J, act[3][:, HALF:])
+        scatter(3, 0, J, updated[3][:])
 
         nc.sync.dma_start(out=y_rows[3], in_=page[3][:])
         for q in SCALAR_PIECES:

@@ -27,12 +27,10 @@ RUN = 4
 SCALE_ROWS = 16
 SCALE_ROW0 = 4
 HALF = J // 2
-FIRST = 384
-REST = J - FIRST
-SECOND = 768
-CHUNKS = {"a": (0, FIRST), "b": (FIRST, SECOND), "c": (SECOND, J)}
+FIRST = 256
+CHUNKS = {"a": (0, FIRST), "b": (FIRST, HALF), "c": (HALF, J)}
 UN_SCALAR = 80
-SPREAD = J // P
+SPREAD = FIRST // P
 BANK_BLOCKS = 4
 PIECE = 512
 PIECES = T // PIECE
@@ -84,7 +82,7 @@ def tile_list_tgn_rnnP_kernel(
         weight_row = tile("weight_row", [P, SPREAD], F32)
         identity = tile("identity", [P, P], F32)
         x_raw = {(c, a): tile("x_raw_%s%d" % (c, a), [P, PACK, width(c)], F32) for c, a in x_parts}
-        x_bf = {}
+        x_bf = {(c, a): tile("x_bf_%s%d" % (c, a), [P, width(c) * PACK], BF16) for c, a in x_parts}
         x_codes = [tile("x_codes%d" % a, [P, J], U32) for a in range(PASSES)]
         x_scale = [tile("x_scale%d" % a, [P, J], U8) for a in range(PASSES)]
         state = [tile("state%d" % t, [P, T], F32) for t in range(PACK)]
@@ -92,9 +90,9 @@ def tile_list_tgn_rnnP_kernel(
         page[3] = page[0]
         y_bf = [tile("y_bf%d" % q, [P, PIECE, PACK], BF16) for q in range(PIECES)]
         y_codes = [tile("y_codes%d" % q, [P, PIECE], I32) for q in range(PIECES)]
-        pair01 = tile("pair01", [P, T], U32)
+        pairs = [tile("pairs%d" % q, [P, 2, PIECE], U32) for q in range(PIECES)]
         y_scale = tile("y_scale", [P, T], U8)
-        spread = [ps.tile([P, BANK_BLOCKS, P], F32, name="spread%d" % h, tag="bank%d" % (6 + h)) for h in range(2)]
+        spread = ps.tile([P, SPREAD, P], F32, name="spread", tag="bank7")
 
         x_rows = x.rearrange("(a p i) j -> a p i j", a=PASSES, i=PACK)
         h_rows = hT.rearrange("(p t) c -> t p c", t=PACK)
@@ -115,6 +113,8 @@ def tile_list_tgn_rnnP_kernel(
         nc.gpsimd.memset(wn_scale_raw[:].bitcast(I32), 0)
         make_identity(nc, identity[:])
         nc.vector.memset(page[0][:].bitcast(I32), 0)
+        for q in range(PIECES):
+            nc.scalar.copy(out=pairs[q][:, 1, :], in_=page[0][:, q * PIECE : (q + 1) * PIECE].bitcast(U32))
 
         nc.sync.dma_start(offsets[:], offs)
         nc.sync.dma_start(
@@ -127,7 +127,7 @@ def tile_list_tgn_rnnP_kernel(
                 in_=tab_scales.bitcast(I32)[0, r:SCALE_ROWS:RUN, :],
             )
         nc.sync.dma_start(out=table[:], in_=tab_words[0].rearrange("p t i -> p (t i)").bitcast(I32))
-        nc.sync.dma_start(out=weight_row[:], in_=wgo[0].rearrange("(r m) -> r m", m=SPREAD))
+        nc.sync.dma_start(out=weight_row[:], in_=wgo[0, :FIRST].rearrange("(r m) -> r m", m=SPREAD))
         for r in range(RUN):
             nc.sync.dma_start(
                 out=wn_scale_raw[r:P:QUADRANT, :].bitcast(I32).rearrange("r (a w) -> r a w", a=PASSES),
@@ -137,20 +137,19 @@ def tile_list_tgn_rnnP_kernel(
         load_x("a")
         nc.sync.dma_start(out=bias[:], in_=bn.rearrange("(p t) -> p t", t=PACK))
         load_state(0)
-        load_state(1)
         load_x("b")
+        load_state(1)
         load_state(2)
+        nc.sync.dma_start(out=weight[:, FIRST:HALF], in_=wgo[:, FIRST:HALF])
         load_x("c")
         load_state(3)
+        nc.sync.dma_start(out=weight[:, HALF:], in_=wgo[:, HALF:])
 
-        for h in range(SPREAD // BANK_BLOCKS):
-            for m in range(BANK_BLOCKS):
-                column = weight_row[:, BANK_BLOCKS * h + m : BANK_BLOCKS * h + m + 1]
-                nc.tensor.transpose(spread[h][:, m, :], column.to_broadcast([P, P]), identity[:])
-            nc.scalar.copy(
-                out=weight[:].rearrange("p (r m) -> p r m", m=SPREAD)[:, :, BANK_BLOCKS * h : BANK_BLOCKS * (h + 1)],
-                in_=spread[h][:].rearrange("p m r -> p r m"),
-            )
+        for m in range(SPREAD):
+            nc.tensor.transpose(spread[:, m, :], weight_row[:, m : m + 1].to_broadcast([P, P]), identity[:])
+        nc.scalar.copy(
+            out=weight[:, :FIRST].rearrange("p (r m) -> p r m", m=SPREAD), in_=spread[:].rearrange("p m r -> p r m")
+        )
 
         def clear_page(t, after):
             page[t] = tile("page%d" % t, [P, T], F32, after)
@@ -169,11 +168,6 @@ def tile_list_tgn_rnnP_kernel(
             in_=wn_scale_raw[:].rearrange("p (a m t) -> p a t m", a=PASSES, t=PACK),
         )
 
-        def make_x_bf(c, after):
-            both = tile("x_bf_" + c, [P, PASSES * width(c) * PACK], BF16, after)
-            for a in range(PASSES):
-                x_bf[c, a] = both[:, a * width(c) * PACK : (a + 1) * width(c) * PACK]
-
         def round_x(c, a, engine_copy=nc.scalar.copy, first=0, last=None):
             last = last or width(c)
             engine_copy(
@@ -181,7 +175,7 @@ def tile_list_tgn_rnnP_kernel(
                 in_=x_raw[c, a][:, :, first:last].rearrange("p i (g e) -> p g i e", e=2),
             )
 
-        def quantize_x(c, a, widths=(256, 128)):
+        def quantize_x(c, a, widths=(512, 256)):
             base = CHUNKS[c][0]
             for first, last in runs(0, width(c), widths):
                 nc.vector.quantize_mx(
@@ -221,30 +215,33 @@ def tile_list_tgn_rnnP_kernel(
         def activate(out, acc, t):
             nc.scalar.activation(out=out, in_=acc[:], func=TANH, bias=bias[:, t : t + 1])
 
-        def gather_add(out, t, first, last, act):
-            nc.vector.tensor_tensor(out, state[t][:].indirect(entries(first, last)), act, ADD)
+        def gather(t, first, last):
+            nc.vector.tensor_copy(held[t][:, first:last], state[t][:].indirect(entries(first, last)))
 
-        def scatter(t, first, last, values):
-            nc.vector.tensor_tensor(page[t][:].indirect(entries(first, last)), values, weight[:, first:last], MULT)
+        def update(t, first, last, out=None):
+            summed = tile("summed%d_%d" % (t, first), [P, last - first], F32, "summed")
+            nc.gpsimd.tensor_tensor(summed[:], act[t][:, first:last], held[t][:, first:last], ADD)
+            out = act[t][:, first:last] if out is None else out
+            nc.gpsimd.tensor_tensor(out, summed[:], weight[:, first:last], MULT)
+
+        def scatter(t, first, last, values=None):
+            values = act[t][:, first:last] if values is None else values
+            nc.vector.tensor_copy(page[t][:].indirect(entries(first, last)), values)
 
         def interleave(engine_copy, t, q):
             engine_copy(out=y_bf[q][:, :, t], in_=page[t][:, q * PIECE : (q + 1) * PIECE])
 
         def finish_row_set(t):
             nc.sync.dma_start(out=y_rows[t], in_=page[t][:])
-            if t < 2:
-                pairs = pair01[:].bitcast(BF16).rearrange("p (c u) -> p c u", u=2)
-                nc.scalar.copy(out=pairs[:, :, t], in_=page[t][:])
             for q in VECTOR_PIECES + SCALAR_PIECES:
-                columns = slice(q * PIECE, (q + 1) * PIECE)
-                if t == 1:
+                piece = page[t][:, q * PIECE : (q + 1) * PIECE]
+                halves = pairs[q][:, t // 2, :].bitcast(BF16).rearrange("p (c u) -> p c u", u=2)
+                if t < 2:
+                    nc.scalar.copy(out=halves[:, :, t], in_=piece)
+                else:
+                    nc.gpsimd.tensor_scalar(halves[:, :, 0], piece, unit[:, 0:1], unit[:, 1:2], MULT, ADD)
                     words = y_bf[q][:].rearrange("p c i -> p (c i)").bitcast(U32).rearrange("p (c u) -> p c u", u=2)
-                    nc.scalar.copy(out=words, in_=pair01[:, columns].unsqueeze(2).to_broadcast([P, PIECE, 2]))
-                elif t == 2 and q in VECTOR_PIECES:
-                    piece = page[t][:, columns]
-                    nc.scalar.copy(out=y_bf[q][:, :, 2:4], in_=piece.unsqueeze(2).to_broadcast([P, PIECE, 2]))
-                elif t == 2:
-                    interleave(nc.scalar.copy, t, q)
+                    nc.scalar.copy(out=words, in_=pairs[q][:].rearrange("p u c -> p c u"))
 
         un_view = un_raw[:].rearrange("p i (m t) -> p m i t", t=PACK)
 
@@ -254,95 +251,82 @@ def tile_list_tgn_rnnP_kernel(
         nc.vector.tensor_copy(out=un_dealt[:, UN_SCALAR:], in_=un_view[:, UN_SCALAR:])
         nc.vector.quantize_mx(out=un_codes[:].bitcast(FP8X4), scales=un_scale[:], in_=un_bf[:])
 
+        act = [tile("act%d" % t, [P, J], F32) for t in range(PACK)]
+        held = {t: tile("held%d" % t, [P, J], F32)[:] for t in (0, 1, 3)}
+
+        def late_group(t, first, last, number):
+            acc = bank("late%d_%d" % (t, first), number, last - first)
+            message_pass(acc, t, first, last, 1, start=True, backwards=True)
+            message_pass(acc, t, first, last, 0)
+            state_pass(acc, t, first, last, stop=True)
+            activate(act[t][:, first:last], acc, t)
+
         blocks = runs(0, FIRST, (P,))
-        first_banks = [bank("first%d" % b, (0, 5, 6)[b], P) for b in range(len(blocks))]
-        lead = {t: bank("lead%d" % t, t, FIRST) for t in (1, 2)}
-        rest = {(0, c): bank("rest0" + c, number, width(c)) for c, number in (("b", 3), ("c", 4))}
-        for acc, block in zip(first_banks, blocks):
-            state_pass(acc, 0, *block, start=True)
-        for c in ("b", "c"):
-            state_pass(rest[0, c], 0, *CHUNKS[c], start=True)
-        x_bf["a", 0] = tile("x_bf_a0", [P, FIRST * PACK], BF16)[:]
-        round_x("a", 0, nc.scalar.copy, 0, 2 * P)
-        round_x("a", 0, nc.vector.tensor_copy, 2 * P, FIRST)
+        first_banks = [bank("first%d" % b, b, P) for b in range(len(blocks))]
+        early = {(0, "b"): 3, (1, "b"): 4, (0, "c"): 5}
+        acc = {(t, c): bank("early%d%s" % (t, c), number, width(c)) for (t, c), number in early.items()}
+        for bank_b, block in zip(first_banks, blocks):
+            state_pass(bank_b, 0, *block, start=True)
+        for t, c in early:
+            state_pass(acc[t, c], t, *CHUNKS[c], start=True)
+        round_x("a", 0)
         quantize_x("a", 0)
-        for acc, block in zip(first_banks, blocks):
-            message_pass(acc, 0, *block, 0)
-        x_bf["a", 1] = tile("x_bf_a1", [P, FIRST * PACK], BF16, "x_bf_a0")[:]
+        for bank_b, block in zip(first_banks, blocks):
+            message_pass(bank_b, 0, *block, 0)
         round_x("a", 1, nc.vector.tensor_copy, 0, P)
-        round_x("a", 1, nc.scalar.copy, P, 2 * P)
-        round_x("a", 1, nc.vector.tensor_copy, 2 * P, FIRST)
+        round_x("a", 1, nc.scalar.copy, P, FIRST)
         quantize_x("a", 1, (P,))
-        lead_updated = {t: tile("lead_updated%d" % t, [P, FIRST], F32) for t in range(2)}
-        first_act = tile("first_act", [P, FIRST], F32)
-        for acc, (first, last) in zip(first_banks, blocks):
-            message_pass(acc, 0, first, last, 1, stop=True)
-            activate(first_act[:, first:last], acc, 0)
-        gather_add(lead_updated[0][:], 0, 0, FIRST, first_act[:])
-        scatter(0, 0, FIRST, lead_updated[0][:])
-        for t in (1, 2):
-            message_pass(lead[t], t, 0, FIRST, 1, start=True, backwards=True)
-            message_pass(lead[t], t, 0, FIRST, 0)
-            state_pass(lead[t], t, 0, FIRST, stop=True)
-        lead_act = tile("lead_act1", [P, FIRST], F32, "first_act")
-        activate(lead_act[:], lead[1], 1)
-        gather_add(lead_updated[1][:], 1, 0, FIRST, lead_act[:])
-        scatter(1, 0, FIRST, lead_updated[1][:])
-        lead_act = tile("lead_act2", [P, FIRST], F32)
-        activate(lead_act[:], lead[2], 2)
-        make_x_bf("b", "lead_updated0")
-        round_x("b", 0)
-        round_x("b", 1)
-        quantize_x("b", 0)
-        message_pass(rest[0, "b"], 0, *CHUNKS["b"], 0)
-        lead_updated[2] = tile("lead_updated2", [P, FIRST], F32, "x_raw_b1")
-        gather_add(lead_updated[2][:], 2, 0, FIRST, lead_act[:])
-        quantize_x("b", 1)
-        message_pass(rest[0, "b"], 0, *CHUNKS["b"], 1, stop=True)
-        scatter(2, 0, FIRST, lead_updated[2][:])
-        rest[1, "b"] = bank("rest1b", 5, width("b"))
-        message_pass(rest[1, "b"], 1, *CHUNKS["b"], 1, start=True, backwards=True)
-        message_pass(rest[1, "b"], 1, *CHUNKS["b"], 0)
-        state_pass(rest[1, "b"], 1, *CHUNKS["b"], stop=True)
-        rest[1, "c"] = bank("rest1c", 6, width("c"))
-        state_pass(rest[1, "c"], 1, *CHUNKS["c"], start=True)
-        make_x_bf("c", "lead_updated0")
+        for bank_b, (first, last) in zip(first_banks, blocks):
+            message_pass(bank_b, 0, first, last, 1, stop=True)
+            activate(act[0][:, first:last], bank_b, 0)
+        late_group(1, 0, FIRST, 2)
+        gather(0, 0, FIRST)
+        gather(0, FIRST, J)
+        update(0, 0, FIRST)
+        scatter(0, 0, FIRST)
+
+        for a in range(PASSES):
+            round_x("b", a)
+            quantize_x("b", a)
+            for t in range(2):
+                message_pass(acc[t, "b"], t, FIRST, HALF, a, stop=a == 1)
+        for t in range(2):
+            activate(act[t][:, FIRST:HALF], acc[t, "b"], t)
+        late_group(2, 0, HALF, 6)
+        late_group(3, 0, HALF, 7)
+        gather(1, 0, FIRST)
+        gather(1, FIRST, J)
+        update(1, 0, FIRST)
+        scatter(1, 0, FIRST)
+        held[2] = tile("held2_ab", [P, HALF], F32)[:]
+        gather(2, 0, HALF)
+        for t in range(2):
+            update(t, FIRST, HALF)
+            scatter(t, FIRST, HALF)
+
         for a in range(PASSES):
             round_x("c", a)
             quantize_x("c", a)
-            for t in range(2):
-                message_pass(rest[t, "c"], t, *CHUNKS["c"], a, stop=a == 1)
-
-        act01 = tile("act01", [P, 2 * REST], F32, "x_raw_c1")
-        act = {t: act01[:, t * REST : (t + 1) * REST] for t in range(2)}
-        act[2] = tile("act2", [P, REST], F32)[:]
-        act[3] = tile("act3", [P, J], F32)[:]
-        updated = {t: tile("updated%d" % t, [P, REST], F32) for t in range(3)}
-        for c in ("b", "c"):
-            first, last = CHUNKS[c]
-            part = slice(first - FIRST, last - FIRST)
-            for t in range(2):
-                activate(act[t][:, part], rest[t, c], t)
-                gather_add(updated[t][:, part], t, first, last, act[t][:, part])
-        late = [(2, FIRST, FIRST + HALF, 7), (2, FIRST + HALF, J, 0), (3, 0, HALF, 4), (3, HALF, J, 3)]
-        for t, first, last, number in late:
-            acc = bank("late%d_%d" % (t, first), number, last - first)
-            message_pass(acc, t, first, last, 1, start=True)
-            message_pass(acc, t, first, last, 0)
-            state_pass(acc, t, first, last, stop=True)
-            base = 0 if t == 3 else FIRST
-            activate(act[t][:, first - base : last - base], acc, t)
-        scatter(0, FIRST, J, updated[0][:])
-        finish_row_set(0)
-        scatter(1, FIRST, J, updated[1][:])
-        finish_row_set(1)
-        updated[3] = tile("updated3", [P, J], F32, "updated0")
-        gather_add(updated[2][:], 2, FIRST, J, act[2])
-        gather_add(updated[3][:, :HALF], 3, 0, HALF, act[3][:, :HALF])
-        scatter(2, FIRST, J, updated[2][:])
-        finish_row_set(2)
-        gather_add(updated[3][:, HALF:], 3, HALF, J, act[3][:, HALF:])
-        scatter(3, 0, J, updated[3][:])
+            message_pass(acc[0, "c"], 0, HALF, J, a, stop=a == 1)
+        activate(act[0][:, HALF:], acc[0, "c"], 0)
+        for t, number in ((1, 0), (2, 1), (3, 2)):
+            late_group(t, HALF, J, number)
+        weighed = tile("weighed2", [P, HALF], F32, "x_bf_c1")
+        update(2, 0, HALF, weighed[:])
+        held[2] = tile("held2_c", [P, J], F32, "x_raw_c1")[:]
+        gather(2, HALF, J)
+        gather(3, 0, J)
+        scatter(2, 0, HALF, weighed[:])
+        for t in range(3):
+            update(t, HALF, J)
+        update(3, 0, J)
+        unit = tile("unit", [P, 2], F32, "weight")
+        nc.gpsimd.memset(unit[:, 0:1], 1.0)
+        nc.gpsimd.memset(unit[:, 1:2], 0.0)
+        for t in range(3):
+            scatter(t, HALF, J)
+            finish_row_set(t)
+        scatter(3, 0, J)
 
         nc.sync.dma_start(out=y_rows[3], in_=page[3][:])
         for q in SCALAR_PIECES:

@@ -29,7 +29,7 @@ SCALE_ROW0 = 4
 HALF = J // 2
 FIRST = 256
 CHUNKS = {"a": (0, FIRST), "b": (FIRST, HALF), "c": (HALF, J)}
-UN_SCALAR = 80
+UN_SCALAR = 64
 SPREAD = FIRST // P
 BANK_BLOCKS = 4
 PIECE = 512
@@ -72,7 +72,7 @@ def tile_list_tgn_rnnP_kernel(
         wn_scale = tile("wn_scale", [P, PASSES * N], U8)
         table = tile("table", [P, T], I32)
         table_scale = tile("table_scale", [P, T], U8)
-        picked = tile("picked", [P, J], I32)
+        picked = {0: tile("picked0", [P, HALF], I32)}
         picked_scale = tile("picked_scale", [P, J], U8)
         un_raw = tile("un_raw", [P, PACK, N], F32)
         un_codes = tile("un_codes", [P, N], U32)
@@ -101,6 +101,10 @@ def tile_list_tgn_rnnP_kernel(
 
         def entries(first, last):
             return offsets[:, first // GROUP : last // GROUP]
+
+        def pick_words(h):
+            window = table[:].bitcast(U32)
+            nc.vector.tensor_copy(picked[h][:].bitcast(U32), window.indirect(entries(h * HALF, (h + 1) * HALF)))
 
         def load_state(t):
             nc.sync.dma_start(out=state[t][:], in_=h_rows[t])
@@ -162,7 +166,7 @@ def tile_list_tgn_rnnP_kernel(
         clear_page(1, "wn_raw")
         nc.vector.tensor_copy(picked_scale[:], table_scale[:].indirect(offsets[:]))
         clear_page(2, "table_scale")
-        nc.vector.tensor_copy(picked[:].bitcast(U32), table[:].bitcast(U32).indirect(offsets[:]))
+        pick_words(0)
         nc.vector.tensor_copy(
             out=wn_scale[:].rearrange("p (a t m) -> p a t m", a=PASSES, t=PACK),
             in_=wn_scale_raw[:].rearrange("p (a m t) -> p a t m", a=PASSES, t=PACK),
@@ -206,7 +210,7 @@ def tile_list_tgn_rnnP_kernel(
                     out=acc[:, j0 - first : j1 - first],
                     lhsT=un_codes[:, t * P : (t + 1) * P].bitcast(FP8X4),
                     lhsT_scale=un_scale[:, t * P : (t + 1) * P],
-                    rhs=picked[:, j0:j1].bitcast(FP8X4),
+                    rhs=picked[j0 // HALF][:, j0 % HALF : j0 % HALF + j1 - j0].bitcast(FP8X4),
                     rhs_scale=picked_scale[SCALE_ROW0:P, j0:j1],
                     start=start and j0 == first,
                     stop=stop and j1 == last,
@@ -223,6 +227,12 @@ def tile_list_tgn_rnnP_kernel(
             nc.gpsimd.tensor_tensor(summed[:], act[t][:, first:last], held[t][:, first:last], ADD)
             out = act[t][:, first:last] if out is None else out
             nc.gpsimd.tensor_tensor(out, summed[:], weight[:, first:last], MULT)
+
+        def update_first(t):
+            summed = tile("summed%d_0" % t, [P, FIRST], F32, "summed")
+            nc.vector.tensor_tensor(summed[:], state[t][:].indirect(entries(0, FIRST)), act[t][:, :FIRST], ADD)
+            gather(t, FIRST, J)
+            nc.gpsimd.tensor_tensor(act[t][:, :FIRST], summed[:], weight[:, :FIRST], MULT)
 
         def scatter(t, first, last, values=None):
             values = act[t][:, first:last] if values is None else values
@@ -267,22 +277,23 @@ def tile_list_tgn_rnnP_kernel(
         acc = {(t, c): bank("early%d%s" % (t, c), number, width(c)) for (t, c), number in early.items()}
         for bank_b, block in zip(first_banks, blocks):
             state_pass(bank_b, 0, *block, start=True)
-        for t, c in early:
-            state_pass(acc[t, c], t, *CHUNKS[c], start=True)
-        round_x("a", 0)
+        for t in range(2):
+            state_pass(acc[t, "b"], t, FIRST, HALF, start=True)
+        round_x("a", 0, nc.vector.tensor_copy, 0, P)
+        round_x("a", 0, nc.scalar.copy, P, FIRST)
         quantize_x("a", 0)
         for bank_b, block in zip(first_banks, blocks):
             message_pass(bank_b, 0, *block, 0)
         round_x("a", 1, nc.vector.tensor_copy, 0, P)
         round_x("a", 1, nc.scalar.copy, P, FIRST)
         quantize_x("a", 1, (P,))
+        picked[1] = tile("picked1", [P, HALF], I32, "x_raw_a1")
+        pick_words(1)
         for bank_b, (first, last) in zip(first_banks, blocks):
             message_pass(bank_b, 0, first, last, 1, stop=True)
             activate(act[0][:, first:last], bank_b, 0)
         late_group(1, 0, FIRST, 2)
-        gather(0, 0, FIRST)
-        gather(0, FIRST, J)
-        update(0, 0, FIRST)
+        update_first(0)
         scatter(0, 0, FIRST)
 
         for a in range(PASSES):
@@ -294,9 +305,7 @@ def tile_list_tgn_rnnP_kernel(
             activate(act[t][:, FIRST:HALF], acc[t, "b"], t)
         late_group(2, 0, HALF, 6)
         late_group(3, 0, HALF, 7)
-        gather(1, 0, FIRST)
-        gather(1, FIRST, J)
-        update(1, 0, FIRST)
+        update_first(1)
         scatter(1, 0, FIRST)
         held[2] = tile("held2_ab", [P, HALF], F32)[:]
         gather(2, 0, HALF)
@@ -307,7 +316,9 @@ def tile_list_tgn_rnnP_kernel(
         for a in range(PASSES):
             round_x("c", a)
             quantize_x("c", a)
-            message_pass(acc[0, "c"], 0, HALF, J, a, stop=a == 1)
+            message_pass(acc[0, "c"], 0, HALF, J, a, start=a == 0, stop=a == 1)
+            if a == 0:
+                state_pass(acc[0, "c"], 0, HALF, J)
         activate(act[0][:, HALF:], acc[0, "c"], 0)
         for t, number in ((1, 0), (2, 1), (3, 2)):
             late_group(t, HALF, J, number)

@@ -28,7 +28,7 @@ SCALE_ROWS = 16
 SCALE_ROW0 = 4
 HALF = J // 2
 FIRST = 256
-CHUNKS = {"a": (0, FIRST), "b": (FIRST, HALF), "c": (HALF, J)}
+CHUNKS = {"a": (0, FIRST), "b": (FIRST, HALF), "c": (HALF, HALF + FIRST), "d": (HALF + FIRST, J)}
 UN_SCALAR = 64
 SPREAD = FIRST // P
 BANK_BLOCKS = 4
@@ -82,7 +82,11 @@ def tile_list_tgn_rnnP_kernel(
         weight_row = tile("weight_row", [P, SPREAD], F32)
         identity = tile("identity", [P, P], F32)
         x_raw = {(c, a): tile("x_raw_%s%d" % (c, a), [P, PACK, width(c)], F32) for c, a in x_parts}
-        x_bf = {(c, a): tile("x_bf_%s%d" % (c, a), [P, width(c) * PACK], BF16) for c, a in x_parts}
+        x_bf = {(c, a): tile("x_bf_%s%d" % (c, a), [P, FIRST * PACK], BF16)[:] for c in "ab" for a in range(PASSES)}
+        x_bf_late = [tile("x_bf_late%d" % a, [P, HALF * PACK], BF16) for a in range(PASSES)]
+        for a in range(PASSES):
+            x_bf["c", a] = x_bf_late[a][:, : FIRST * PACK]
+            x_bf["d", a] = x_bf_late[a][:, FIRST * PACK :]
         x_codes = [tile("x_codes%d" % a, [P, J], U32) for a in range(PASSES)]
         x_scale = [tile("x_scale%d" % a, [P, J], U8) for a in range(PASSES)]
         state = [tile("state%d" % t, [P, T], F32) for t in range(PACK)]
@@ -109,9 +113,10 @@ def tile_list_tgn_rnnP_kernel(
         def load_state(t):
             nc.sync.dma_start(out=state[t][:], in_=h_rows[t])
 
-        def load_x(c):
+        def load_x(chunks):
             for a in range(PASSES):
-                nc.sync.dma_start(out=x_raw[c, a][:], in_=x_rows[a][:, :, CHUNKS[c][0] : CHUNKS[c][1]])
+                for c in chunks:
+                    nc.sync.dma_start(out=x_raw[c, a][:], in_=x_rows[a][:, :, CHUNKS[c][0] : CHUNKS[c][1]])
 
         nc.gpsimd.memset(table_scale[:].bitcast(I32), 0)
         nc.gpsimd.memset(wn_scale_raw[:].bitcast(I32), 0)
@@ -145,7 +150,7 @@ def tile_list_tgn_rnnP_kernel(
         load_state(1)
         load_state(2)
         nc.sync.dma_start(out=weight[:, FIRST:HALF], in_=wgo[:, FIRST:HALF])
-        load_x("c")
+        load_x("cd")
         load_state(3)
         nc.sync.dma_start(out=weight[:, HALF:], in_=wgo[:, HALF:])
 
@@ -179,7 +184,7 @@ def tile_list_tgn_rnnP_kernel(
                 in_=x_raw[c, a][:, :, first:last].rearrange("p i (g e) -> p g i e", e=2),
             )
 
-        def quantize_x(c, a, widths=(512, 256)):
+        def quantize_x(c, a, widths=(256,)):
             base = CHUNKS[c][0]
             for first, last in runs(0, width(c), widths):
                 nc.vector.quantize_mx(
@@ -222,11 +227,14 @@ def tile_list_tgn_rnnP_kernel(
         def gather(t, first, last):
             nc.vector.tensor_copy(held[t][:, first:last], state[t][:].indirect(entries(first, last)))
 
-        def update(t, first, last, out=None):
+        def add_state(t, first, last):
             summed = tile("summed%d_%d" % (t, first), [P, last - first], F32, "summed")
             nc.gpsimd.tensor_tensor(summed[:], act[t][:, first:last], held[t][:, first:last], ADD)
-            out = act[t][:, first:last] if out is None else out
-            nc.gpsimd.tensor_tensor(out, summed[:], weight[:, first:last], MULT)
+            return summed
+
+        def update(t, first, last):
+            summed = add_state(t, first, last)
+            nc.gpsimd.tensor_tensor(act[t][:, first:last], summed[:], weight[:, first:last], MULT)
 
         def update_first(t):
             summed = tile("summed%d_0" % t, [P, FIRST], F32, "summed")
@@ -273,8 +281,7 @@ def tile_list_tgn_rnnP_kernel(
 
         blocks = runs(0, FIRST, (P,))
         first_banks = [bank("first%d" % b, b, P) for b in range(len(blocks))]
-        early = {(0, "b"): 3, (1, "b"): 4, (0, "c"): 5}
-        acc = {(t, c): bank("early%d%s" % (t, c), number, width(c)) for (t, c), number in early.items()}
+        acc = {(t, "b"): bank("early%d" % t, 3 + t, FIRST) for t in range(2)}
         for bank_b, block in zip(first_banks, blocks):
             state_pass(bank_b, 0, *block, start=True)
         for t in range(2):
@@ -293,6 +300,9 @@ def tile_list_tgn_rnnP_kernel(
             message_pass(bank_b, 0, first, last, 1, stop=True)
             activate(act[0][:, first:last], bank_b, 0)
         late_group(1, 0, FIRST, 2)
+        for t in range(PACK):
+            acc[t, "c"] = bank("second_half%d" % t, (5, 0, 1, 2)[t], HALF)
+            state_pass(acc[t, "c"], t, HALF, J, start=True)
         update_first(0)
         scatter(0, 0, FIRST)
 
@@ -315,19 +325,24 @@ def tile_list_tgn_rnnP_kernel(
 
         for a in range(PASSES):
             round_x("c", a)
-            quantize_x("c", a)
-            message_pass(acc[0, "c"], 0, HALF, J, a, start=a == 0, stop=a == 1)
-            if a == 0:
-                state_pass(acc[0, "c"], 0, HALF, J)
+            round_x("d", a)
+            nc.vector.quantize_mx(out=x_codes[a][:, HALF:].bitcast(FP8X4), scales=x_scale[a][:, HALF:], in_=x_bf_late[a][:])
+            message_pass(acc[0, "c"], 0, HALF, J, a, stop=a == 1)
         activate(act[0][:, HALF:], acc[0, "c"], 0)
-        for t, number in ((1, 0), (2, 1), (3, 2)):
-            late_group(t, HALF, J, number)
-        weighed = tile("weighed2", [P, HALF], F32, "x_bf_c1")
-        update(2, 0, HALF, weighed[:])
-        held[2] = tile("held2_c", [P, J], F32, "x_raw_c1")[:]
+        for t in range(1, PACK):
+            message_pass(acc[t, "c"], t, HALF, J, 1)
+            message_pass(acc[t, "c"], t, HALF, J, 0, stop=True)
+            activate(act[t][:, HALF:], acc[t, "c"], t)
+        weighed = tile("weighed2", [P, HALF], F32, "x_bf_late1")
+        summed = add_state(2, 0, HALF)
+        for c in "ab":
+            part = slice(*CHUNKS[c])
+            nc.gpsimd.tensor_tensor(weighed[:, part], summed[:, part], weight[:, part], MULT)
+        held[2] = tile("held2_c", [P, J], F32, "x_raw_d1")[:]
         gather(2, HALF, J)
+        scatter(2, 0, FIRST, weighed[:, :FIRST])
         gather(3, 0, J)
-        scatter(2, 0, HALF, weighed[:])
+        scatter(2, FIRST, HALF, weighed[:, FIRST:])
         for t in range(3):
             update(t, HALF, J)
         update(3, 0, J)

@@ -148,10 +148,10 @@ def tile_list_tgn_rnnP_kernel(
         load_state(0)
         load_x("b")
         load_state(1)
-        load_state(2)
+        load_state(3)
         nc.sync.dma_start(out=weight[:, FIRST:HALF], in_=wgo[:, FIRST:HALF])
         load_x("cd")
-        load_state(3)
+        load_state(2)
         nc.sync.dma_start(out=weight[:, HALF:], in_=wgo[:, HALF:])
 
         for m in range(SPREAD):
@@ -170,7 +170,6 @@ def tile_list_tgn_rnnP_kernel(
         )
         clear_page(1, "wn_raw")
         nc.vector.tensor_copy(picked_scale[:], table_scale[:].indirect(offsets[:]))
-        clear_page(2, "table_scale")
         pick_words(0)
         nc.vector.tensor_copy(
             out=wn_scale[:].rearrange("p (a t m) -> p a t m", a=PASSES, t=PACK),
@@ -227,13 +226,9 @@ def tile_list_tgn_rnnP_kernel(
         def gather(t, first, last):
             nc.vector.tensor_copy(held[t][:, first:last], state[t][:].indirect(entries(first, last)))
 
-        def add_state(t, first, last):
-            summed = tile("summed%d_%d" % (t, first), [P, last - first], F32, "summed")
+        def update(t, first, last, slot):
+            summed = tile("summed%d_%d" % (t, first), [P, last - first], F32, slot)
             nc.gpsimd.tensor_tensor(summed[:], act[t][:, first:last], held[t][:, first:last], ADD)
-            return summed
-
-        def update(t, first, last):
-            summed = add_state(t, first, last)
             nc.gpsimd.tensor_tensor(act[t][:, first:last], summed[:], weight[:, first:last], MULT)
 
         def update_first(t):
@@ -257,7 +252,7 @@ def tile_list_tgn_rnnP_kernel(
                 if t < 2:
                     nc.scalar.copy(out=halves[:, :, t], in_=piece)
                 else:
-                    nc.gpsimd.tensor_scalar(halves[:, :, 0], piece, unit[:, 0:1], unit[:, 1:2], MULT, ADD)
+                    nc.gpsimd.tensor_scalar(halves[:, :, 0], piece, unit[:], 0.0, MULT, ADD)
                     words = y_bf[q][:].rearrange("p c i -> p (c i)").bitcast(U32).rearrange("p (c u) -> p c u", u=2)
                     nc.scalar.copy(out=words, in_=pairs[q][:].rearrange("p u c -> p c u"))
 
@@ -270,14 +265,16 @@ def tile_list_tgn_rnnP_kernel(
         nc.vector.quantize_mx(out=un_codes[:].bitcast(FP8X4), scales=un_scale[:], in_=un_bf[:])
 
         act = [tile("act%d" % t, [P, J], F32) for t in range(PACK)]
-        held = {t: tile("held%d" % t, [P, J], F32)[:] for t in (0, 1, 3)}
+        held = {t: tile("held%d" % t, [P, J], F32)[:] for t in range(PACK)}
 
-        def late_group(t, first, last, number):
+        act2_early = tile("act2_early", [P, J], F32)
+
+        def late_group(t, first, last, number, out):
             acc = bank("late%d_%d" % (t, first), number, last - first)
             message_pass(acc, t, first, last, 1, start=True, backwards=True)
             message_pass(acc, t, first, last, 0)
             state_pass(acc, t, first, last, stop=True)
-            activate(act[t][:, first:last], acc, t)
+            activate(out, acc, t)
 
         blocks = runs(0, FIRST, (P,))
         first_banks = [bank("first%d" % b, b, P) for b in range(len(blocks))]
@@ -296,10 +293,11 @@ def tile_list_tgn_rnnP_kernel(
         quantize_x("a", 1, (P,))
         picked[1] = tile("picked1", [P, HALF], I32, "x_raw_a1")
         pick_words(1)
+        clear_page(2, "x_bf_a1")
         for bank_b, (first, last) in zip(first_banks, blocks):
             message_pass(bank_b, 0, first, last, 1, stop=True)
             activate(act[0][:, first:last], bank_b, 0)
-        late_group(1, 0, FIRST, 2)
+        late_group(1, 0, FIRST, 2, act[1][:, :FIRST])
         for t in range(PACK):
             acc[t, "c"] = bank("second_half%d" % t, (5, 0, 1, 2)[t], HALF)
             state_pass(acc[t, "c"], t, HALF, J, start=True)
@@ -313,15 +311,15 @@ def tile_list_tgn_rnnP_kernel(
                 message_pass(acc[t, "b"], t, FIRST, HALF, a, stop=a == 1)
         for t in range(2):
             activate(act[t][:, FIRST:HALF], acc[t, "b"], t)
-        late_group(2, 0, HALF, 6)
-        late_group(3, 0, HALF, 7)
+        late_group(3, 0, HALF, 6, act[3][:, :HALF])
+        late_group(2, 0, HALF, 7, act2_early[:, :HALF])
         update_first(1)
         scatter(1, 0, FIRST)
-        held[2] = tile("held2_ab", [P, HALF], F32)[:]
-        gather(2, 0, HALF)
+        gather(3, 0, HALF)
         for t in range(2):
-            update(t, FIRST, HALF)
+            update(t, FIRST, HALF, "summed")
             scatter(t, FIRST, HALF)
+        update(3, 0, HALF, "summed")
 
         for a in range(PASSES):
             round_x("c", a)
@@ -333,22 +331,17 @@ def tile_list_tgn_rnnP_kernel(
             message_pass(acc[t, "c"], t, HALF, J, 1)
             message_pass(acc[t, "c"], t, HALF, J, 0, stop=True)
             activate(act[t][:, HALF:], acc[t, "c"], t)
-        weighed = tile("weighed2", [P, HALF], F32, "x_bf_late1")
-        summed = add_state(2, 0, HALF)
-        for c in "ab":
-            part = slice(*CHUNKS[c])
-            nc.gpsimd.tensor_tensor(weighed[:, part], summed[:, part], weight[:, part], MULT)
-        held[2] = tile("held2_c", [P, J], F32, "x_raw_d1")[:]
+        summed = tile("summed2_0", [P, HALF], F32, "x_raw_d1")
+        nc.vector.tensor_tensor(summed[:], state[2][:].indirect(entries(0, HALF)), act2_early[:, :HALF], ADD)
         gather(2, HALF, J)
-        scatter(2, 0, FIRST, weighed[:, :FIRST])
-        gather(3, 0, J)
-        scatter(2, FIRST, HALF, weighed[:, FIRST:])
-        for t in range(3):
-            update(t, HALF, J)
-        update(3, 0, J)
-        unit = tile("unit", [P, 2], F32, "weight")
-        nc.gpsimd.memset(unit[:, 0:1], 1.0)
-        nc.gpsimd.memset(unit[:, 1:2], 0.0)
+        held[3] = tile("held3_late", [P, J], F32, "act2_early")[:]
+        gather(3, HALF, J)
+        nc.gpsimd.tensor_tensor(act[2][:, :HALF], summed[:], weight[:, :HALF], MULT)
+        scatter(2, 0, HALF)
+        for t in range(PACK):
+            update(t, HALF, J, "x_raw_d1")
+        unit = tile("unit", [P, 1], F32, "weight")
+        nc.gpsimd.memset(unit[:], 1.0)
         for t in range(3):
             scatter(t, HALF, J)
             finish_row_set(t)

@@ -90,7 +90,7 @@ def tile_list_tgn_rnnP_kernel(
         x_codes = [tile("x_codes%d" % a, [P, J], U32) for a in range(PASSES)]
         x_scale = [tile("x_scale%d" % a, [P, J], U8) for a in range(PASSES)]
         state = [tile("state%d" % t, [P, T], F32) for t in range(PACK)]
-        page = {0: tile("page0", [P, T], F32)}
+        page = {t: tile("page%d" % t, [P, T], F32) for t in range(2)}
         page[3] = page[0]
         y_bf = [tile("y_bf%d" % q, [P, PIECE, PACK], BF16) for q in range(PIECES)]
         y_codes = [tile("y_codes%d" % q, [P, PIECE], I32) for q in range(PIECES)]
@@ -121,7 +121,8 @@ def tile_list_tgn_rnnP_kernel(
         nc.gpsimd.memset(table_scale[:].bitcast(I32), 0)
         nc.gpsimd.memset(wn_scale_raw[:].bitcast(I32), 0)
         make_identity(nc, identity[:])
-        nc.vector.memset(page[0][:].bitcast(I32), 0)
+        for t in range(2):
+            nc.vector.memset(page[t][:].bitcast(I32), 0)
         for q in range(PIECES):
             nc.scalar.copy(out=pairs[q][:, 1, :], in_=page[0][:, q * PIECE : (q + 1) * PIECE].bitcast(U32))
 
@@ -168,7 +169,6 @@ def tile_list_tgn_rnnP_kernel(
             out=wn_dealt[:].bitcast(U16).rearrange("p (a t m) -> p a t m", a=PASSES, t=PACK),
             in_=wn_raw[:].bitcast(U16).rearrange("p (a m t) -> p a t m", a=PASSES, t=PACK),
         )
-        clear_page(1, "wn_raw")
         nc.vector.tensor_copy(picked_scale[:], table_scale[:].indirect(offsets[:]))
         pick_words(0)
         nc.vector.tensor_copy(

@@ -149,10 +149,10 @@ def tile_list_tgn_rnnP_kernel(
         load_state(0)
         load_x("b")
         load_state(1)
-        load_state(3)
+        load_state(2)
         nc.sync.dma_start(out=weight[:, FIRST:HALF], in_=wgo[:, FIRST:HALF])
         load_x("cd")
-        load_state(2)
+        load_state(3)
         nc.sync.dma_start(out=weight[:, HALF:], in_=wgo[:, HALF:])
 
         for m in range(SPREAD):
@@ -226,16 +226,26 @@ def tile_list_tgn_rnnP_kernel(
         def gather(t, first, last):
             nc.vector.tensor_copy(held[t][:, first:last], state[t][:].indirect(entries(first, last)))
 
-        def update(t, first, last, slot):
+        def add_state(t, first, last, slot):
             summed = tile("summed%d_%d" % (t, first), [P, last - first], F32, slot)
             nc.gpsimd.tensor_tensor(summed[:], act[t][:, first:last], held[t][:, first:last], ADD)
-            nc.gpsimd.tensor_tensor(act[t][:, first:last], summed[:], weight[:, first:last], MULT)
+            return summed
 
-        def update_first(t):
-            summed = tile("summed%d_0" % t, [P, FIRST], F32, "summed")
-            nc.vector.tensor_tensor(summed[:], state[t][:].indirect(entries(0, FIRST)), act[t][:, :FIRST], ADD)
-            gather(t, FIRST, J)
-            nc.gpsimd.tensor_tensor(act[t][:, :FIRST], summed[:], weight[:, :FIRST], MULT)
+        def weigh(engine, t, first, last, summed, after=None):
+            out = act[t][:, first:last]
+            if after:
+                out = tile("weighed%d_%d" % (t, first), [P, last - first], F32, after)[:]
+            engine.tensor_tensor(out, summed[:], weight[:, first:last], MULT)
+            return out
+
+        def gather_sum(t, first, last, values=None, after=None):
+            values = act[t][:, first:last] if values is None else values
+            summed = tile("gathered%d_%d" % (t, first), [P, last - first], F32, after)
+            nc.vector.tensor_tensor(summed[:], state[t][:].indirect(entries(first, last)), values, ADD)
+            return summed
+
+        def scatter_weighed(t, first, last, summed):
+            nc.vector.tensor_tensor(page[t][:].indirect(entries(first, last)), summed[:], weight[:, first:last], MULT)
 
         def scatter(t, first, last, values=None):
             values = act[t][:, first:last] if values is None else values
@@ -265,9 +275,7 @@ def tile_list_tgn_rnnP_kernel(
         nc.vector.quantize_mx(out=un_codes[:].bitcast(FP8X4), scales=un_scale[:], in_=un_bf[:])
 
         act = [tile("act%d" % t, [P, J], F32) for t in range(PACK)]
-        held = {t: tile("held%d" % t, [P, J], F32)[:] for t in range(PACK)}
-
-        act2_early = tile("act2_early", [P, J], F32)
+        held = {t: tile("held%d" % t, [P, J], F32)[:] for t in range(3)}
 
         def late_group(t, first, last, number, out):
             acc = bank("late%d_%d" % (t, first), number, last - first)
@@ -301,8 +309,9 @@ def tile_list_tgn_rnnP_kernel(
         for t in range(PACK):
             acc[t, "c"] = bank("second_half%d" % t, (5, 0, 1, 2)[t], HALF)
             state_pass(acc[t, "c"], t, HALF, J, start=True)
-        update_first(0)
-        scatter(0, 0, FIRST)
+        summed = gather_sum(0, 0, FIRST)
+        gather(0, HALF, J)
+        scatter_weighed(0, 0, FIRST, summed)
 
         for a in range(PASSES):
             round_x("b", a)
@@ -311,15 +320,18 @@ def tile_list_tgn_rnnP_kernel(
                 message_pass(acc[t, "b"], t, FIRST, HALF, a, stop=a == 1)
         for t in range(2):
             activate(act[t][:, FIRST:HALF], acc[t, "b"], t)
-        late_group(3, 0, HALF, 6, act[3][:, :HALF])
-        late_group(2, 0, HALF, 7, act2_early[:, :HALF])
-        update_first(1)
-        scatter(1, 0, FIRST)
-        gather(3, 0, HALF)
-        for t in range(2):
-            update(t, FIRST, HALF, "summed")
-            scatter(t, FIRST, HALF)
-        update(3, 0, HALF, "summed")
+        late_group(2, 0, HALF, 7, act[2][:, :HALF])
+        act3_early = tile("act3_early", [P, HALF], F32)
+        late_group(3, 0, HALF, 6, act3_early[:])
+        first1 = gather_sum(1, 0, FIRST)
+        gather(1, HALF, J)
+        second0 = gather_sum(0, FIRST, HALF)
+        scatter_weighed(1, 0, FIRST, first1)
+        second1 = gather_sum(1, FIRST, HALF)
+        scatter_weighed(0, FIRST, HALF, second0)
+        gather(2, HALF, J)
+        summed2 = gather_sum(2, 0, HALF)
+        scatter_weighed(1, FIRST, HALF, second1)
 
         for a in range(PASSES):
             round_x("c", a)
@@ -331,21 +343,22 @@ def tile_list_tgn_rnnP_kernel(
             message_pass(acc[t, "c"], t, HALF, J, 1)
             message_pass(acc[t, "c"], t, HALF, J, 0, stop=True)
             activate(act[t][:, HALF:], acc[t, "c"], t)
-        summed = tile("summed2_0", [P, HALF], F32, "x_raw_d1")
-        nc.vector.tensor_tensor(summed[:], state[2][:].indirect(entries(0, HALF)), act2_early[:, :HALF], ADD)
-        gather(2, HALF, J)
-        held[3] = tile("held3_late", [P, J], F32, "act2_early")[:]
+        summed3 = gather_sum(3, 0, HALF, act3_early[:], "x_raw_d1")
+        weighed2 = weigh(nc.vector, 2, 0, HALF, summed2, "act3_early")
+        held[3] = tile("held3", [P, J], F32, "x_bf_late0")[:]
         gather(3, HALF, J)
-        nc.gpsimd.tensor_tensor(act[2][:, :HALF], summed[:], weight[:, :HALF], MULT)
-        scatter(2, 0, HALF)
-        for t in range(PACK):
-            update(t, HALF, J, "x_raw_d1")
+        scatter(2, 0, HALF, weighed2)
+        for t in range(3):
+            weigh(nc.gpsimd, t, HALF, J, add_state(t, HALF, J, "state3"))
+        last = tile("weighed3", [P, J], F32, "held2")
+        nc.gpsimd.tensor_tensor(last[:, :HALF], summed3[:], weight[:, :HALF], MULT)
+        nc.gpsimd.tensor_tensor(last[:, HALF:], add_state(3, HALF, J, "state3")[:], weight[:, HALF:], MULT)
         unit = tile("unit", [P, 1], F32, "weight")
         nc.gpsimd.memset(unit[:], 1.0)
         for t in range(3):
             scatter(t, HALF, J)
             finish_row_set(t)
-        scatter(3, 0, J)
+        scatter(3, 0, J, last[:])
 
         nc.sync.dma_start(out=y_rows[3], in_=page[3][:])
         for q in SCALAR_PIECES:

@@ -221,7 +221,7 @@ def tile_list_tgn_rnnP_kernel(
                 )
 
         def activate(out, acc, t):
-            nc.scalar.activation(out=out, in_=acc[:], func=TANH, bias=bias[:, t : t + 1])
+            nc.scalar.activation(out=out, in_=acc[:, :], func=TANH, bias=bias[:, t : t + 1])
 
         def gather(t, first, last):
             nc.vector.tensor_copy(held[t][:, first:last], state[t][:].indirect(entries(first, last)))
@@ -275,14 +275,16 @@ def tile_list_tgn_rnnP_kernel(
         nc.vector.quantize_mx(out=un_codes[:].bitcast(FP8X4), scales=un_scale[:], in_=un_bf[:])
 
         act = [tile("act%d" % t, [P, J], F32) for t in range(PACK)]
-        held = {t: tile("held%d" % t, [P, J], F32)[:] for t in range(3)}
+        held = {t: tile("held%d" % t, [P, J], F32)[:] for t in range(2)}
 
         def late_group(t, first, last, number, out):
             acc = bank("late%d_%d" % (t, first), number, last - first)
             message_pass(acc, t, first, last, 1, start=True, backwards=True)
             message_pass(acc, t, first, last, 0)
             state_pass(acc, t, first, last, stop=True)
-            activate(out, acc, t)
+            for part, piece in enumerate(out):
+                size = (last - first) // len(out)
+                activate(piece, acc[:, part * size : (part + 1) * size], t)
 
         blocks = runs(0, FIRST, (P,))
         first_banks = [bank("first%d" % b, b, P) for b in range(len(blocks))]
@@ -305,7 +307,7 @@ def tile_list_tgn_rnnP_kernel(
         for bank_b, (first, last) in zip(first_banks, blocks):
             message_pass(bank_b, 0, first, last, 1, stop=True)
             activate(act[0][:, first:last], bank_b, 0)
-        late_group(1, 0, FIRST, 2, act[1][:, :FIRST])
+        late_group(1, 0, FIRST, 2, [act[1][:, :FIRST]])
         for t in range(PACK):
             acc[t, "c"] = bank("second_half%d" % t, (5, 0, 1, 2)[t], HALF)
             state_pass(acc[t, "c"], t, HALF, J, start=True)
@@ -320,16 +322,15 @@ def tile_list_tgn_rnnP_kernel(
                 message_pass(acc[t, "b"], t, FIRST, HALF, a, stop=a == 1)
         for t in range(2):
             activate(act[t][:, FIRST:HALF], acc[t, "b"], t)
-        late_group(2, 0, HALF, 7, act[2][:, :HALF])
-        act3_early = tile("act3_early", [P, HALF], F32)
-        late_group(3, 0, HALF, 6, act3_early[:])
+        late_group(2, 0, HALF, 7, [act[2][:, :HALF]])
+        act3_early = [tile("act3_early%d" % b, [P, FIRST], F32)[:] for b in range(2)]
+        late_group(3, 0, HALF, 6, act3_early)
         first1 = gather_sum(1, 0, FIRST)
         gather(1, HALF, J)
         second0 = gather_sum(0, FIRST, HALF)
         scatter_weighed(1, 0, FIRST, first1)
         second1 = gather_sum(1, FIRST, HALF)
         scatter_weighed(0, FIRST, HALF, second0)
-        gather(2, HALF, J)
         summed2 = gather_sum(2, 0, HALF)
         scatter_weighed(1, FIRST, HALF, second1)
 
@@ -343,16 +344,20 @@ def tile_list_tgn_rnnP_kernel(
             message_pass(acc[t, "c"], t, HALF, J, 1)
             message_pass(acc[t, "c"], t, HALF, J, 0, stop=True)
             activate(act[t][:, HALF:], acc[t, "c"], t)
-        summed3 = gather_sum(3, 0, HALF, act3_early[:], "x_raw_d1")
-        weighed2 = weigh(nc.vector, 2, 0, HALF, summed2, "act3_early")
-        held[3] = tile("held3", [P, J], F32, "x_bf_late0")[:]
-        gather(3, HALF, J)
+        summed3 = tile("gathered3_0", [P, HALF], F32, "x_raw_d1")
+        for b in range(2):
+            window = state[3][:].indirect(entries(b * FIRST, (b + 1) * FIRST))
+            nc.vector.tensor_tensor(summed3[:, b * FIRST : (b + 1) * FIRST], window, act3_early[b], ADD)
+        weighed2 = weigh(nc.gpsimd, 2, 0, HALF, summed2, "act3_early0")
+        for t, after in ((3, "x_bf_late1"), (2, "act3_early1")):
+            held[t] = tile("held%d" % t, [P, J], F32, after)[:]
+            gather(t, HALF, J)
         scatter(2, 0, HALF, weighed2)
         for t in range(3):
-            weigh(nc.gpsimd, t, HALF, J, add_state(t, HALF, J, "state3"))
-        last = tile("weighed3", [P, J], F32, "held2")
+            weigh(nc.gpsimd, t, HALF, J, add_state(t, HALF, J, "gathered2_0"))
+        last = tile("weighed3", [P, J], F32, "held1")
         nc.gpsimd.tensor_tensor(last[:, :HALF], summed3[:], weight[:, :HALF], MULT)
-        nc.gpsimd.tensor_tensor(last[:, HALF:], add_state(3, HALF, J, "state3")[:], weight[:, HALF:], MULT)
+        nc.gpsimd.tensor_tensor(last[:, HALF:], add_state(3, HALF, J, "act3_early1")[:], weight[:, HALF:], MULT)
         unit = tile("unit", [P, 1], F32, "weight")
         nc.gpsimd.memset(unit[:], 1.0)
         for t in range(3):

@@ -311,8 +311,9 @@ def tile_list_tgn_rnnP_kernel(
         for t in range(PACK):
             acc[t, "c"] = bank("second_half%d" % t, (5, 0, 1, 2)[t], HALF)
             state_pass(acc[t, "c"], t, HALF, J, start=True)
+        gather(0, *CHUNKS["c"])
         summed = gather_sum(0, 0, FIRST)
-        gather(0, HALF, J)
+        gather(0, *CHUNKS["d"])
         scatter_weighed(0, 0, FIRST, summed)
 
         for a in range(PASSES):
@@ -327,8 +328,8 @@ def tile_list_tgn_rnnP_kernel(
         late_group(3, 0, HALF, 6, act3_early)
         first1 = gather_sum(1, 0, FIRST)
         gather(1, HALF, J)
-        second0 = gather_sum(0, FIRST, HALF)
         scatter_weighed(1, 0, FIRST, first1)
+        second0 = gather_sum(0, FIRST, HALF)
         second1 = gather_sum(1, FIRST, HALF)
         scatter_weighed(0, FIRST, HALF, second0)
         summed2 = gather_sum(2, 0, HALF)

@@ -169,6 +169,7 @@ def tile_list_tgn_rnnP_kernel(
             out=wn_dealt[:].bitcast(U16).rearrange("p (a t m) -> p a t m", a=PASSES, t=PACK),
             in_=wn_raw[:].bitcast(U16).rearrange("p (a m t) -> p a t m", a=PASSES, t=PACK),
         )
+        clear_page(2, "wn_raw")
         nc.vector.tensor_copy(picked_scale[:], table_scale[:].indirect(offsets[:]))
         pick_words(0)
         nc.vector.tensor_copy(
@@ -303,7 +304,6 @@ def tile_list_tgn_rnnP_kernel(
         quantize_x("a", 1, (P,))
         picked[1] = tile("picked1", [P, HALF], I32, "x_raw_a1")
         pick_words(1)
-        clear_page(2, "x_bf_a1")
         for bank_b, (first, last) in zip(first_banks, blocks):
             message_pass(bank_b, 0, first, last, 1, stop=True)
             activate(act[0][:, first:last], bank_b, 0)

@@ -27,24 +27,15 @@ RUN = 4
 SCALE_ROWS = 16
 SCALE_ROW0 = 4
 HALF = J // 2
-FIRST = 256
-CHUNKS = {"a": (0, FIRST), "b": (FIRST, HALF), "c": (HALF, HALF + FIRST), "d": (HALF + FIRST, J)}
+QUARTER = J // 4
+CHUNKS = {"a": (0, QUARTER), "b": (QUARTER, HALF), "h": (HALF, J)}
 UN_SCALAR = 64
-SPREAD = FIRST // P
+SPREAD = J // P
 BANK_BLOCKS = 4
 PIECE = 512
 PIECES = T // PIECE
 VECTOR_PIECES = (2, 3)
 SCALAR_PIECES = (0, 1)
-
-
-def runs(first, last, widths):
-    out = []
-    for width in widths:
-        while last - first >= width:
-            out.append((first, first + width))
-            first = first + width
-    return out
 
 
 def tile_list_tgn_rnnP_kernel(
@@ -58,13 +49,12 @@ def tile_list_tgn_rnnP_kernel(
         def tile(name, shape, dtype, after=None):
             return sb.tile(shape, dtype, name=name, tag=after or name, align_bytes=64)
 
-        def bank(name, number, width):
-            return ps.tile([P, width], F32, name=name, tag="bank%d" % number)
+        def bank(name, number, shape):
+            return ps.tile([P] + shape, F32, name=name, tag="bank%d" % number)
 
         def width(c):
             return CHUNKS[c][1] - CHUNKS[c][0]
 
-        x_parts = [(c, a) for c in CHUNKS for a in range(PASSES)]
         offsets = tile("offsets", [P, J // GROUP], U16)
         wn_raw = tile("wn_raw", [P, PASSES * N // 2], I32)
         wn_dealt = tile("wn_dealt", [P, PASSES * N // 2], I32)
@@ -75,20 +65,15 @@ def tile_list_tgn_rnnP_kernel(
         picked = {0: tile("picked0", [P, HALF], I32)}
         picked_scale = tile("picked_scale", [P, J], U8)
         un_raw = tile("un_raw", [P, PACK, N], F32)
+        un_bf = tile("un_bf", [P, PACK * N], BF16)
         un_codes = tile("un_codes", [P, N], U32)
         un_scale = tile("un_scale", [P, N], U8)
         bias = tile("bias", [P, PACK], F32)
         weight = tile("weight", [P, J], F32)
         weight_row = tile("weight_row", [P, SPREAD], F32)
         identity = tile("identity", [P, P], F32)
-        x_raw = {(c, a): tile("x_raw_%s%d" % (c, a), [P, PACK, width(c)], F32) for c, a in x_parts}
-        x_bf = {(c, a): tile("x_bf_%s%d" % (c, a), [P, FIRST * PACK], BF16)[:] for c in "ab" for a in range(PASSES)}
-        x_bf_late = [tile("x_bf_late%d" % a, [P, HALF * PACK], BF16) for a in range(PASSES)]
-        for a in range(PASSES):
-            x_bf["c", a] = x_bf_late[a][:, : FIRST * PACK]
-            x_bf["d", a] = x_bf_late[a][:, FIRST * PACK :]
-        x_codes = [tile("x_codes%d" % a, [P, J], U32) for a in range(PASSES)]
-        x_scale = [tile("x_scale%d" % a, [P, J], U8) for a in range(PASSES)]
+        x_raw = {(c, a): tile("x_raw_%s%d" % (c, a), [P, PACK, width(c)], F32) for c in CHUNKS for a in range(PASSES)}
+        x_bf, x_codes, x_scale = {}, {}, {}
         state = [tile("state%d" % t, [P, T], F32) for t in range(PACK)]
         page = {t: tile("page%d" % t, [P, T], F32) for t in range(2)}
         page[3] = page[0]
@@ -96,7 +81,6 @@ def tile_list_tgn_rnnP_kernel(
         y_codes = [tile("y_codes%d" % q, [P, PIECE], I32) for q in range(PIECES)]
         pairs = [tile("pairs%d" % q, [P, 2, PIECE], U32) for q in range(PIECES)]
         y_scale = tile("y_scale", [P, T], U8)
-        spread = ps.tile([P, SPREAD, P], F32, name="spread", tag="bank7")
 
         x_rows = x.rearrange("(a p i) j -> a p i j", a=PASSES, i=PACK)
         h_rows = hT.rearrange("(p t) c -> t p c", t=PACK)
@@ -113,10 +97,9 @@ def tile_list_tgn_rnnP_kernel(
         def load_state(t):
             nc.sync.dma_start(out=state[t][:], in_=h_rows[t])
 
-        def load_x(chunks):
+        def load_x(c):
             for a in range(PASSES):
-                for c in chunks:
-                    nc.sync.dma_start(out=x_raw[c, a][:], in_=x_rows[a][:, :, CHUNKS[c][0] : CHUNKS[c][1]])
+                nc.sync.dma_start(out=x_raw[c, a][:], in_=x_rows[a][:, :, CHUNKS[c][0] : CHUNKS[c][1]])
 
         nc.gpsimd.memset(table_scale[:].bitcast(I32), 0)
         nc.gpsimd.memset(wn_scale_raw[:].bitcast(I32), 0)
@@ -137,7 +120,7 @@ def tile_list_tgn_rnnP_kernel(
                 in_=tab_scales.bitcast(I32)[0, r:SCALE_ROWS:RUN, :],
             )
         nc.sync.dma_start(out=table[:], in_=tab_words[0].rearrange("p t i -> p (t i)").bitcast(I32))
-        nc.sync.dma_start(out=weight_row[:], in_=wgo[0, :FIRST].rearrange("(r m) -> r m", m=SPREAD))
+        nc.sync.dma_start(out=weight_row[:], in_=wgo[0, :].rearrange("(r m) -> r m", m=SPREAD))
         for r in range(RUN):
             nc.sync.dma_start(
                 out=wn_scale_raw[r:P:QUADRANT, :].bitcast(I32).rearrange("r (a w) -> r a w", a=PASSES),
@@ -147,29 +130,29 @@ def tile_list_tgn_rnnP_kernel(
         load_x("a")
         nc.sync.dma_start(out=bias[:], in_=bn.rearrange("(p t) -> p t", t=PACK))
         load_state(0)
-        load_x("b")
         load_state(1)
+        load_x("b")
         load_state(2)
-        nc.sync.dma_start(out=weight[:, FIRST:HALF], in_=wgo[:, FIRST:HALF])
-        load_x("cd")
+        load_x("h")
         load_state(3)
-        nc.sync.dma_start(out=weight[:, HALF:], in_=wgo[:, HALF:])
 
-        for m in range(SPREAD):
-            nc.tensor.transpose(spread[:, m, :], weight_row[:, m : m + 1].to_broadcast([P, P]), identity[:])
-        nc.scalar.copy(
-            out=weight[:, :FIRST].rearrange("p (r m) -> p r m", m=SPREAD), in_=spread[:].rearrange("p m r -> p r m")
-        )
-
-        def clear_page(t, after):
-            page[t] = tile("page%d" % t, [P, T], F32, after)
-            nc.gpsimd.memset(page[t][:].bitcast(I32), 0)
+        weight_view = weight[:].rearrange("p (r m) -> p r m", m=SPREAD)
+        for half in range(SPREAD // BANK_BLOCKS):
+            spread = bank("spread%d" % half, 4 + half, [BANK_BLOCKS, P])
+            for m in range(BANK_BLOCKS):
+                column = half * BANK_BLOCKS + m
+                nc.tensor.transpose(spread[:, m, :], weight_row[:, column : column + 1].to_broadcast([P, P]), identity[:])
+            nc.scalar.copy(
+                out=weight_view[:, :, half * BANK_BLOCKS : (half + 1) * BANK_BLOCKS],
+                in_=spread[:].rearrange("p m r -> p r m"),
+            )
 
         nc.vector.tensor_copy(
             out=wn_dealt[:].bitcast(U16).rearrange("p (a t m) -> p a t m", a=PASSES, t=PACK),
             in_=wn_raw[:].bitcast(U16).rearrange("p (a m t) -> p a t m", a=PASSES, t=PACK),
         )
-        clear_page(2, "wn_raw")
+        page[2] = tile("page2", [P, T], F32, "wn_raw")
+        nc.gpsimd.memset(page[2][:].bitcast(I32), 0)
         nc.vector.tensor_copy(picked_scale[:], table_scale[:].indirect(offsets[:]))
         pick_words(0)
         nc.vector.tensor_copy(
@@ -184,72 +167,47 @@ def tile_list_tgn_rnnP_kernel(
                 in_=x_raw[c, a][:, :, first:last].rearrange("p i (g e) -> p g i e", e=2),
             )
 
-        def quantize_x(c, a, widths=(256,)):
-            base = CHUNKS[c][0]
-            for first, last in runs(0, width(c), widths):
-                nc.vector.quantize_mx(
-                    out=x_codes[a][:, base + first : base + last].bitcast(FP8X4),
-                    scales=x_scale[a][:, base + first : base + last],
-                    in_=x_bf[c, a][:, first * PACK : last * PACK],
-                )
+        def quantize(codes, scales, values):
+            nc.vector.quantize_mx(out=codes.bitcast(FP8X4), scales=scales, in_=values)
 
-        def message_pass(acc, t, first, last, a, start=False, stop=False, backwards=False):
+        def message_pass(acc, t, c, a, blocks, start=False, stop=False, base=0):
             column = (a * PACK + t) * P
-            parts = runs(first, last, (512, 128))
-            if backwards:
-                parts = parts[::-1]
-            for j0, j1 in parts:
+            for first, last in blocks:
                 nc.tensor.matmul_mx(
-                    out=acc[:, j0 - first : j1 - first],
+                    out=acc[:, first - base : last - base],
                     lhsT=wn_dealt[:].bitcast(U8)[:, 2 * column : 2 * (column + P)].bitcast(FP4X4),
                     lhsT_scale=wn_scale[:, column : column + P],
-                    rhs=x_codes[a][:, j0:j1].bitcast(FP8X4),
-                    rhs_scale=x_scale[a][:, j0:j1],
-                    start=start and (j0, j1) == parts[0],
-                    stop=stop and (j0, j1) == parts[-1],
+                    rhs=x_codes[c, a][:, first:last].bitcast(FP8X4),
+                    rhs_scale=x_scale[c, a][:, first:last],
+                    start=start and (first, last) == blocks[0],
+                    stop=stop and (first, last) == blocks[-1],
                 )
 
         def state_pass(acc, t, first, last, start=False, stop=False):
-            for j0, j1 in runs(first, last, (512, 256, 128)):
-                nc.tensor.matmul_mx(
-                    out=acc[:, j0 - first : j1 - first],
-                    lhsT=un_codes[:, t * P : (t + 1) * P].bitcast(FP8X4),
-                    lhsT_scale=un_scale[:, t * P : (t + 1) * P],
-                    rhs=picked[j0 // HALF][:, j0 % HALF : j0 % HALF + j1 - j0].bitcast(FP8X4),
-                    rhs_scale=picked_scale[SCALE_ROW0:P, j0:j1],
-                    start=start and j0 == first,
-                    stop=stop and j1 == last,
-                )
+            h = first // HALF
+            nc.tensor.matmul_mx(
+                out=acc,
+                lhsT=un_codes[:, t * P : (t + 1) * P].bitcast(FP8X4),
+                lhsT_scale=un_scale[:, t * P : (t + 1) * P],
+                rhs=picked[h][:, first - h * HALF : last - h * HALF].bitcast(FP8X4),
+                rhs_scale=picked_scale[SCALE_ROW0:P, first:last],
+                start=start,
+                stop=stop,
+            )
 
         def activate(out, acc, t):
-            nc.scalar.activation(out=out, in_=acc[:, :], func=TANH, bias=bias[:, t : t + 1])
+            nc.scalar.activation(out=out, in_=acc, func=TANH, bias=bias[:, t : t + 1])
 
-        def gather(t, first, last):
-            nc.vector.tensor_copy(held[t][:, first:last], state[t][:].indirect(entries(first, last)))
+        def gather(out, t, first, last):
+            nc.vector.tensor_copy(out, state[t][:].indirect(entries(first, last)))
 
-        def add_state(t, first, last, slot):
-            summed = tile("summed%d_%d" % (t, first), [P, last - first], F32, slot)
-            nc.gpsimd.tensor_tensor(summed[:], act[t][:, first:last], held[t][:, first:last], ADD)
-            return summed
-
-        def weigh(engine, t, first, last, summed, after=None):
-            out = act[t][:, first:last]
-            if after:
-                out = tile("weighed%d_%d" % (t, first), [P, last - first], F32, after)[:]
-            engine.tensor_tensor(out, summed[:], weight[:, first:last], MULT)
-            return out
-
-        def gather_sum(t, first, last, values=None, after=None):
-            values = act[t][:, first:last] if values is None else values
-            summed = tile("gathered%d_%d" % (t, first), [P, last - first], F32, after)
-            nc.vector.tensor_tensor(summed[:], state[t][:].indirect(entries(first, last)), values, ADD)
-            return summed
+        def gather_sum(out, t, first, last, values):
+            nc.vector.tensor_tensor(out, state[t][:].indirect(entries(first, last)), values, ADD)
 
         def scatter_weighed(t, first, last, summed):
-            nc.vector.tensor_tensor(page[t][:].indirect(entries(first, last)), summed[:], weight[:, first:last], MULT)
+            nc.vector.tensor_tensor(page[t][:].indirect(entries(first, last)), summed, weight[:, first:last], MULT)
 
-        def scatter(t, first, last, values=None):
-            values = act[t][:, first:last] if values is None else values
+        def scatter(t, first, last, values):
             nc.vector.tensor_copy(page[t][:].indirect(entries(first, last)), values)
 
         def interleave(engine_copy, t, q):
@@ -268,101 +226,162 @@ def tile_list_tgn_rnnP_kernel(
                     nc.scalar.copy(out=words, in_=pairs[q][:].rearrange("p u c -> p c u"))
 
         un_view = un_raw[:].rearrange("p i (m t) -> p m i t", t=PACK)
-
-        un_bf = tile("un_bf", [P, PACK * N], BF16)
         un_dealt = un_bf[:].rearrange("p (t m i) -> p m i t", t=PACK, i=PACK)
         nc.scalar.copy(out=un_dealt[:, :UN_SCALAR], in_=un_view[:, :UN_SCALAR])
         nc.vector.tensor_copy(out=un_dealt[:, UN_SCALAR:], in_=un_view[:, UN_SCALAR:])
-        nc.vector.quantize_mx(out=un_codes[:].bitcast(FP8X4), scales=un_scale[:], in_=un_bf[:])
+        quantize(un_codes[:], un_scale[:], un_bf[:])
 
-        act = [tile("act%d" % t, [P, J], F32) for t in range(PACK)]
-        held = {t: tile("held%d" % t, [P, J], F32)[:] for t in range(2)}
-
-        def late_group(t, first, last, number, out):
-            acc = bank("late%d_%d" % (t, first), number, last - first)
-            message_pass(acc, t, first, last, 1, start=True, backwards=True)
-            message_pass(acc, t, first, last, 0)
-            state_pass(acc, t, first, last, stop=True)
-            for part, piece in enumerate(out):
-                size = (last - first) // len(out)
-                activate(piece, acc[:, part * size : (part + 1) * size], t)
-
-        blocks = runs(0, FIRST, (P,))
-        first_banks = [bank("first%d" % b, b, P) for b in range(len(blocks))]
-        acc = {(t, "b"): bank("early%d" % t, 3 + t, FIRST) for t in range(2)}
-        for bank_b, block in zip(first_banks, blocks):
-            state_pass(bank_b, 0, *block, start=True)
+        blocks = [(0, P), (P, QUARTER)]
+        whole = [(0, HALF)]
+        first_banks = [bank("first%d" % b, b, [P]) for b in range(len(blocks))]
+        acc_b = [bank("chunk_b%d" % t, 4 + t, [QUARTER]) for t in range(3)]
+        acc3 = bank("first_half3", 7, [HALF])
+        for acc, block in zip(first_banks, blocks):
+            state_pass(acc[:], 0, *block, start=True)
         for t in range(2):
-            state_pass(acc[t, "b"], t, FIRST, HALF, start=True)
+            state_pass(acc_b[t][:], t, QUARTER, HALF, start=True)
+        state_pass(acc3[:], 3, 0, HALF, start=True)
+
+        for a in range(PASSES):
+            x_bf["a", a] = tile("x_bf_a%d" % a, [P, QUARTER * PACK], BF16)[:]
+            x_codes["a", a] = tile("x_codes_a%d" % a, [P, QUARTER], U32)[:]
+            x_scale["a", a] = tile("x_scale_a%d" % a, [P, QUARTER], U8)[:]
         round_x("a", 0, nc.vector.tensor_copy, 0, P)
-        round_x("a", 0, nc.scalar.copy, P, FIRST)
-        quantize_x("a", 0)
-        for bank_b, block in zip(first_banks, blocks):
-            message_pass(bank_b, 0, *block, 0)
+        round_x("a", 0, nc.scalar.copy, P, QUARTER)
+        quantize(x_codes["a", 0], x_scale["a", 0], x_bf["a", 0])
         round_x("a", 1, nc.vector.tensor_copy, 0, P)
-        round_x("a", 1, nc.scalar.copy, P, FIRST)
-        quantize_x("a", 1, (P,))
+        round_x("a", 1, nc.scalar.copy, P, QUARTER)
+        for first, last in blocks:
+            values = x_bf["a", 1][:, first * PACK : last * PACK]
+            quantize(x_codes["a", 1][:, first:last], x_scale["a", 1][:, first:last], values)
         picked[1] = tile("picked1", [P, HALF], I32, "x_raw_a1")
         pick_words(1)
-        for bank_b, (first, last) in zip(first_banks, blocks):
-            message_pass(bank_b, 0, first, last, 1, stop=True)
-            activate(act[0][:, first:last], bank_b, 0)
-        late_group(1, 0, FIRST, 2, [act[1][:, :FIRST]])
-        for t in range(PACK):
-            acc[t, "c"] = bank("second_half%d" % t, (5, 0, 1, 2)[t], HALF)
-            state_pass(acc[t, "c"], t, HALF, J, start=True)
-        gather(0, *CHUNKS["c"])
-        summed = gather_sum(0, 0, FIRST)
-        gather(0, *CHUNKS["d"])
-        scatter_weighed(0, 0, FIRST, summed)
 
+        act_a = [tile("act_a%d" % t, [P, QUARTER], F32) for t in range(3)]
         for a in range(PASSES):
-            round_x("b", a)
-            quantize_x("b", a)
-            for t in range(2):
-                message_pass(acc[t, "b"], t, FIRST, HALF, a, stop=a == 1)
-        for t in range(2):
-            activate(act[t][:, FIRST:HALF], acc[t, "b"], t)
-        late_group(2, 0, HALF, 7, [act[2][:, :HALF]])
-        act3_early = [tile("act3_early%d" % b, [P, FIRST], F32)[:] for b in range(2)]
-        late_group(3, 0, HALF, 6, act3_early)
-        first1 = gather_sum(1, 0, FIRST)
-        gather(1, HALF, J)
-        scatter_weighed(1, 0, FIRST, first1)
-        second0 = gather_sum(0, FIRST, HALF)
-        second1 = gather_sum(1, FIRST, HALF)
-        scatter_weighed(0, FIRST, HALF, second0)
-        summed2 = gather_sum(2, 0, HALF)
-        scatter_weighed(1, FIRST, HALF, second1)
-
-        for a in range(PASSES):
-            round_x("c", a)
-            round_x("d", a)
-            nc.vector.quantize_mx(out=x_codes[a][:, HALF:].bitcast(FP8X4), scales=x_scale[a][:, HALF:], in_=x_bf_late[a][:])
-            message_pass(acc[0, "c"], 0, HALF, J, a, stop=a == 1)
-        activate(act[0][:, HALF:], acc[0, "c"], 0)
-        for t in range(1, PACK):
-            message_pass(acc[t, "c"], t, HALF, J, 1)
-            message_pass(acc[t, "c"], t, HALF, J, 0, stop=True)
-            activate(act[t][:, HALF:], acc[t, "c"], t)
-        summed3 = tile("gathered3_0", [P, HALF], F32, "x_raw_d1")
+            for acc, (first, last) in zip(first_banks, blocks):
+                nc.tensor.matmul_mx(
+                    out=acc[:],
+                    lhsT=wn_dealt[:].bitcast(U8)[:, 2 * a * PACK * P : 2 * (a * PACK + 1) * P].bitcast(FP4X4),
+                    lhsT_scale=wn_scale[:, a * PACK * P : (a * PACK + 1) * P],
+                    rhs=x_codes["a", a][:, first:last].bitcast(FP8X4),
+                    rhs_scale=x_scale["a", a][:, first:last],
+                    start=False,
+                    stop=a == PASSES - 1,
+                )
+                if a == PASSES - 1:
+                    activate(act_a[0][:, first:last], acc[:], 0)
+        for t in (1, 2):
+            acc = bank("chunk_a%d" % t, 1 + t, [QUARTER])
+            message_pass(acc, t, "a", 1, blocks[::-1], start=True)
+            message_pass(acc, t, "a", 0, blocks)
+            state_pass(acc[:], t, 0, QUARTER, stop=True)
+            activate(act_a[t][:], acc[:], t)
+        acc_h0 = [bank("second_half0_%d" % b, b, [QUARTER]) for b in range(2)]
         for b in range(2):
-            window = state[3][:].indirect(entries(b * FIRST, (b + 1) * FIRST))
-            nc.vector.tensor_tensor(summed3[:, b * FIRST : (b + 1) * FIRST], window, act3_early[b], ADD)
-        weighed2 = weigh(nc.gpsimd, 2, 0, HALF, summed2, "act3_early0")
-        for t, after in ((3, "x_bf_late1"), (2, "act3_early1")):
-            held[t] = tile("held%d" % t, [P, J], F32, after)[:]
-            gather(t, HALF, J)
-        scatter(2, 0, HALF, weighed2)
+            state_pass(acc_h0[b][:], 0, HALF + b * QUARTER, HALF + (b + 1) * QUARTER, start=True)
+        acc_h = {t: bank("second_half%d" % t, 1 + t, [HALF]) for t in (1, 2)}
+        for t in (1, 2):
+            state_pass(acc_h[t][:], t, HALF, J, start=True)
+        message_pass(acc3, 3, "a", 1, blocks[::-1])
+        message_pass(acc3, 3, "a", 0, blocks)
+
+        held = {0: tile("held0", [P, HALF], F32)}
+        sum_a = [tile("sum_a%d" % t, [P, QUARTER], F32) for t in range(2)]
+        gather(held[0][:, :QUARTER], 0, HALF, HALF + QUARTER)
+        gather_sum(sum_a[0][:], 0, 0, QUARTER, act_a[0][:])
+        gather(held[0][:, QUARTER:], 0, HALF + QUARTER, J)
+        scatter_weighed(0, 0, QUARTER, sum_a[0][:])
+        held[1] = tile("held1", [P, HALF], F32, "act_a0")
+        gather_sum(sum_a[1][:], 1, 0, QUARTER, act_a[1][:])
+        gather(held[1][:, :QUARTER], 1, HALF, HALF + QUARTER)
+        scatter_weighed(1, 0, QUARTER, sum_a[1][:])
+        gather(held[1][:, QUARTER:], 1, HALF + QUARTER, J)
+
+        b_bf = tile("x_bf_b", [P, PASSES * QUARTER * PACK], BF16, "act_a1")
+        b_codes = tile("x_codes_b", [P, PASSES * QUARTER], U32)
+        b_scale = tile("x_scale_b", [P, PASSES * QUARTER], U8)
+        for a in range(PASSES):
+            x_bf["b", a] = b_bf[:, a * QUARTER * PACK : (a + 1) * QUARTER * PACK]
+            x_codes["b", a] = b_codes[:, a * QUARTER : (a + 1) * QUARTER]
+            x_scale["b", a] = b_scale[:, a * QUARTER : (a + 1) * QUARTER]
+            round_x("b", a)
+        quantize(b_codes[:], b_scale[:], b_bf[:])
+        early2 = tile("early2", [P, QUARTER + P], F32, "x_raw_b1")
+        gather_sum(early2[:, :QUARTER], 2, 0, QUARTER, act_a[2][:])
+        gather(early2[:, QUARTER:], 2, HALF, HALF + P)
+        scatter_weighed(2, 0, QUARTER, early2[:, :QUARTER])
+
+        act_b = tile("act_b", [P, 3 * QUARTER], F32, "act_a2")
         for t in range(3):
-            weigh(nc.gpsimd, t, HALF, J, add_state(t, HALF, J, "gathered2_0"))
-        last = tile("weighed3", [P, J], F32, "held1")
-        nc.gpsimd.tensor_tensor(last[:, :HALF], summed3[:], weight[:, :HALF], MULT)
-        nc.gpsimd.tensor_tensor(last[:, HALF:], add_state(3, HALF, J, "act3_early1")[:], weight[:, HALF:], MULT)
+            for a in range(PASSES):
+                message_pass(acc_b[t], t, "b", a, blocks, start=t == 2 and a == 0, stop=t < 2 and a == PASSES - 1)
+            if t == 2:
+                state_pass(acc_b[t][:], t, QUARTER, HALF, stop=True)
+            activate(act_b[:, t * QUARTER : (t + 1) * QUARTER], acc_b[t][:], t)
+        for a in range(PASSES):
+            message_pass(acc3[:, QUARTER:], 3, "b", a, blocks, stop=a == PASSES - 1)
+        sum_b = [tile("sum_b%d" % t, [P, QUARTER], F32) for t in range(3)]
+        for t in range(2):
+            gather_sum(sum_b[t][:], t, QUARTER, HALF, act_b[:, t * QUARTER : (t + 1) * QUARTER])
+        scatter_weighed(0, QUARTER, HALF, sum_b[0][:])
+        gather_sum(sum_b[2][:], 2, QUARTER, HALF, act_b[:, 2 * QUARTER :])
+        scatter_weighed(1, QUARTER, HALF, sum_b[1][:])
+
+        h_bf = tile("x_bf_h", [P, PASSES * HALF * PACK], BF16, "picked0")
+        act_h = [tile("act_h%d" % t, [P, HALF], F32) for t in range(PACK)]
+        acc_h[3] = bank("second_half3", 4, [HALF])
+        state_pass(acc_h[3][:], 3, HALF, J, start=True)
+        for a in range(PASSES):
+            x_bf["h", a] = h_bf[:, a * HALF * PACK : (a + 1) * HALF * PACK]
+            x_codes["h", a] = tile("x_codes_h%d" % a, [P, HALF], U32, "act_a2" if a == 0 else None)[:]
+            x_scale["h", a] = tile("x_scale_h%d" % a, [P, HALF], U8)[:]
+            round_x("h", a)
+            for first, last in whole if a == 0 else [(0, QUARTER), (QUARTER, HALF)]:
+                values = x_bf["h", a][:, first * PACK : last * PACK]
+                quantize(x_codes["h", a][:, first:last], x_scale["h", a][:, first:last], values)
+            for b in range(2):
+                shifted = [(first + b * QUARTER, last + b * QUARTER) for first, last in blocks]
+                message_pass(acc_h0[b], 0, "h", a, shifted, stop=a == PASSES - 1, base=b * QUARTER)
+        act3 = [tile("act3_%d" % b, [P, QUARTER], F32) for b in range(2)]
+        for b in range(2):
+            activate(act3[b][:], acc3[:, b * QUARTER : (b + 1) * QUARTER], 3)
+        for b in range(2):
+            activate(act_h[0][:, b * QUARTER : (b + 1) * QUARTER], acc_h0[b][:], 0)
+        for t in range(1, PACK):
+            message_pass(acc_h[t], t, "h", 1, whole)
+            message_pass(acc_h[t], t, "h", 0, whole, stop=True)
+            activate(act_h[t][:], acc_h[t][:], t)
+
+        sum3 = tile("sum3", [P, HALF], F32, "x_raw_h1")
+        for b in range(2):
+            part = slice(b * QUARTER, (b + 1) * QUARTER)
+            gather_sum(sum3[:, part], 3, part.start, part.stop, act3[b][:])
+        weighed2 = tile("weighed2", [P, QUARTER], F32, "act3_0")
+        nc.gpsimd.tensor_tensor(weighed2[:], sum_b[2][:], weight[:, QUARTER:HALF], MULT)
+        held[3] = tile("held3", [P, HALF], F32, "picked0")
+        gather(held[3][:], 3, HALF, J)
+        held[2] = tile("held2", [P, HALF - P], F32, "act3_1")
+        gather(held[2][:], 2, HALF + P, J)
+        scatter(2, QUARTER, HALF, weighed2[:])
+
+        for t in range(3):
+            summed = tile("sum_h%d" % t, [P, HALF], F32, ("sum_b2", "held0", "act_a0")[t])
+            if t < 2:
+                nc.gpsimd.tensor_tensor(summed[:], act_h[t][:], held[t][:], ADD)
+            else:
+                nc.gpsimd.tensor_tensor(summed[:, :P], act_h[t][:, :P], early2[:, QUARTER:], ADD)
+                nc.gpsimd.tensor_tensor(summed[:, P:], act_h[t][:, P:], held[t][:], ADD)
+            nc.gpsimd.tensor_tensor(act_h[t][:], summed[:], weight[:, HALF:], MULT)
+        summed = tile("sum_h3", [P, HALF], F32, "act3_1")
+        nc.gpsimd.tensor_tensor(summed[:], act_h[3][:], held[3][:], ADD)
+        last = tile("weighed3", [P, J], F32, "picked0")
+        nc.gpsimd.tensor_tensor(last[:, :HALF], sum3[:], weight[:, :HALF], MULT)
+        nc.gpsimd.tensor_tensor(last[:, HALF:], summed[:], weight[:, HALF:], MULT)
         unit = tile("unit", [P, 1], F32, "weight")
         nc.gpsimd.memset(unit[:], 1.0)
         for t in range(3):
-            scatter(t, HALF, J)
+            scatter(t, HALF, J, act_h[t][:])
             finish_row_set(t)
         scatter(3, 0, J, last[:])
 
@@ -372,11 +391,7 @@ def tile_list_tgn_rnnP_kernel(
         for q in VECTOR_PIECES:
             interleave(nc.vector.tensor_copy, 3, q)
         for q in VECTOR_PIECES + SCALAR_PIECES:
-            nc.vector.quantize_mx(
-                out=y_codes[q][:].bitcast(FP8X4),
-                scales=y_scale[:, q * PIECE : (q + 1) * PIECE],
-                in_=y_bf[q][:].rearrange("p c i -> p (c i)"),
-            )
+            quantize(y_codes[q][:], y_scale[:, q * PIECE : (q + 1) * PIECE], y_bf[q][:].rearrange("p c i -> p (c i)"))
             nc.sync.dma_start(out=y_words[:, q * PIECE : (q + 1) * PIECE], in_=y_codes[q][:])
         for r in range(RUN):
             nc.scalar.dma_start(

@@ -28,7 +28,7 @@ SCALE_ROWS = 16
 SCALE_ROW0 = 4
 HALF = J // 2
 QUARTER = J // 4
-CHUNKS = {"a": (0, QUARTER), "b": (QUARTER, HALF), "h": (HALF, J)}
+CHUNKS = {"a": (0, QUARTER), "b": (QUARTER, HALF), "c": (HALF, HALF + QUARTER), "d": (HALF + QUARTER, J)}
 UN_SCALAR = 64
 SPREAD = J // P
 BANK_BLOCKS = 4
@@ -97,9 +97,10 @@ def tile_list_tgn_rnnP_kernel(
         def load_state(t):
             nc.sync.dma_start(out=state[t][:], in_=h_rows[t])
 
-        def load_x(c):
+        def load_x(chunks):
             for a in range(PASSES):
-                nc.sync.dma_start(out=x_raw[c, a][:], in_=x_rows[a][:, :, CHUNKS[c][0] : CHUNKS[c][1]])
+                for c in chunks:
+                    nc.sync.dma_start(out=x_raw[c, a][:], in_=x_rows[a][:, :, CHUNKS[c][0] : CHUNKS[c][1]])
 
         nc.gpsimd.memset(table_scale[:].bitcast(I32), 0)
         nc.gpsimd.memset(wn_scale_raw[:].bitcast(I32), 0)
@@ -133,7 +134,7 @@ def tile_list_tgn_rnnP_kernel(
         load_state(1)
         load_x("b")
         load_state(2)
-        load_x("h")
+        load_x("cd")
         load_state(3)
 
         weight_view = weight[:].rearrange("p (r m) -> p r m", m=SPREAD)
@@ -238,7 +239,7 @@ def tile_list_tgn_rnnP_kernel(
         acc3 = bank("first_half3", 7, [HALF])
         for acc, block in zip(first_banks, blocks):
             state_pass(acc[:], 0, *block, start=True)
-        for t in range(2):
+        for t in (0, 2):
             state_pass(acc_b[t][:], t, QUARTER, HALF, start=True)
         state_pass(acc3[:], 3, 0, HALF, start=True)
 
@@ -315,8 +316,8 @@ def tile_list_tgn_rnnP_kernel(
         act_b = tile("act_b", [P, 3 * QUARTER], F32, "act_a2")
         for t in range(3):
             for a in range(PASSES):
-                message_pass(acc_b[t], t, "b", a, blocks, start=t == 2 and a == 0, stop=t < 2 and a == PASSES - 1)
-            if t == 2:
+                message_pass(acc_b[t], t, "b", a, blocks, start=t == 1 and a == 0, stop=t != 1 and a == PASSES - 1)
+            if t == 1:
                 state_pass(acc_b[t][:], t, QUARTER, HALF, stop=True)
             activate(act_b[:, t * QUARTER : (t + 1) * QUARTER], acc_b[t][:], t)
         for a in range(PASSES):
@@ -334,9 +335,11 @@ def tile_list_tgn_rnnP_kernel(
         state_pass(acc_h[3][:], 3, HALF, J, start=True)
         for a in range(PASSES):
             x_bf["h", a] = h_bf[:, a * HALF * PACK : (a + 1) * HALF * PACK]
+            x_bf["c", a], x_bf["d", a] = x_bf["h", a][:, : QUARTER * PACK], x_bf["h", a][:, QUARTER * PACK :]
             x_codes["h", a] = tile("x_codes_h%d" % a, [P, HALF], U32, "act_a2" if a == 0 else None)[:]
             x_scale["h", a] = tile("x_scale_h%d" % a, [P, HALF], U8)[:]
-            round_x("h", a)
+            round_x("c", a)
+            round_x("d", a)
             for first, last in whole if a == 0 else [(0, QUARTER), (QUARTER, HALF)]:
                 values = x_bf["h", a][:, first * PACK : last * PACK]
                 quantize(x_codes["h", a][:, first:last], x_scale["h", a][:, first:last], values)
@@ -353,7 +356,7 @@ def tile_list_tgn_rnnP_kernel(
             message_pass(acc_h[t], t, "h", 0, whole, stop=True)
             activate(act_h[t][:], acc_h[t][:], t)
 
-        sum3 = tile("sum3", [P, HALF], F32, "x_raw_h1")
+        sum3 = tile("sum3", [P, HALF], F32, "x_raw_d1")
         for b in range(2):
             part = slice(b * QUARTER, (b + 1) * QUARTER)
             gather_sum(sum3[:, part], 3, part.start, part.stop, act3[b][:])

from contextlib import ExitStack

import concourse.mybir as mybir
from concourse.masks import make_identity

K, M, N, T, J = 1024, 512, 512, 2048, 1024
FLOPS = 2 * (K + M) * N * J

F32 = mybir.dt.float32
BF16 = mybir.dt.bfloat16
I32 = mybir.dt.int32
U32 = mybir.dt.uint32
U16 = mybir.dt.uint16
U8 = mybir.dt.uint8
FP8X4 = mybir.dt.float8_e4m3fn_x4
FP4X4 = mybir.dt.float4_e2m1fn_x4
ADD = mybir.AluOpType.add
MULT = mybir.AluOpType.mult
TANH = mybir.ActivationFunctionType.Tanh

P = 128
PACK = 4
PASSES = K // (P * PACK)
GROUP = 16
QUADRANT = 32
RUN = 4
SCALE_ROWS = 16
SCALE_ROW0 = 4
HALF = J // 2
QUARTER = J // 4
CHUNKS = {"a": (0, QUARTER), "b": (QUARTER, HALF), "c": (HALF, HALF + QUARTER), "d": (HALF + QUARTER, J)}
UN_SCALAR = 64
SPREAD = J // P
BANK_BLOCKS = 4
PIECE = 512
PIECES = T // PIECE
VECTOR_PIECES = (2, 3)
SCALAR_PIECES = (0, 1)


def tile_list_tgn_rnnP_kernel(
    tc, x, tab_words, tab_scales, wn_words, wn_scales, un, bn, hT, wgo, offs, out_0, out_1, out_2
):
    nc = tc.nc
    with ExitStack() as ctx:
        sb = ctx.enter_context(tc.tile_pool(name="sb", bufs=1))
        ps = ctx.enter_context(tc.psum_pool(name="ps", bufs=1))

        def tile(name, shape, dtype, after=None):
            return sb.tile(shape, dtype, name=name, tag=after or name, align_bytes=64)

        def bank(name, number, shape):
            return ps.tile([P] + shape, F32, name=name, tag="bank%d" % number)

        def width(c):
            return CHUNKS[c][1] - CHUNKS[c][0]

        offsets = tile("offsets", [P, J // GROUP], U16)
        wn_raw = tile("wn_raw", [P, PASSES * N // 2], I32)
        wn_dealt = tile("wn_dealt", [P, PASSES * N // 2], I32)
        wn_scale_raw = tile("wn_scale_raw", [P, PASSES * N], U8)
        wn_scale = tile("wn_scale", [P, PASSES * N], U8)
        table = tile("table", [P, T], I32)
        table_scale = tile("table_scale", [P, T], U8)
        picked = {0: tile("picked0", [P, HALF], I32)}
        picked_scale = tile("picked_scale", [P, J], U8)
        un_raw = tile("un_raw", [P, PACK, N], F32)
        un_bf = tile("un_bf", [P, PACK * N], BF16)
        un_codes = tile("un_codes", [P, N], U32)
        un_scale = tile("un_scale", [P, N], U8)
        bias = tile("bias", [P, PACK], F32)
        weight = tile("weight", [P, J], F32)
        weight_row = tile("weight_row", [P, SPREAD], F32)
        identity = tile("identity", [P, P], F32)
        x_raw = {(c, a): tile("x_raw_%s%d" % (c, a), [P, PACK, width(c)], F32) for c in CHUNKS for a in range(PASSES)}
        x_bf, x_codes, x_scale = {}, {}, {}
        state = [tile("state%d" % t, [P, T], F32) for t in range(PACK)]
        page = {t: tile("page%d" % t, [P, T], F32) for t in range(2)}
        page[3] = page[0]
        y_bf = [tile("y_bf%d" % q, [P, PIECE, PACK], BF16) for q in range(PIECES)]
        y_codes = [tile("y_codes%d" % q, [P, PIECE], I32) for q in range(PIECES)]
        pairs = [tile("pairs%d" % q, [P, 2, PIECE], U32) for q in range(PIECES)]
        y_scale = tile("y_scale", [P, T], U8)

        x_rows = x.rearrange("(a p i) j -> a p i j", a=PASSES, i=PACK)
        h_rows = hT.rearrange("(p t) c -> t p c", t=PACK)
        y_rows = out_0.rearrange("(p t) c -> t p c", t=PACK)
        y_words = out_1[0].rearrange("p t i -> p (t i)").bitcast(I32)

        def entries(first, last):
            return offsets[:, first // GROUP : last // GROUP]

        def pick_words(h):
            window = table[:].bitcast(U32)
            nc.vector.tensor_copy(picked[h][:].bitcast(U32), window.indirect(entries(h * HALF, (h + 1) * HALF)))

        def load_state(t):
            nc.sync.dma_start(out=state[t][:], in_=h_rows[t])

        def load_x(chunks):
            for a in range(PASSES):
                for c in chunks:
                    nc.sync.dma_start(out=x_raw[c, a][:], in_=x_rows[a][:, :, CHUNKS[c][0] : CHUNKS[c][1]])

        nc.gpsimd.memset(table_scale[:].bitcast(I32), 0)
        nc.gpsimd.memset(wn_scale_raw[:].bitcast(I32), 0)
        make_identity(nc, identity[:])
        for t in range(2):
            nc.vector.memset(page[t][:].bitcast(I32), 0)
        for q in range(PIECES):
            nc.scalar.copy(out=pairs[q][:, 1, :], in_=page[0][:, q * PIECE : (q + 1) * PIECE].bitcast(U32))

        nc.sync.dma_start(offsets[:], offs)
        nc.sync.dma_start(
            out=wn_raw[:].rearrange("p (a w) -> p a w", a=PASSES),
            in_=wn_words.bitcast(I32).rearrange("a p w -> p a w"),
        )
        for r in range(RUN):
            nc.sync.dma_start(
                out=table_scale[SCALE_ROW0 + r : P : QUADRANT, :].bitcast(I32),
                in_=tab_scales.bitcast(I32)[0, r:SCALE_ROWS:RUN, :],
            )
        nc.sync.dma_start(out=table[:], in_=tab_words[0].rearrange("p t i -> p (t i)").bitcast(I32))
        nc.sync.dma_start(out=weight_row[:], in_=wgo[0, :].rearrange("(r m) -> r m", m=SPREAD))
        for r in range(RUN):
            nc.sync.dma_start(
                out=wn_scale_raw[r:P:QUADRANT, :].bitcast(I32).rearrange("r (a w) -> r a w", a=PASSES),
                in_=wn_scales.bitcast(I32)[:, r:SCALE_ROWS:RUN, :].rearrange("a r w -> r a w"),
            )
        nc.sync.dma_start(out=un_raw[:], in_=un.rearrange("(p i) n -> p i n", i=PACK))
        load_x("a")
        nc.sync.dma_start(out=bias[:], in_=bn.rearrange("(p t) -> p t", t=PACK))
        load_state(0)
        load_state(1)
        load_x("b")
        load_state(2)
        load_x("cd")
        load_state(3)

        weight_view = weight[:].rearrange("p (r m) -> p r m", m=SPREAD)
        for half in range(SPREAD // BANK_BLOCKS):
            spread = bank("spread%d" % half, 4 + half, [BANK_BLOCKS, P])
            for m in range(BANK_BLOCKS):
                column = half * BANK_BLOCKS + m
                nc.tensor.transpose(spread[:, m, :], weight_row[:, column : column + 1].to_broadcast([P, P]), identity[:])
            nc.scalar.copy(
                out=weight_view[:, :, half * BANK_BLOCKS : (half + 1) * BANK_BLOCKS],
                in_=spread[:].rearrange("p m r -> p r m"),
            )

        nc.vector.tensor_copy(
            out=wn_dealt[:].bitcast(U16).rearrange("p (a t m) -> p a t m", a=PASSES, t=PACK),
            in_=wn_raw[:].bitcast(U16).rearrange("p (a m t) -> p a t m", a=PASSES, t=PACK),
        )
        page[2] = tile("page2", [P, T], F32, "wn_raw")
        nc.gpsimd.memset(page[2][:].bitcast(I32), 0)
        nc.vector.tensor_copy(picked_scale[:], table_scale[:].indirect(offsets[:]))
        pick_words(0)
        nc.vector.tensor_copy(
            out=wn_scale[:].rearrange("p (a t m) -> p a t m", a=PASSES, t=PACK),
            in_=wn_scale_raw[:].rearrange("p (a m t) -> p a t m", a=PASSES, t=PACK),
        )

        def round_x(c, a, engine_copy=nc.scalar.copy, first=0, last=None):
            last = last or width(c)
            engine_copy(
                out=x_bf[c, a][:, first * PACK : last * PACK].rearrange("p (g e i) -> p g i e", e=2, i=PACK),
                in_=x_raw[c, a][:, :, first:last].rearrange("p i (g e) -> p g i e", e=2),
            )

        def quantize(codes, scales, values):
            nc.vector.quantize_mx(out=codes.bitcast(FP8X4), scales=scales, in_=values)

        def message_pass(acc, t, c, a, blocks, start=False, stop=False, base=0):
            column = (a * PACK + t) * P
            for first, last in blocks:
                nc.tensor.matmul_mx(
                    out=acc[:, first - base : last - base],
                    lhsT=wn_dealt[:].bitcast(U8)[:, 2 * column : 2 * (column + P)].bitcast(FP4X4),
                    lhsT_scale=wn_scale[:, column : column + P],
                    rhs=x_codes[c, a][:, first:last].bitcast(FP8X4),
                    rhs_scale=x_scale[c, a][:, first:last],
                    start=start and (first, last) == blocks[0],
                    stop=stop and (first, last) == blocks[-1],
                )

        def state_pass(acc, t, first, last, start=False, stop=False):
            h = first // HALF
            nc.tensor.matmul_mx(
                out=acc,
                lhsT=un_codes[:, t * P : (t + 1) * P].bitcast(FP8X4),
                lhsT_scale=un_scale[:, t * P : (t + 1) * P],
                rhs=picked[h][:, first - h * HALF : last - h * HALF].bitcast(FP8X4),
                rhs_scale=picked_scale[SCALE_ROW0:P, first:last],
                start=start,
                stop=stop,
            )

        def activate(out, acc, t):
            nc.scalar.activation(out=out, in_=acc, func=TANH, bias=bias[:, t : t + 1])

        def gather(out, t, first, last):
            nc.vector.tensor_copy(out, state[t][:].indirect(entries(first, last)))

        def gather_sum(out, t, first, last, values):
            nc.vector.tensor_tensor(out, state[t][:].indirect(entries(first, last)), values, ADD)

        def scatter_weighed(t, first, last, summed):
            nc.vector.tensor_tensor(page[t][:].indirect(entries(first, last)), summed, weight[:, first:last], MULT)

        def scatter(t, first, last, values):
            nc.vector.tensor_copy(page[t][:].indirect(entries(first, last)), values)

        def interleave(engine_copy, t, q):
            engine_copy(out=y_bf[q][:, :, t], in_=page[t][:, q * PIECE : (q + 1) * PIECE])

        def finish_row_set(t):
            nc.sync.dma_start(out=y_rows[t], in_=page[t][:])
            for q in VECTOR_PIECES + SCALAR_PIECES:
                piece = page[t][:, q * PIECE : (q + 1) * PIECE]
                halves = pairs[q][:, t // 2, :].bitcast(BF16).rearrange("p (c u) -> p c u", u=2)
                if t < 2:
                    nc.scalar.copy(out=halves[:, :, t], in_=piece)
                else:
                    nc.gpsimd.tensor_scalar(halves[:, :, 0], piece, unit[:], 0.0, MULT, ADD)
                    words = y_bf[q][:].rearrange("p c i -> p (c i)").bitcast(U32).rearrange("p (c u) -> p c u", u=2)
                    nc.scalar.copy(out=words, in_=pairs[q][:].rearrange("p u c -> p c u"))

        un_view = un_raw[:].rearrange("p i (m t) -> p m i t", t=PACK)
        un_dealt = un_bf[:].rearrange("p (t m i) -> p m i t", t=PACK, i=PACK)
        nc.scalar.copy(out=un_dealt[:, :UN_SCALAR], in_=un_view[:, :UN_SCALAR])
        nc.vector.tensor_copy(out=un_dealt[:, UN_SCALAR:], in_=un_view[:, UN_SCALAR:])
        quantize(un_codes[:], un_scale[:], un_bf[:])

        blocks = [(0, P), (P, QUARTER)]
        whole = [(0, HALF)]
        first_banks = [bank("first%d" % b, b, [P]) for b in range(len(blocks))]
        acc_b = [bank("chunk_b%d" % t, 4 + t, [QUARTER]) for t in range(3)]
        acc3 = bank("first_half3", 7, [HALF])
        for acc, block in zip(first_banks, blocks):
            state_pass(acc[:], 0, *block, start=True)
        for t in (0, 2):
            state_pass(acc_b[t][:], t, QUARTER, HALF, start=True)
        state_pass(acc3[:], 3, 0, HALF, start=True)

        for a in range(PASSES):
            x_bf["a", a] = tile("x_bf_a%d" % a, [P, QUARTER * PACK], BF16)[:]
            x_codes["a", a] = tile("x_codes_a%d" % a, [P, QUARTER], U32)[:]
            x_scale["a", a] = tile("x_scale_a%d" % a, [P, QUARTER], U8)[:]
        round_x("a", 0, nc.vector.tensor_copy, 0, P)
        round_x("a", 0, nc.scalar.copy, P, QUARTER)
        quantize(x_codes["a", 0], x_scale["a", 0], x_bf["a", 0])
        round_x("a", 1, nc.vector.tensor_copy, 0, P)
        round_x("a", 1, nc.scalar.copy, P, QUARTER)
        for first, last in blocks:
            values = x_bf["a", 1][:, first * PACK : last * PACK]
            quantize(x_codes["a", 1][:, first:last], x_scale["a", 1][:, first:last], values)
        picked[1] = tile("picked1", [P, HALF], I32, "x_raw_a1")
        pick_words(1)

        act_a = [tile("act_a%d" % t, [P, QUARTER], F32) for t in range(3)]
        for a in range(PASSES):
            for acc, (first, last) in zip(first_banks, blocks):
                nc.tensor.matmul_mx(
                    out=acc[:],
                    lhsT=wn_dealt[:].bitcast(U8)[:, 2 * a * PACK * P : 2 * (a * PACK + 1) * P].bitcast(FP4X4),
                    lhsT_scale=wn_scale[:, a * PACK * P : (a * PACK + 1) * P],
                    rhs=x_codes["a", a][:, first:last].bitcast(FP8X4),
                    rhs_scale=x_scale["a", a][:, first:last],
                    start=False,
                    stop=a == PASSES - 1,
                )
                if a == PASSES - 1:
                    activate(act_a[0][:, first:last], acc[:], 0)
        for t in (1, 2):
            acc = bank("chunk_a%d" % t, 1 + t, [QUARTER])
            message_pass(acc, t, "a", 1, blocks[::-1], start=True)
            message_pass(acc, t, "a", 0, blocks)
            state_pass(acc[:], t, 0, QUARTER, stop=True)
            activate(act_a[t][:], acc[:], t)
        acc_h0 = [bank("second_half0_%d" % b, b, [QUARTER]) for b in range(2)]
        for b in range(2):
            state_pass(acc_h0[b][:], 0, HALF + b * QUARTER, HALF + (b + 1) * QUARTER, start=True)
        acc_h = {t: bank("second_half%d" % t, 1 + t, [HALF]) for t in (1, 2)}
        for t in (1, 2):
            state_pass(acc_h[t][:], t, HALF, J, start=True)
        message_pass(acc3, 3, "a", 1, blocks[::-1])
        message_pass(acc3, 3, "a", 0, blocks)

        held = {0: tile("held0", [P, HALF], F32)}
        sum_a = [tile("sum_a%d" % t, [P, QUARTER], F32) for t in range(2)]
        gather(held[0][:, :QUARTER], 0, HALF, HALF + QUARTER)
        gather_sum(sum_a[0][:], 0, 0, QUARTER, act_a[0][:])
        gather(held[0][:, QUARTER:], 0, HALF + QUARTER, J)
        scatter_weighed(0, 0, QUARTER, sum_a[0][:])
        held[1] = tile("held1", [P, HALF], F32, "act_a0")
        gather_sum(sum_a[1][:], 1, 0, QUARTER, act_a[1][:])
        gather(held[1][:, :QUARTER], 1, HALF, HALF + QUARTER)
        scatter_weighed(1, 0, QUARTER, sum_a[1][:])
        gather(held[1][:, QUARTER:], 1, HALF + QUARTER, J)

        b_bf = tile("x_bf_b", [P, PASSES * QUARTER * PACK], BF16, "act_a1")
        b_codes = tile("x_codes_b", [P, PASSES * QUARTER], U32)
        b_scale = tile("x_scale_b", [P, PASSES * QUARTER], U8)
        for a in range(PASSES):
            x_bf["b", a] = b_bf[:, a * QUARTER * PACK : (a + 1) * QUARTER * PACK]
            x_codes["b", a] = b_codes[:, a * QUARTER : (a + 1) * QUARTER]
            x_scale["b", a] = b_scale[:, a * QUARTER : (a + 1) * QUARTER]
            round_x("b", a)
        quantize(b_codes[:], b_scale[:], b_bf[:])
        early2 = tile("early2", [P, QUARTER + P], F32, "x_raw_b1")
        gather_sum(early2[:, :QUARTER], 2, 0, QUARTER, act_a[2][:])
        gather(early2[:, QUARTER:], 2, HALF, HALF + P)
        scatter_weighed(2, 0, QUARTER, early2[:, :QUARTER])

        act_b = tile("act_b", [P, 3 * QUARTER], F32, "act_a2")
        for t in range(3):
            for a in range(PASSES):
                message_pass(acc_b[t], t, "b", a, blocks, start=t == 1 and a == 0, stop=t != 1 and a == PASSES - 1)
            if t == 1:
                state_pass(acc_b[t][:], t, QUARTER, HALF, stop=True)
            activate(act_b[:, t * QUARTER : (t + 1) * QUARTER], acc_b[t][:], t)
        for a in range(PASSES):
            message_pass(acc3[:, QUARTER:], 3, "b", a, blocks, stop=a == PASSES - 1)
        sum_b = [tile("sum_b%d" % t, [P, QUARTER], F32) for t in range(3)]
        for t in range(2):
            gather_sum(sum_b[t][:], t, QUARTER, HALF, act_b[:, t * QUARTER : (t + 1) * QUARTER])
        scatter_weighed(0, QUARTER, HALF, sum_b[0][:])
        gather_sum(sum_b[2][:], 2, QUARTER, HALF, act_b[:, 2 * QUARTER :])
        scatter_weighed(1, QUARTER, HALF, sum_b[1][:])

        h_bf = tile("x_bf_h", [P, PASSES * HALF * PACK], BF16, "picked0")
        act_h = [tile("act_h%d" % t, [P, HALF], F32) for t in range(PACK)]
        acc_h[3] = bank("second_half3", 4, [HALF])
        state_pass(acc_h[3][:], 3, HALF, J, start=True)
        for a in range(PASSES):
            x_bf["h", a] = h_bf[:, a * HALF * PACK : (a + 1) * HALF * PACK]
            x_bf["c", a], x_bf["d", a] = x_bf["h", a][:, : QUARTER * PACK], x_bf["h", a][:, QUARTER * PACK :]
            x_codes["h", a] = tile("x_codes_h%d" % a, [P, HALF], U32, "act_a2" if a == 0 else None)[:]
            x_scale["h", a] = tile("x_scale_h%d" % a, [P, HALF], U8)[:]
            round_x("c", a)
            round_x("d", a)
            for first, last in whole if a == 0 else [(0, QUARTER), (QUARTER, HALF)]:
                values = x_bf["h", a][:, first * PACK : last * PACK]
                quantize(x_codes["h", a][:, first:last], x_scale["h", a][:, first:last], values)
            for b in range(2):
                shifted = [(first + b * QUARTER, last + b * QUARTER) for first, last in blocks]
                message_pass(acc_h0[b], 0, "h", a, shifted, stop=a == PASSES - 1, base=b * QUARTER)
        act3 = [tile("act3_%d" % b, [P, QUARTER], F32) for b in range(2)]
        for b in range(2):
            activate(act3[b][:], acc3[:, b * QUARTER : (b + 1) * QUARTER], 3)
        for b in range(2):
            activate(act_h[0][:, b * QUARTER : (b + 1) * QUARTER], acc_h0[b][:], 0)
        for t in range(1, PACK):
            message_pass(acc_h[t], t, "h", 1, whole)
            message_pass(acc_h[t], t, "h", 0, whole, stop=True)
            activate(act_h[t][:], acc_h[t][:], t)

        sum3 = tile("sum3", [P, HALF], F32, "x_raw_d1")
        for b in range(2):
            part = slice(b * QUARTER, (b + 1) * QUARTER)
            gather_sum(sum3[:, part], 3, part.start, part.stop, act3[b][:])
        weighed2 = tile("weighed2", [P, QUARTER], F32, "act3_0")
        nc.gpsimd.tensor_tensor(weighed2[:], sum_b[2][:], weight[:, QUARTER:HALF], MULT)
        held[3] = tile("held3", [P, HALF], F32, "picked0")
        gather(held[3][:], 3, HALF, J)
        held[2] = tile("held2", [P, HALF - P], F32, "act3_1")
        gather(held[2][:], 2, HALF + P, J)
        scatter(2, QUARTER, HALF, weighed2[:])

        for t in range(3):
            summed = tile("sum_h%d" % t, [P, HALF], F32, ("sum_b2", "held0", "act_a0")[t])
            if t < 2:
                nc.gpsimd.tensor_tensor(summed[:], act_h[t][:], held[t][:], ADD)
            else:
                nc.gpsimd.tensor_tensor(summed[:, :P], act_h[t][:, :P], early2[:, QUARTER:], ADD)
                nc.gpsimd.tensor_tensor(summed[:, P:], act_h[t][:, P:], held[t][:], ADD)
            nc.gpsimd.tensor_tensor(act_h[t][:], summed[:], weight[:, HALF:], MULT)
        summed = tile("sum_h3", [P, HALF], F32, "act3_1")
        nc.gpsimd.tensor_tensor(summed[:], act_h[3][:], held[3][:], ADD)
        last = tile("weighed3", [P, J], F32, "picked0")
        nc.gpsimd.tensor_tensor(last[:, :HALF], sum3[:], weight[:, :HALF], MULT)
        nc.gpsimd.tensor_tensor(last[:, HALF:], summed[:], weight[:, HALF:], MULT)
        unit = tile("unit", [P, 1], F32, "weight")
        nc.gpsimd.memset(unit[:], 1.0)
        for t in range(3):
            scatter(t, HALF, J, act_h[t][:])
            finish_row_set(t)
        scatter(3, 0, J, last[:])

        nc.sync.dma_start(out=y_rows[3], in_=page[3][:])
        for q in SCALAR_PIECES:
            interleave(nc.scalar.copy, 3, q)
        for q in VECTOR_PIECES:
            interleave(nc.vector.tensor_copy, 3, q)
        for q in VECTOR_PIECES + SCALAR_PIECES:
            quantize(y_codes[q][:], y_scale[:, q * PIECE : (q + 1) * PIECE], y_bf[q][:].rearrange("p c i -> p (c i)"))
            nc.sync.dma_start(out=y_words[:, q * PIECE : (q + 1) * PIECE], in_=y_codes[q][:])
        for r in range(RUN):
            nc.scalar.dma_start(
                out=out_2.bitcast(I32)[0, r:SCALE_ROWS:RUN, :], in_=y_scale[r:P:QUADRANT, :].bitcast(I32)
            )
